import numpy as np, ml_dtypes
CORES = [2,3,42,43,82,83,122,123]
N = 8
BF = ml_dtypes.bfloat16
W, A, S, RO, H = 4096, 128, 2, 8, 2
def parts(rng):
    z = rng.integers(0, 256, (N, 8, 16, W)); w = rng.integers(0, 256, (N, 8, 16, 3)); w[..., 2] = rng.integers(0, 2048, (N, 8, 16))
    return z, w, rng.choice(np.array([750, 850, 950, 1200]), (N, 8, 1, 1))
def loose(rng):
    share = rng.choice(np.array([0.06, 0.15, 0.4, 0.9]), (N, 8, 1, A))
    return np.where(rng.random((N, 8, 16, A)) < share, rng.integers(0, W, (N, 8, 16, A)), -1)
def objects(rng, z, n):
    ix = np.argsort(rng.random((N, 8, W)), axis=-1)[..., :S * 2 * n]
    base = rng.integers(40, 216, (8, 16, 1, 1, n)); dev = rng.integers(-16, 17, (8, 16, 16, 2, n))
    order = np.argsort(rng.random((8, 16, n)), axis=1); rows = np.arange(16)[None, :, None]
    up = rows == order[:, :1]; down = rows == order[:, 1:2]
    v = base + np.where(up[:, None, :, None, :], 16, np.where(down[:, None, :, None, :], -16, dev))
    for q in range(N):
        np.put_along_axis(z[q], np.broadcast_to(ix[q][:, None, :], (8, 16, S * 2 * n)), v[:, :, S * q:S * q + S].reshape(8, 16, S * 2 * n), 2)
    return np.ascontiguousarray(ix.reshape(N, 8, S, 2, n).transpose(1, 0, 2, 3, 4)).reshape(8, 16, 2, n), up | down
def follow(rng, obj, am):
    out = []
    for r in range(N):
        c = rng.integers(0, obj.shape[-1], (8, 1, A))
        one = np.take_along_axis(obj[:, :, 0], c, 2); two = np.take_along_axis(obj[:, :, 1], c, 2); anchor = np.take_along_axis(am, c, 2)
        v = (rng.random((8, 16, A)) < rng.choice(np.array([0, 0, 0.1, 0.5]), (8, 1, A))) & ~anchor
        keep = anchor | (rng.random((8, 16, A)) < rng.random((8, 1, A)))
        out.append(np.where(keep, np.where(v, two, one), -1))
    return np.stack(out)
def pack(z, w, t, p, s):
    return {"tz": np.ascontiguousarray(z.reshape(N, 128, W)).astype(np.float32).astype(BF), "tp": np.ascontiguousarray(p.reshape(N, 128, A)).astype(np.int32),
            "sd": np.ascontiguousarray(s.reshape(N, 128, A)).astype(np.int32), "hw": np.ascontiguousarray(w.reshape(N, 128, 3)).astype(np.int32),
            "th": np.repeat(t.reshape(N, 8, 1), 16, axis=1).astype(np.int32)}
def setup_inputs(rng):
    z, w, t = parts(rng); obj, am = objects(rng, z, A // 4)
    p = np.where(rng.random((N, 8, 1, A)) < 0.5, follow(rng, obj, am), loose(rng))
    s = np.where(rng.random((N, 8, 1, A)) < 0.5, follow(rng, obj, am), loose(rng))
    return pack(z, w, t, p, s)
def setup_inputs_twins(rng):
    z, w, t = parts(rng); obj, am = objects(rng, z, 4); t[:] = 4096
    p = follow(rng, obj, am); p[:, 6:] = loose(rng)[:, 6:]; p[..., A // 2:] = p[..., :A // 2].copy()
    return pack(z, w, t, p, follow(rng, obj, am))
def setup_inputs_ties(rng):
    z, w, t = parts(rng)
    z = np.take_along_axis(rng.integers(0, 256, (N, 8, 16, 6)), rng.integers(0, 6, (N, 8, 1, W)), 3)
    t = rng.choice(np.array([1000, 4096]), (N, 8, 1, 1)); p = loose(rng); s = loose(rng)
    w[:, 0, :, :2] = 0; w[:, 1, :, 2] = 0; w[:, 4, :, 2] = rng.choice(np.array([5, 1031]), (N, 16)); t[:, :2] = 4096
    z[:, 2:4] = 100; t[::2, 2] = 0; t[1::2, 2] = 1; t[:, 3] = 432; p[:, 2:4, :, ::4] = -1
    return pack(z, w, t, p, s)
def setup_inputs_ends(rng):
    z = 255 * rng.integers(0, 2, (N, 8, 16, W)); ends = np.array([-1, 0, 1, W - 2, W - 1])
    p = rng.choice(ends, (N, 8, 16, A)); s = rng.choice(ends, (N, 8, 16, A)); t = rng.choice(np.array([0, 1, 2040, 4080, 4096]), (N, 8, 1, 1))
    w = rng.choice(np.array([0, 1, 254, 255]), (N, 8, 16, 3)); w[..., 2] = rng.choice(np.array([0, 1, 1025, 2046, 2047]), (N, 8, 16))
    p[:, 4] = rng.integers(0, W, (N, 16, A)); t[:, 4] = 4096
    z[:, 5] = 255; w[:, 5, :, :2] = 0; w[:, 5, 0, :2] = 255; w[:, 5, 1, :2] = 2; w[:, 5, :, 2] = 2047; t[:, 5] = 4096
    p[:, 6] = -1; t[:, 6] = 4096
    z[::2, 7] = 255; z[1::2, 7] = 0; p[:, 7] = rng.integers(0, W, (N, 16, A)); p[:, 7, (np.arange(16) // S) % 2 == 1] = -1
    t[1::4, 7] = 4081; t[3::4, 7] = 4080
    w[1::2, 7, :, 0] = 0; w[1::2, 7, :, 1] = 254 * rng.integers(0, 2, (N // 2, 16)); w[1::2, 7, 0, 1] = 255; w[1::2, 7, 0, 2] = rng.integers(1, 2048, N // 2)
    return pack(z, w, t, p, s)
def setup_inputs_sparse(rng):
    z, w, t = parts(rng); t = rng.choice(np.array([900, 4096]), (N, 8, 1, 1)); t[:, 0] = 4096
    p = np.where(rng.random((N, 8, 16, A)) < 0.06, rng.integers(0, W, (N, 8, 16, A)), -1); p[rng.integers(0, N)] = -1
    s = loose(rng); s[:, rng.permutation(8)[:4]] = -1
    return pack(z, w, t, p, s)
def setup_inputs_spread(rng):
    z = np.minimum((np.exp2(8.0 * rng.random((N, 8, 1, W))) * rng.random((N, 8, 16, W))).astype(np.int64), 255)
    w = np.minimum(np.exp2(8.0 * rng.random((N, 8, 16, 3))).astype(np.int64), 255); w[..., 2] = np.minimum(np.exp2(11.0 * rng.random((N, 8, 16))).astype(np.int64), 2047)
    t = np.minimum(np.exp2(7.0 + 5.0 * rng.random((N, 8, 1, 1))).astype(np.int64), 4096)
    ps = []
    for i in range(2):
        nm = np.minimum((W * rng.random((N, 8, 16, A)) ** 3).astype(np.int64), W - 1)
        ps.append(np.where(rng.random((N, 8, 16, A)) < rng.random((N, 8, 1, A)), nm, -1))
    return pack(z, w, t, ps[0], ps[1])
def check_inputs(d):
    bad = []; v = np.asarray(d["tz"]).astype(np.float32)
    if not (np.min(v) >= 0 and np.max(v) <= 255 and np.all(v == np.floor(v))): bad.append("tz: whole numbers from 0 to 255")
    for k, lo, hi in (("tp", -1, W - 1), ("sd", -1, W - 1), ("th", 0, 4096)):
        if np.min(d[k]) < lo or np.max(d[k]) > hi: bad.append("range of " + k)
    w = np.asarray(d["hw"])
    if np.min(w) < 0 or np.max(w[..., :2]) > 255 or np.max(w[..., 2]) > 2047: bad.append("range of hw")
    t = np.asarray(d["th"]).reshape(-1, 16)
    if np.any(t != t[:, :1]): bad.append("th: one number a group")
    return bad
def reference(tz, tp, sd, hw, th):
    z = tz.astype(np.float32).astype(np.int32).reshape(N, 8, 16, W); w = hw.astype(np.int32).reshape(N, 8, 16, 3); lim = th.astype(np.int32).reshape(N, 8, 16)[:, :, :1]
    p = tp.astype(np.int32).reshape(N, 8, 16, A); s = sd.astype(np.int32).reshape(N, 8, 16, A); lower = np.arange(A)[None, :] < np.arange(A)[:, None]
    for t in range(RO):
        for r in range(N):
            q = (r + 1 + t) % N; x = S * q + t // N
            hi = np.zeros((8, 16, A), np.int32); lo = np.full((8, 16, A), 255, np.int32)
            for j in range(16):
                n = p[r, :, j]; on = (n >= 0)[:, None, :]; v = np.take_along_axis(z[j // S], np.maximum(n, 0)[:, None, :], 2)
                hi = np.where(on, np.maximum(hi, v), hi); lo = np.where(on, np.minimum(lo, v), lo)
            e = (hi + lo) >> 1; c = e
            best = np.full((8, A), 4097); name = np.zeros((8, A), np.int64)
            for k in range(H):
                u1 = np.add.reduce(w[q, :, :, 0:1] * c, axis=1) & (W - 1); u2 = np.add.reduce(w[q, :, :, 1:2] * c, axis=1) & (W - 1)
                h = (((u1 * u2) >> 5)[:, None, :] + w[q, :, :, 2:3] * u2[:, None, :]) & (W - 1)
                v = np.take_along_axis(z[q], h.reshape(8, 1, 16 * A), 2).reshape(8, 16, 16, A)
                d = np.add.reduce(np.abs(v - e[:, :, None, :]), axis=1)
                m = np.argmin(d, axis=1); dm = np.min(d, axis=1); n = np.take_along_axis(h, m[:, None, :], 1)[:, 0]
                less = dm < best; name = np.where(less, n, name); best = np.where(less, dm, best)
                c = (e + np.take_along_axis(z[q], n[:, None, :], 2)) >> 1
            n = np.where(best < lim[q], name, -1); p[r, :, x] = n
            low = (n[:, :, None] == n[:, None, :]) & (n >= 0)[:, :, None] & lower
            g, b = np.nonzero(np.count_nonzero(low, axis=2) == 1); a = np.argmax(low[g, b], axis=1)
            pa = p[r][g, :, a]; pb = p[r][g, :, b]; differ = (pa >= 0) & (pb >= 0) & (pa != pb); clash = np.any(differ, axis=1)[:, None]
            p[r][g, :, a] = np.where(clash, np.where(differ, -1, pa), np.where(pa >= 0, pa, pb))
            p[r][g, :, b] = np.where(clash, np.where(differ, -1, pb), s[r][g, :, b])
    return {"yp": p.reshape(N, 128, A).astype(np.float32)}

@@ -1,0 +1,668 @@
+from concourse.bass import DstId, RemoteDMATransfer
+from concourse.mybir import AluOpType, AxisListType, ActivationFunctionType
+
+OP = AluOpType
+AF = ActivationFunctionType
+NR, W = 8, 4096
+MAGIC = 25165824.0
+
+f32, b16, h16, i32, u16 = "float32", "bfloat16", "float16", "int32", "uint16"
+SCRATCH = {}
+for _d, _l in (
+        (b16, "TZ 32768 F 8192 F0 2064 X 4096 Z0 1024 Z1 1024 VF 2048 VA 2048 MX 2048 MN 2048 EREP 2048 SB 4096 Y 4096 RM 1024 R255 1024 "
+              "BOB 128 IB 128 IBN 128 WD 144 MK 64 PC1 64 PC2 256 W1L 1024 W2L 1024 C2 128 E20 64 E21 64 E1 128 CLE 128"),
+        (h16, "TPH 256 PERM 512 NMO 256 NM 256 NMT 256 SW 272 HWO 4 HWN 64 BOH 128 BOK 128 IH 128 WS 144 RCA 1024 RCB 1024 CB 1024 "
+              "A16 128 CW 128 KX 1024 HGD 128 HTS 128 KBX 128"),
+        (i32, "TPI 128 SDI 128 HWI 3 THI 1 IP 16 IC 256 IC15 256 ICG 128 C48 64 L0T 128 S2 128 UI 16 UA 16 PP 8 VI 16 HI 128 HM 256 KI 16 "
+              "KFI 64 S1 128 NP1 128 NP2 128 KBI 8"),
+        (u16, "EL 64 REP 8 REP4 4 LL 256 LE 128 LH 256 LP 16 LN 8 LF 8 LPI 8"),
+        (f32, "COL 32 DL 128 RU 128 RB 64 CWT 128 C128 128 CT 8 CTT 8 CBC 8 SG 128 NMX 8 W1F 8 W2F 8 KCF 8 THK 8 KC 1024 SDV 128 S0M 128 "
+              "US 256 KK 128 HC 272 KS 256 CS 128 E2M 128 HIM 128 SUM 128 NFT 8 KB 8 KRS 128 KRP 128 PR 1024 YO 128")):
+    _l = _l.split()
+    for _i in range(0, len(_l), 2):
+        SCRATCH[_l[_i]] = ("sbuf", [128, int(_l[_i + 1])], _d)
+BANKS = ("BK0", "BK1", "PK0", "PK1", "HS", "KA", "VP0", "VP1")
+for _n in BANKS:
+    SCRATCH[_n] = ("psum", [128, 512], f32)
+SEMAPHORES = ["v", "s", "t", "gp", "nm", "hn", "ft", "fs", "ls", "hz0", "hz1"] + ["d%d" % i for i in range(20)] + \
+    ["ta%d" % q for q in range(NR)] + ["tb%d" % q for q in range(NR)]
+
+
+def mask_of(engs):
+    return sum(1 << e for e in engs)
+
+
+def places(T, topo):
+    chips, relay, used = [], {}, []
+    for r, c in enumerate(T.cores):
+        if not chips or topo.chip(T.cores[chips[-1][0]]) != topo.chip(c):
+            chips.append([])
+        chips[-1].append(r)
+        relay[r] = [x for x in topo.cores_of(c) if x not in T.cores and x not in used and topo.die(x) != topo.die(c)
+                    and all(topo.may_write(x, d) for d in T.cores)][0]
+        used.append(relay[r])
+    return chips, relay
+
+
+def rank_program(g, core, T, topo):
+    chips, relay = places(T, topo)
+    ncl = len(chips)
+    ls = [0]
+
+    def targets(r):
+        n = [i for i in range(ncl) if r in chips[i]][0]
+        return [T.cores[chips[(n - 1 - d) % ncl][-1]] for d in range(ncl - 1)]
+
+    def send(dst, lo, hi, sem, engs):
+        rid, pid = topo.addr(dst)[:2]
+        g.remote_dma(T.TZ[:, lo:hi], T.TZ[:, lo:hi], T.sem[sem], T.sem.ls, pid, rid, mask_of(engs))
+        ls[0] += len(engs)
+
+    rank = T.rank_of(core)
+    H2, Q4 = W // 2, W // 4
+    if rank is None:
+        for r in range(NR):
+            if relay[r] == core:
+                for n, d in enumerate(targets(r)):
+                    for i in range(2):
+                        if n == 0:
+                            g.wait_ge(T.sem["hz%d" % i], 8)
+                        o = r * W + H2 + i * Q4
+                        send(d, o, o + Q4, "tb%d" % r, topo.engines(core, d)[:8])
+                g.wait_ge(T.sem.ls, ls[0])
+        return
+
+    Q = {"v": g.vector, "s": g.scalar, "t": g.tensor, "g": g, "y": g.sync}
+    SEM = {"v": "v", "s": "s", "t": "t", "g": "gp"}
+    cnt = {e: 0 for e in SEM}
+    clk = {e: {} for e in Q}
+    hist, lastw, readers, ndma = {}, {}, {}, [0]
+
+    def wait(e, need):
+        for s, n in sorted(need.items()):
+            if clk[e].get(s, 0) < n:
+                Q[e].wait_ge(T.sem[s], n)
+                for s2, n2 in hist.get((s, n), {}).items():
+                    clk[e][s2] = max(clk[e].get(s2, 0), n2)
+                clk[e][s] = max(clk[e].get(s, 0), n)
+
+    def deps(e, R, Wt):
+        toks = [k for tg in R for k in lastw.get(tg, ())]
+        toks += [k for tg in R if tg in BANKS for k in readers.get(tg, {}).items() if k[0] != SEM.get(e)]
+        toks += [k for tg in Wt for k in lastw.get(tg, ()) if not (e == "t" and k[0] == "t")]
+        toks += [k for tg in Wt for k in readers.get(tg, {}).items() if k[0] != SEM.get(e)]
+        need = {}
+        for s, n in toks:
+            need[s] = max(need.get(s, 0), n)
+        return need
+
+    def done(tok, R, Wt):
+        for tg in R:
+            readers.setdefault(tg, {})[tok[0]] = tok[1]
+        for tg in Wt:
+            lastw[tg] = [tok]
+            readers[tg] = {}
+
+    def op(e, fn, R, Wt):
+        wait(e, deps(e, R, Wt))
+        ins = fn()
+        for i in (ins if isinstance(ins, list) else [ins]):
+            i.then_inc(T.sem[SEM[e]], 1)
+            cnt[e] += 1
+            hist[(SEM[e], cnt[e])] = dict(clk[e])
+        done((SEM[e], cnt[e]), R, Wt)
+
+    def dma(e, out, in_, R, Wt):
+        wait(e, deps(e, R, Wt))
+        s = "d%d" % ndma[0]
+        ndma[0] += 1
+        Q[e].dma_start(out, in_).then_inc(T.sem[s], 16)
+        hist[(s, 16)] = dict(clk[e])
+        done((s, 16), R, Wt)
+
+    V, S, PE = g.vector, g.scalar, g.tensor
+    mm = PE.matmul
+
+    def ts(out, a, s1, o1, R, Wt, s2=None, o2=None):
+        if o2 is None:
+            op("v", lambda: V.tensor_scalar(out, a, s1, None, o1), R, Wt)
+        else:
+            op("v", lambda: V.tensor_scalar(out, a, s1, s2, o1, o2), R, Wt)
+
+    def tt(out, a, b, o, R, Wt):
+        op("v", lambda: V.tensor_tensor(out, a, b, o), R, Wt)
+
+    def cp(out, a, R, Wt):
+        op("v", lambda: V.tensor_copy(out, a), R, Wt)
+
+    def fill(ap, x, Wt):
+        op("v", lambda: V.memset(ap, x), [], Wt)
+
+    def scan(out, d0, d1, o0, o1, R, Wt):
+        op("v", lambda: V.tensor_tensor_scan(out, d0, d1, 0.0, o0, o1), R, Wt)
+
+    def act(out, a, R, Wt, func=AF.Copy, bias=0.0, scale=1.0):
+        op("s", lambda: S.activation(out, a, func, bias=bias, scale=scale), R, Wt)
+
+    z0 = rank * W
+    dma("y", T.TPI[:], T.tp[:], [], ["TPI"])
+    dma("s", T.SDI[:], T.sd[:], [], ["SDI"])
+    dma("y", T.HWI[:], T.hw[:], [], ["HWI"])
+    dma("s", T.THI[:], T.th[:], [], ["THI"])
+    dma("y", T.TZ[:, z0:z0 + H2], T.tz[:, 0:H2], [], ["TZa%d" % rank])
+    dma("s", T.TZ[:, z0 + H2:z0 + W], T.tz[:, H2:W], [], ["TZb%d" % rank])
+    op("g", lambda: g.iota(T.IP[:, 0:1], [[0, 1]], 0, 1), [], ["IP"])
+    op("g", lambda: g.iota(T.IC[:], [[1, 256]], 0, 0), [], ["IC"])
+
+    C = {}
+    ip = {"P": T.IP[:, 0:1]}
+
+    def icol(name, *a):
+        n = len(ip)
+        ip[name] = T.IP[:, n:n + 1]
+        ts(ip[name], ip["P"], a[0], a[1], ["IP"], ["i" + name], *a[2:])
+
+    def col(name, src, s1, o1, s2=None, o2=None, R=()):
+        i = len(C)
+        C[name] = T.COL[:, i:i + 1]
+        ts(C[name], src, s1, o1, ["IP"] + ["i" + x for x in ip] + list(R), ["c" + name], s2, o2)
+
+    AND, SHR = OP.bitwise_and, OP.arith_shift_right
+    icol("K", 15, AND)
+    icol("Q", 14, AND)
+    icol("S", 1, AND)
+    icol("G", 4, SHR)
+    icol("B3", 3, SHR, 1, AND)
+    icol("B4", 4, SHR, 1, AND)
+    icol("B5", 5, SHR)
+    icol("L", 7, AND)
+    col("S8", ip["S"], 8.0, OP.mult)
+    col("G8", ip["G"], 1.0, OP.mult)
+    col("PM0", ip["Q"], 16.0, OP.mult, C["S8"], OP.add, ["cS8"])
+    col("PM", C["PM0"], C["G8"], OP.add, None, None, ["cPM0", "cG8"])
+    col("P", ip["P"], 1.0, OP.mult)
+    ts(T.PERM[:, 0:256], T.IC[:], C["PM"], OP.is_equal, ["IC", "cPM"], ["PERM0"])
+    ts(T.PERM[:, 256:512], T.IC[:], -16.0, OP.add, ["IC", "cPM"], ["PERM1"], C["PM"], OP.is_equal)
+    ts(T.IH[:], T.IC[:, 0:128], C["P"], OP.is_equal, ["IC", "cP"], ["IH"])
+    ts(T.TPH[:, 0:128], T.TPI[:], -2047.0, OP.add, ["TPI"], ["TPH0"])
+    ts(T.TPH[:, 128:256], T.SDI[:], -2047.0, OP.add, ["SDI"], ["TPH1"])
+
+    def turn():
+        mm(T.HS[:, 0:256], T.TPH[:, 0:128], T.PERM[:, 0:256], True, False)
+        return mm(T.HS[:, 0:256], T.TPH[:, 128:256], T.PERM[:, 256:512], False, True)
+    op("t", turn, ["TPH0", "TPH1", "PERM0", "PERM1"], ["HS"])
+    cp(T.HWO[:, 0:3], T.HWI[:], ["HWI"], ["HWO0"])
+    ts(T.HWO[:, 3:4], T.THI[:], -2048.0, OP.add, ["THI"], ["HWO1"])
+    cp(T.NMO[:], T.HS[:, 0:256], ["HS"], ["NMO"])
+    cp(T.NM[:, rank * 32:rank * 32 + 32], T.NMO[:, rank * 32:rank * 32 + 32], ["NMO"], ["NMo"])
+    cp(T.HWN[:, rank * 8:rank * 8 + 4], T.HWO[:], ["HWO0", "HWO1"], ["HWo"])
+
+    mine = [c for c in chips if rank in c][0]
+    far = [r for r in range(NR) if r not in mine]
+    near = [r for r in mine if r != rank][0]
+    others = far + [near]
+    last = rank == mine[-1]
+    fe = topo.engines(core, T.cores[far[0]])
+    ne = [e for e in topo.engines(core, T.cores[near]) if e not in fe]
+    slots = fe[:6] + [fe[6]] if last else fe[4:] + fe[4:6] + [ne[0]]
+
+    def did(r):
+        a = topo.addr(T.cores[r])
+        return DstId(rid=a[0], pnc=a[1])
+
+    def spread(src, dst, sem, engs):
+        todo = [(r, e) for r, e in zip(others, engs)]
+        while todo:
+            tr, seen, rest = [], [], []
+            for r, e in todo:
+                if e in seen:
+                    rest.append((r, e))
+                else:
+                    seen.append(e)
+                    tr.append(RemoteDMATransfer(dst_ids=[did(r)], dma_engine_mask=1 << e, remote_sem=T.sem[sem], srcs=[src(r)], dsts=[dst]))
+            g.remote_dma_fused(tr, local_sem=T.sem.ls)
+            ls[0] += len(tr)
+            todo = rest
+
+    wait("g", deps("g", ["NMO"], []))
+    spread(lambda r: T.NMO[:, r * 32:r * 32 + 32], T.NM[:, rank * 32:rank * 32 + 32], "nm", fe)
+    wait("g", deps("g", ["HWO0", "HWO1"], []))
+    g.remote_dma_fused([RemoteDMATransfer(dst_ids=[did(r) for r in others], dma_engine_mask=1 << fe[7], remote_sem=T.sem.hn, srcs=[T.HWO[:]],
+                                          dsts=[T.HWN[:, rank * 8:rank * 8 + 4] for _ in others])], local_sem=T.sem.ls)
+    ls[0] += 1
+    lastw["NM"], lastw["HWN"] = [("nm", 7)], [("hn", 7)]
+
+    def direct(d, engs):
+        wait("g", deps("g", ["TZa%d" % rank], []))
+        for i in range(8 // len(engs)):
+            n = H2 * len(engs) // 8
+            send(d, z0 + i * n, z0 + i * n + n, "ta%d" % rank, engs)
+
+    def to_relay():
+        wait("g", deps("g", ["TZb%d" % rank], []))
+        for i in range(2):
+            send(relay[rank], z0 + H2 + i * Q4, z0 + H2 + (i + 1) * Q4, "hz%d" % i, ne[:8])
+
+    def hand_on(q):
+        for h, x in enumerate("ab"):
+            wait("g", deps("g", ["TZ%s%d" % (x, q)], []))
+            send(T.cores[near], q * W + h * H2, q * W + (h + 1) * H2, "t%s%d" % (x, q), ne)
+
+    if last:
+        hand_on(rank)
+    else:
+        direct(targets(rank)[0], fe[:4])
+        to_relay()
+    ntb = {q: 16 if last and q in far else 8 for q in range(NR)}
+    for q in range(NR):
+        if q != rank:
+            lastw["TZa%d" % q] = [("ta%d" % q, 8)]
+            lastw["TZb%d" % q] = [("tb%d" % q, ntb[q])]
+
+    col("K", ip["K"], 1.0, OP.mult)
+    col("PG", ip["G"], 16.0, OP.mult)
+    col("PGF", C["PG"], 15.0, OP.add, None, None, ["cPG"])
+    col("QB", ip["Q"], 512.0, OP.mult)
+    col("S128", ip["S"], 128.0, OP.mult)
+    col("E0", ip["K"], 0.0, OP.is_equal)
+    col("E1", ip["K"], 1.0, OP.is_equal, 2048.0, OP.mult)
+    col("J128", ip["K"], 128.0, OP.mult)
+    col("B3", ip["B3"], 8.0, OP.add)
+    col("R2", ip["B5"], 2.0, OP.mult, C["B3"], OP.add, ["cB3"])
+    col("SW", ip["L"], 16.0, OP.mult, C["R2"], OP.add, ["cR2"])
+    col("T1", ip["B4"], 1.0, OP.mult)
+    col("T0", ip["B4"], 0.0, OP.is_equal)
+    ic = T.IC[:, 0:128]
+    for ty in range(2):
+        ts(T.SW[:, ty * 136:ty * 136 + 136], T.IC[:, 0:136], C["SW"], OP.is_equal, ["IC", "cSW", "cT%d" % ty], ["SW%d" % ty], C["T%d" % ty], OP.mult)
+    fill(T.F0[:, 2048:2064], -256.0, ["F0e"])
+    ts(T.L0T[:], ic, C["J128"], OP.add, ["IC", "cJ128"], ["L0T"])
+    pr = [T.PR[:, i * 128:i * 128 + 128] for i in range(8)]
+    ts(pr[0], T.TPI[:], 0.0, OP.is_lt, ["TPI"], ["pr0"], 2048.0, OP.mult)
+    tt(pr[1], T.L0T[:], pr[0], OP.max, ["L0T", "pr0"], ["pr1"])
+    cp(T.LE[:], pr[1], ["pr1"], ["LE"])
+    for b, (x, y) in enumerate(((0.0, 1.0), (255.0, 0.0))):
+        rm = (T.RM, T.R255)[b]
+        fill(rm[:], y, ["RM%d" % b])
+        fill(rm[:, 0::16], x, ["RM%d" % b])
+    fill(T.RU[:], 0.0, ["RU"])
+    fill(T.RU[:, 0::16], -1e9, ["RU"])
+    fill(T.RB[:], 0.0, ["RB"])
+    fill(T.RB[:, 0::16], 1e9, ["RB"])
+    op("t", lambda: [mm(T.HS[:, b * 128:b * 128 + 128], T.NM[:, b * 128:b * 128 + 128], T.IH[:], True, True) for b in range(2)],
+       ["NM", "NMo", "IH"], ["HS"])
+    cp(T.NMT[:], T.HS[:, 0:256], ["HS"], ["NMT"])
+
+    def back():
+        out = []
+        for ty in range(2):
+            o = T.KA[:, ty * 128:ty * 128 + 128]
+            mm(o, T.SW[:, ty * 136 + 8:ty * 136 + 136], T.NMT[:, 0:128], True, False)
+            out.append(mm(o, T.SW[:, ty * 136:ty * 136 + 128], T.NMT[:, 128:256], False, True))
+        return out
+    op("t", back, ["SW0", "SW1", "NMT"], ["KA"])
+    ts(T.LL[:], T.KA[:, 0:256], 2047.0, OP.add, ["KA"], ["LL"], 0.0, OP.max)
+    tzo = ["TZa%d" % rank, "TZb%d" % rank]
+
+    def feats(ty):
+        y0 = ty * 2048
+        win = T.TZ[:, z0:z0 + W]
+        act(T.Y[:, y0:y0 + 1024], win.indirect(T.LL[:, ty * 128:ty * 128 + 64]), tzo + ["LL"], ["Ya%d" % ty])
+        cp(T.Y[:, y0 + 1024:y0 + 2048], win.indirect(T.LL[:, ty * 128 + 64:ty * 128 + 128]), tzo + ["LL"], ["Yb%d" % ty])
+        for r in others + [rank]:
+            for s in range(2):
+                src = T.Y[:, y0 + 2 * r + s:y0 + 2048:16]
+                o = r * 512 + ty * 256 + s * 128
+                out, tag = T.SB[:, o:o + 128], "SB%d_%d_%d" % (r, ty, s)
+                if r == rank and ty == 0:
+                    out, tag = T.F0[:, rank * 256 + s * 128:rank * 256 + s * 128 + 128], "F0o%d" % s
+                elif r == rank:
+                    o = rank * 1024 + 256 + s * 128
+                    out, tag = T.F[:, o:o + 128], "Fso%d" % s
+                (cp if s == 0 else act)(out, src, ["Ya%d" % ty, "Yb%d" % ty], [tag])
+        wait("g", deps("g", ["SB%d_%d_%d" % (r, ty, s) for r in others for s in range(2)], []))
+        d = T.F0[:, rank * 256:rank * 256 + 256] if ty == 0 else T.F[:, rank * 1024 + 256:rank * 1024 + 512]
+        spread(lambda r: T.SB[:, r * 512 + ty * 256:r * 512 + ty * 256 + 256], d, "fs" if ty else "ft", slots)
+        lastw["Fsr" if ty else "F0r"] = [("fs" if ty else "ft", 7)]
+
+    feats(0)
+    feats(1)
+    f0 = ["F0r", "F0o0", "F0o1", "F0e"]
+    if last:
+        direct(targets(rank)[0], fe)
+        to_relay()
+    for d in targets(rank)[1:]:
+        direct(d, fe)
+    if not last:
+        hand_on(rank)
+    else:
+        n = [i for i in range(ncl) if rank in chips[i]][0]
+        for d in range(1, ncl):
+            for q in chips[(n + d) % ncl]:
+                hand_on(q)
+
+    ts(T.IC15[:], T.IC[:], 15, AND, ["IC"], ["IC15"])
+    ts(T.ICG[:], ic, 112, AND, ["IC"], ["ICG"])
+    ts(T.C48[:], T.IC[:, 0:64], 48, AND, ["IC"], ["C48"])
+    ts(T.EL[:], T.C48[:], C["K"], OP.add, ["C48", "cK"], ["EL"])
+    ts(T.MK[:], T.IC15[:, 0:64], C["K"], OP.not_equal, ["IC15", "cK"], ["MK"], -4194304.0, OP.mult)
+    ts(T.IB[:], ic, C["P"], OP.is_equal, ["IC", "cP"], ["IB"])
+    ts(T.IBN[:], ic, C["P"], OP.is_equal, ["IC", "cP"], ["IBN"], -1.0, OP.mult)
+    ts(T.DL[:], T.IC15[:, 0:128], C["K"], OP.is_equal, ["IC15", "cK"], ["DL"])
+    ts(T.BOB[:], T.ICG[:], C["PG"], OP.is_equal, ["ICG", "cPG"], ["BOB"])
+    ts(T.BOH[:], T.ICG[:], C["PG"], OP.is_equal, ["ICG", "cPG"], ["BOH"])
+    ts(T.BOK[:], T.ICG[:], C["PG"], OP.is_equal, ["ICG", "cPG"], ["BOK"], 1024.0, OP.mult)
+    cp(T.REP[:], T.IC[:, 0:8], ["IC"], ["REP"])
+    cp(T.REP4[:], T.IC[:, 4:8], ["IC"], ["REP4"])
+    ts(T.WD[:], T.IC[:, 0:144], C["PGF"], OP.is_equal, ["IC", "cPGF"], ["WD"], 4096.0, OP.mult)
+    ts(T.WS[:], T.IC[:, 0:144], C["PGF"], OP.is_equal, ["IC", "cPGF"], ["WS"], 1024.0, OP.mult)
+    ts(T.PC1[:], T.IC15[:, 0:64], 16.0, OP.mult, ["IC15", "cK"], ["PC1"], C["K"], OP.add)
+    for i in range(4):
+        ts(T.PC2[:, i * 64:i * 64 + 64], T.C48[:], 16.0, OP.mult, ["C48"], ["PC2%d" % i], 1024.0 * i, OP.add)
+    hwn = ["HWN", "HWo"]
+    for i, x in enumerate((T.W1F, T.W2F, T.KCF)):
+        cp(x[:], T.HWN[:, i::8], hwn, ["hw%d" % i])
+    ts(T.THK[:], T.HWN[:, 3::8], 2048.0, OP.add, hwn, ["THK"], 4096.0, OP.mult)
+
+    def hash_consts(q):
+        o = slice(q * 128, q * 128 + 128)
+        ts(T.W1L[:, o], T.BOB[:], T.W1F[:, q:q + 1], OP.mult, ["BOB", "hw0"], ["W1L%d" % q], 0.5, OP.mult)
+        ts(T.W2L[:, o], T.BOB[:], T.W2F[:, q:q + 1], OP.mult, ["BOB", "hw1"], ["W2L%d" % q], 0.5, OP.mult)
+        ts(T.KX[:, o], T.DL[:], T.KCF[:, q:q + 1], OP.mult, ["DL", "hw2"], ["KX%d" % q])
+        op("t", lambda: mm(T.KA[:, 256:384], T.BOH[:], T.KX[:, o], True, True), ["BOH", "KX%d" % q], ["KA"])
+        act(T.KC[:, o], T.KA[:, 256:384], ["KA"], ["KC%d" % q])
+
+    for t in range(NR):
+        hash_consts((rank + 1 + t) % NR)
+    for q in range(NR):
+        fill(T.F[:, q * 1024 + 512:(q + 1) * 1024], -256.0, ["FW%d" % q])
+    for h in range(2):
+        fill(T.E1[:, h * 64 + 48:h * 64 + 64], 0.0, ["E1z"])
+    ts(T.CWT[:], ic, 512.0, OP.add, ["IC"], ["CWT"], 1.0 / 1024, OP.mult)
+    ts(T.CW[:], T.CWT[:], C["E0"], OP.mult, ["CWT", "cE0", "cE1"], ["CW"], C["E1"], OP.add)
+    ts(T.C128[:], ic, 128.0, OP.add, ["IC"], ["C128"])
+    ts(T.CTT[:], T.IC[:, 0:8], 16.0, OP.mult, ["IC", "cK"], ["CTT"], C["K"], OP.add)
+    ts(T.CT[:], T.CTT[:], 256.0, OP.add, ["CTT"], ["CT"], 1.0 / 256, OP.mult)
+    ts(T.SG[:], ic, C["S128"], OP.add, ["IC", "cS128"], ["SG"])
+    ts(T.NMX[:], T.IC[:, 0:8], 2.0, OP.mult, ["IC", "cK"], ["NMX"], C["K"], OP.not_equal)
+    fill(T.HC[:, 256:272], -2048.0, ["HCe"])
+    for src, add, out, tag in ((T.TPI, 0.0, T.S2, "S2"), (T.SDI, 256.0, T.SDV, "SDV")):
+        ts(pr[2], src[:], 1.0, OP.add, ["TPI", "SDI"], ["pr2"], 1024.0, OP.mult)
+        tt(pr[3], pr[2], T.SG[:], OP.add, ["pr2", "SG"], ["pr3"])
+        ts(out[:], pr[3], add, OP.add, ["pr3"], [tag], 767.0, OP.max)
+    cp(T.A16[:], ic, ["IC"], ["A16"])
+    ts(T.CBC[:], T.IC[:, 0:8], C["G8"], OP.is_equal, ["IC", "cG8"], ["CBC"], -1024.0, OP.mult)
+    for c in range(8):
+        o = slice(c * 128, c * 128 + 128)
+        ts(T.RCA[:, o], ic, T.CTT[:, c:c + 1], OP.is_ge, ["IC", "CTT"], ["RCA%d" % c], 128.0, OP.mult)
+        ts(T.RCB[:, o], ic, T.CTT[:, c:c + 1], OP.is_equal, ["IC", "CTT"], ["RCB%d" % c], 128.0, OP.mult)
+        ts(T.CB[:, o], T.A16[:], 0.0, OP.mult, ["A16", "CBC"], ["CB%d_%d" % (c // 4, c % 4)], T.CBC[:, c:c + 1], OP.add)
+    for q in range(NR):
+        dma("y", T.F[:, q * 1024:q * 1024 + 256], T.F0[:, q * 256:q * 256 + 256], f0, ["Ft%d" % q])
+    fall = ["Ft%d" % q for q in range(NR)] + ["FW%d" % q for q in range(NR)] + ["Fsr", "Fso0", "Fso1"]
+
+    def run(*gens):
+        now, ready, rk = 0, [0] * len(gens), [0] * len(gens)
+        live = list(range(len(gens)))
+        while live:
+            i = min(live, key=lambda j: (max(ready[j], now), rk[j], j))
+            try:
+                cost, lat, rk[i] = next(gens[i])
+            except StopIteration:
+                live.remove(i)
+                continue
+            now = max(now, ready[i]) + cost
+            ready[i] = now + lat
+
+    bk = [T.BK0, T.BK1]
+
+    def u_mm(q, h, src, tag):
+        o = slice(q * 128, q * 128 + 128)
+
+        def f():
+            out = []
+            for u, wl in enumerate((T.W1L, T.W2L)):
+                mm(bk[h][:, u * 64:u * 64 + 64], T.IB[:], T.MK[:], True, False)
+                out.append(mm(bk[h][:, u * 64:u * 64 + 64], wl[:, o], src, False, True))
+            return out
+        op("t", f, ["IB", "MK", "W1L%d" % q, "W2L%d" % q, tag], ["BK%d" % h])
+
+    def e_load(win, R):
+        for h in range(2):
+            o, l = h * 1024, h * 64
+            act(T.VF[:, o:o + 512], win.indirect(T.LE[:, l:l + 32]), R + ["LE"], ["VFa%d" % h])
+            cp(T.VF[:, o + 512:o + 1024], win.indirect(T.LE[:, l + 32:l + 64]), R + ["LE"], ["VFb%d" % h])
+            act(T.VA[:, o:o + 1024], T.VF[:, o:o + 1024], ["VFa%d" % h, "VFb%d" % h], ["VA%d" % h], AF.Abs)
+
+    def e_gen(h, q):
+        o = slice(h * 1024, h * 1024 + 1024)
+        hh = slice(h * 64, h * 64 + 64)
+        end = slice(h * 1024 + 15, h * 1024 + 1024, 16)
+        scan(T.MX[:, o], T.RM[:], T.VF[:, o], OP.mult, OP.max, ["RM0", "VFa%d" % h, "VFb%d" % h], ["MX%d" % h])
+        yield 500, 400, 0
+        ts(T.HIM[:, hh], T.MX[:, end], -0.5, OP.add, ["MX%d" % h], ["HIM%d" % h])
+        scan(T.MN[:, o], T.R255[:], T.VA[:, o], OP.max, OP.min, ["RM1", "VA%d" % h], ["MN%d" % h])
+        yield 500, 180, 0
+        tt(T.SUM[:, hh], T.HIM[:, hh], T.MN[:, end], OP.add, ["HIM%d" % h, "MN%d" % h], ["SUM%d" % h])
+        yield 120, 180, 0
+        e2 = T["E2%d" % h]
+        tg = "E2%d" % h
+        ts(e2[:], T.SUM[:, hh], MAGIC, OP.add, ["SUM%d" % h], [tg], MAGIC, OP.subtract)
+        u_mm(q, h, e2[:], tg)
+        act(T.EREP[:, o], e2[:].indirect(T.EL[:]), [tg, "EL"], ["EREP%d" % h], scale=0.5)
+        b = h * 64
+        act(T.E2M[:, b:b + 48], e2[:, 0:48], [tg], ["E2Ma%d" % h], AF.Identity, bias=-0.5)
+        act(T.E2M[:, b + 48:b + 64], e2[:, 48:64], [tg], ["E2Mb%d" % h], AF.Identity, bias=-0.5, scale=0.5)
+        act(T.E1[:, b:b + 48], e2[:, 0:48], [tg, "E1z"], ["E1%d" % h], scale=0.5)
+        yield 60, 700, 0
+
+    def hash_gen(p, h, q):
+        x = "%d" % h
+        i = p * 2 + h
+        us, kk, hi = T.US[:, h * 128:h * 128 + 128], T.KK[:, h * 64:h * 64 + 64], T.HI[:, h * 64:h * 64 + 64]
+        ui, ua, pp, vi = T.UI[:, h * 8:h * 8 + 8], T.UA[:, h * 8:h * 8 + 8], T.PP[:, h * 4:h * 4 + 4], T.VI[:, h * 8:h * 8 + 4]
+        scan(us, T.RU[:], bk[h][:, 0:128], OP.add, OP.max, ["RU", "BK" + x], ["US" + x])
+        yield 120, 180, 0
+        cp(ui, T.US[:, h * 128 + 15:h * 128 + 128:16], ["US" + x], ["UI" + x])
+        yield 60, 180, 0
+        ts(ua, ui, 4095, AND, ["UI" + x], ["UA" + x])
+        yield 60, 180, 0
+        tt(pp, T.UA[:, h * 8:h * 8 + 4], T.UA[:, h * 8 + 4:h * 8 + 8], OP.mult, ["UA" + x], ["PP" + x])
+        tt(kk, ua.indirect(T.REP4[:]), T.KC[:, q * 128:q * 128 + 64], OP.mult, ["UA" + x, "REP4", "KC%d" % q], ["KK" + x])
+        yield 230, 120, 0
+        ts(vi, pp, 5, SHR, ["PP" + x], ["VI" + x])
+        yield 60, 180, 0
+        tt(hi, vi.indirect(T.REP[:, 0:4]), kk, OP.add, ["VI" + x, "KK" + x, "REP"], ["HI" + x])
+        yield 150, 180, 0
+        hm = T.HM[:, i * 64:i * 64 + 64]
+        ts(hm, hi, 4095, AND, ["HI" + x], ["HM%d" % i])
+        yield 60, 180, 0
+        cp(T.LH[:, i * 64:i * 64 + 64], hm, ["HM%d" % i], ["LH%d" % i])
+        yield 60, 180, 1
+
+    issued = []
+
+    def cand(p, h, q):
+        i = p * 2 + h
+        x0, l0, e0 = i * 1024, i * 64, h * 1024
+        tz = T.TZ[:, q * W:q * W + W]
+        R = ["TZa%d" % q, "TZb%d" % q, "LH%d" % i]
+        zb, xp = T["Z%d" % h], T["VP%d" % h][:, 0:256]
+        act(T.X[:, x0 + 768:x0 + 1024], tz.indirect(T.LH[:, l0 + 48:l0 + 64]), R, ["X%d_r" % i])
+
+        def f():
+            mm(xp, T.IB[:], T.X[:, x0 + 768:x0 + 1024], True, False)
+            return mm(xp, T.IBN[:], T.EREP[:, e0 + 768:e0 + 1024], False, True)
+        op("t", f, ["IB", "IBN", "X%d_r" % i, "EREP%d" % h], ["VP%d" % h])
+        key = bk[h][:, 128:192]
+
+        def keys():
+            mm(key, T.IB[:], T.PC1[:], True, False)
+            return mm(key, T.IB[:], T.PC2[:, i * 64:i * 64 + 64], False, False)
+        op("t", keys, ["IB", "PC1", "PC2%d" % i], ["BK%d" % h])
+        if h == 1:
+            first_dist(p)
+        tt(T.X[:, x0:x0 + 768], tz.indirect(T.LH[:, l0:l0 + 48]), T.EREP[:, e0:e0 + 768], OP.subtract, R + ["EREP%d" % h], ["X%d_0" % i])
+        act(zb[:, 0:768], T.X[:, x0:x0 + 768], ["X%d_0" % i], ["Z%d_0" % h], AF.Abs)
+        act(zb[:, 768:1024], xp, ["VP%d" % h], ["Z%d_r" % h], AF.Abs)
+        if h == 1:
+            dist(p, 1)
+        yield 400, 2300, 0
+
+    def first_dist(p):
+        if p not in issued:
+            issued.append(p)
+            dist(p, 0)
+
+    def dist(p, h):
+        zb = T["Z%d" % h]
+
+        def f():
+            for k in range(16):
+                r_ = mm(bk[h][:, 128:192], T.WD[:, 15 - k:143 - k], zb[:, k::16], False, k == 15)
+            return r_
+        op("t", f, ["WD", "Z%d_0" % h, "Z%d_r" % h], ["BK%d" % h])
+
+    def names(p, h):
+        i = p * 2 + h
+        ts(T.HC[:, i * 64:i * 64 + 64], T.HM[:, i * 64:i * 64 + 64], -2047.0, OP.add, ["HM%d" % i], ["HC%d" % i])
+
+    def best(p, h):
+        i = p * 2 + h
+        first_dist(p)
+        scan(T.KS[:, i * 64:i * 64 + 64], T.RB[:], bk[h][:, 128:192], OP.max, OP.min, ["RB", "BK%d" % h], ["KS%d" % i])
+
+    def arg_gen(h, q):
+        x = "%d" % h
+        hh = slice(h * 64, h * 64 + 64)
+        best(0, h)
+        yield 60, 180, 0
+        ki = T.KI[:, h * 8:h * 8 + 4]
+        ka = T.KI[:, h * 8 + 4:h * 8 + 8]
+        cp(ki, T.KS[:, h * 64 + 15:h * 64 + 64:16], ["KS" + x], ["KI" + x])
+        yield 60, 180, 0
+        ts(ka, ki, 1023, AND, ["KI" + x], ["KA_" + x])
+        yield 60, 180, 0
+        lp = T.LP[:, h * 8:h * 8 + 4]
+        cp(lp, ka, ["KA_" + x], ["LP" + x])
+        yield 60, 180, 0
+        tt(T.CS[:, hh], T.X[:, h * 1024:h * 1024 + 1024].indirect(lp), T.E2M[:, hh], OP.add,
+           ["X%s_0" % x, "X%s_r" % x, "LP" + x, "E2Ma" + x, "E2Mb" + x], ["CS" + x])
+        yield 160, 180, 0
+        ts(T.C2[:, hh], T.CS[:, hh], MAGIC, OP.add, ["CS" + x], ["C2" + x], MAGIC, OP.subtract)
+        u_mm(q, h, T.C2[:, hh], "C2" + x)
+        yield 60, 700, 0
+
+    def chain(h, q):
+        yield 0, 1100 * h, 0
+        for x in (e_gen(h, q), hash_gen(0, h, q), cand(0, h, q), arg_gen(h, q), hash_gen(1, h, q), cand(1, h, q)):
+            for y in x:
+                yield y
+        names(0, h)
+        yield 60, 0, 0
+        names(1, h)
+        yield 60, 2100, 0
+        best(1, h)
+        yield 60, 0, 0
+
+    def r_mm(b):
+        pk = T["PK%d" % b]
+        mm(pk[:], T.IH[:], T.RCA[:, b * 512:b * 512 + 512], True, False)
+        for c in range(4):
+            mm(pk[:, c * 128:c * 128 + 128], T.IH[:], T.A16[:], False, False)
+        return mm(pk[:], T.IH[:], T.RCB[:, b * 512:b * 512 + 512], False, False)
+
+    def ahead(q):
+        for b in range(2):
+            op("t", lambda: r_mm(b), ["IH", "A16"] + ["RC%s%d" % (x, c) for x in "AB" for c in range(8)], ["PK%d" % b])
+        ts(T.S0M[:], T.S2[:], T.NMX[:, q:q + 1], OP.mult, ["S2", "NMX"], ["S0M"], 767.0, OP.max)
+        yield 150, 0, 0
+
+    for t in range(NR):
+        q = (rank + 1 + t) % NR
+        if t == 0:
+            e_load(T.F0[:, 0:2064], f0)
+        else:
+            e_load(T.F[:], fall)
+        issued.clear()
+        run(chain(0, q), chain(1, q), ahead(q))
+        kf, nf, ps, pm, kl, pia = (T.KFI[:, i * 8:i * 8 + 8] for i in range(6))
+        tt(kf, T.KS[:, 15:128:16], T.KS[:, 143:256:16], OP.min, ["KS0", "KS1", "KS2", "KS3"], ["kf"])
+        ts(nf, kf, T.THK[:, q:q + 1], OP.is_ge, ["kf", "THK"], ["nf"], 256.0, OP.mult)
+        ts(ps, kf, 4095, AND, ["kf"], ["ps"], 4, SHR)
+        tt(pm, nf, ps, OP.max, ["nf", "ps"], ["pm"])
+        cp(T.LN[:], pm, ["pm"], ["LN"])
+        tt(T.HGD[:], T.HC[:].indirect(T.LN[:]), T.DL[:], OP.mult, ["HC0", "HC1", "HC2", "HC3", "HCe", "LN", "DL"], ["HGD"])
+        op("t", lambda: mm(T.HS[:, 0:128], T.HGD[:], T.IH[:], True, True), ["HGD", "IH"], ["HS"])
+
+        def sv():
+            wl = T.WS[:, 15 - 2 * q:143 - 2 * q]
+            mm(T.HS[:, 128:256], wl, T.CW[:], True, False)
+            return mm(T.HS[:, 128:256], wl, T.HGD[:], False, True)
+        op("t", sv, ["WS", "CW", "HGD"], ["HS"])
+        for b in range(2):
+            pk = T["PK%d" % b]
+            op("t", lambda: [mm(pk[:, c * 128:c * 128 + 128], T.BOK[:], T.HGD[:], False, False) for c in range(4)][-1],
+               ["BOK", "HGD"], ["PK%d" % b])
+            if b == 0:
+                cp(T.HTS[:], T.HS[:, 0:128], ["HS"], ["HTS"])
+            op("t", lambda: mm(pk[:], T.HTS[:], T.CB[:, b * 512:b * 512 + 512], False, True),
+               ["HTS"] + ["CB%d_%d" % (b, c) for c in range(4)], ["PK%d" % b])
+        tt(T.S1[:], T.HS[:, 128:256], T.S0M[:], OP.max, ["HS", "S0M"], ["S1"])
+        tt(T.NFT[:], nf, T.CT[:], OP.mult, ["nf", "CT"], ["NFT"])
+        ts(kl, kf, 4095, AND, ["kf"], ["kl"])
+        ts(T.NP1[:], T.S1[:], 10, SHR, ["S1"], ["NP1"])
+        cp(T.LF[:], kl, ["kl"], ["LF"])
+        ts(T.NP2[:], T.S1[:], 10, SHR, ["S1"], ["NP2"])
+        for c in range(8):
+            pk = T["PK%d" % (c // 4)]
+            op("v", lambda: V.tensor_reduce(T.KB[:, c:c + 1], pk[:, (c % 4) * 128:(c % 4) * 128 + 128], AxisListType.X, OP.min,
+                                            apply_absolute_value=True), ["PK%d" % (c // 4)], ["KB%d" % c])
+            if c == 3 and t < NR - 1:
+                tt(T.F[:, q * 1024 + 512:q * 1024 + 640], T.X[:].indirect(T.LF[:]), T.E1[:], OP.add,
+                   ["X%d_%s" % (i, j) for i in range(4) for j in "0r"] + ["LF", "E10", "E11", "E1z"], ["FW%d" % q])
+        tt(T.KBI[:], T.KB[:], T.NFT[:], OP.max, ["KB%d" % c for c in range(8)] + ["NFT"], ["KBI"])
+        tt(T.KBX[:], T.KBI[:].indirect(T.REP[:]), T.DL[:], OP.mult, ["KBI", "REP", "DL"], ["KBX"])
+        ts(pia, T.KBI[:], 127, AND, ["KBI"], ["pia"])
+        op("t", lambda: mm(T.KA[:, 0:128], T.BOH[:], T.KBX[:], True, True), ["BOH", "KBX"], ["KA"])
+        act(T.KRS[:], T.KA[:, 0:128], ["KA"], ["KRS"])
+        cp(T.LPI[:], pia, ["pia"], ["LPI"])
+        act(T.KRP[:], T.KRS[:].indirect(T.LPI[:]), ["KRS", "LPI"], ["KRP"])
+        sp, nq, mnn, cl, bm, dsb, alt, dd = pr
+        am, ef, sa, m_, ds, kep, k0, nan = (T["VP%d" % (i // 4)][:, (i % 4) * 128:(i % 4) * 128 + 128] for i in range(8))
+        tt(nq, T.NP1[:].indirect(T.LPI[:]), T.NP2[:], OP.not_equal, ["NP1", "NP2", "LPI"], ["nq"])
+        tt(mnn, T.NP1[:].indirect(T.LPI[:]), T.NP2[:], OP.min, ["NP1", "NP2", "LPI"], ["mnn"])
+        cp(sp, T.S1[:].indirect(T.LPI[:]), ["S1", "LPI"], ["sp"])
+        ts(am, T.KRS[:], 128.0, OP.is_ge, ["KRS", "VP0", "VP1"], ["am"])
+        tt(cl, nq, mnn, OP.mult, ["nq", "mnn"], ["cl"])
+        tt(sa, sp, am, OP.mult, ["sp", "am"], ["sa"])
+        tt(bm, T.KRP[:], T.C128[:], OP.is_equal, ["KRP", "C128"], ["bm"])
+        tt(m_, T.S1[:], sa, OP.max, ["S1", "sa"], ["m"])
+        tt(ef, am, bm, OP.max, ["am", "bm"], ["ef"])
+        tt(ds, T.SDV[:], m_, OP.subtract, ["SDV", "m"], ["ds"])
+        tt(T.CLE[:], cl, ef, OP.mult, ["cl", "ef"], ["CLE"])
+        op("t", lambda: mm(T.KA[:, 128:256], T.BOB[:], T.CLE[:], True, True), ["BOB", "CLE"], ["KA"])
+        tt(dsb, ds, bm, OP.mult, ["ds", "bm"], ["dsb"])
+        ts(kep, T.CLE[:], 0.0, OP.is_equal, ["CLE"], ["kep"])
+        tt(alt, m_, dsb, OP.add, ["m", "dsb"], ["alt"])
+        tt(k0, T.S1[:], kep, OP.mult, ["S1", "kep"], ["k0"])
+        ts(k0, k0, 767.0, OP.max, ["k0"], ["k0"])
+        ts(nan, T.KA[:, 128:256], 0.0, OP.is_equal, ["KA"], ["nan"])
+        tt(dd, alt, k0, OP.subtract, ["alt", "k0"], ["dd"])
+        tt(dsb, dd, nan, OP.mult, ["dd", "nan"], ["dsb"])
+        tt(T.S2[:], k0, dsb, OP.add, ["k0", "dsb", "VP0", "VP1"], ["S2"])
+        if t < NR - 1:
+            ts(T.L0T[:], T.S2[:], 1023, AND, ["S2"], ["L0T"])
+            ts(T.LE[:], T.L0T[:], C["QB"], OP.add, ["L0T", "cQB"], ["LE"])
+    ts(T.L0T[:], T.S2[:], 10, SHR, ["S2"], ["L0T"])
+    ts(T.YO[:], T.L0T[:], -1.0, OP.add, ["L0T"], ["YO"])
+    dma("y", T.yp[:], T.YO[:], ["YO"], ["yp"])
+
+    need = {"v": cnt["v"], "s": cnt["s"], "t": cnt["t"], "gp": cnt["g"], "ls": ls[0], "nm": 7, "hn": 7, "ft": 7, "fs": 7}
+    for i in range(ndma[0]):
+        need["d%d" % i] = 16
+    for q in range(NR):
+        if q != rank:
+            need["ta%d" % q] = 8
+            need["tb%d" % q] = ntb[q]
+    wait("y", need)

@@ -4,28 +4,31 @@ from concourse.mybir import AluOpType, AxisListType, ActivationFunctionType
 OP = AluOpType
 AF = ActivationFunctionType
 NR, W = 8, 4096
-MAGIC = 25165824.0
+H2, Q4 = W // 2, W // 4
+MSG = 272
+FT, FS, FW = 16, 16 + NR * MSG, 16 + NR * MSG + 2048
+WAKE = 160
 
 f32, b16, h16, i32, u16 = "float32", "bfloat16", "float16", "int32", "uint16"
 SCRATCH = {}
 for _d, _l in (
-        (b16, "TZ 32768 F 8192 F0 2064 X 4096 Z0 1024 Z1 1024 VF 2048 VA 2048 MX 2048 MN 2048 EREP 2048 SB 4096 Y 4096 RM 1024 R255 1024 "
-              "BOB 128 IB 128 IBN 128 WD 144 MK 64 PC1 64 PC2 256 W1L 1024 W2L 1024 C2 128 E20 64 E21 64 E1 128 CLE 128"),
-        (h16, "TPH 256 PERM 512 NMO 256 NM 256 NMT 256 SW 272 HWO 4 HWN 64 BOH 128 BOK 128 IH 128 WS 144 RCA 1024 RCB 1024 CB 1024 "
-              "A16 128 CW 128 KX 1024 HGD 128 HTS 128 KBX 128"),
-        (i32, "TPI 128 SDI 128 HWI 3 THI 1 IP 16 IC 256 IC15 256 ICG 128 C48 64 L0T 128 S2 128 UI 16 UA 16 PP 8 VI 16 HI 128 HM 256 KI 16 "
-              "KFI 64 S1 128 NP1 128 NP2 128 KBI 8"),
-        (u16, "EL 64 REP 8 REP4 4 LL 256 LE 128 LH 256 LP 16 LN 8 LF 8 LPI 8"),
-        (f32, "COL 32 DL 128 RU 128 RB 64 CWT 128 C128 128 CT 8 CTT 8 CBC 8 SG 128 NMX 8 W1F 8 W2F 8 KCF 8 THK 8 KC 1024 SDV 128 S0M 128 "
-              "US 256 KK 128 HC 272 KS 256 CS 128 E2M 128 HIM 128 SUM 128 NFT 8 KB 8 KRS 128 KRP 128 PR 1024 YO 128")):
+        (b16, "TZ 32768 F 5136 X 4224 Z0 1024 Z1 1024 VF 2048 VA 2048 MX 2048 MN 2048 EREP 2048 SBT 2176 SBS 2048 Y 4096 RM 512 R255 512 "
+              "BOB 128 BON 128 IB 128 IBN 128 WD 144 MK 128 PC 256 E2 128 E1 128 FLW 272 NE1 128 NE2 128 KRP 128 M1 128 MU 128 CSEL 8 TI2 256"),
+        (h16, "TPH 256 PERM 512 NMO 256 NM 256 NMT 256 SW 272 BOH 128 IH 128 WS 144 RR 512 SGP 1024 SGN 1024 "
+              "A16 128 KX 128 HGD 128 W1L 1024 W2L 1024 NEG 64 E2H 128 C2 128"),
+        (i32, "TPI 128 SDI 128 HWI 3 THI 1 HT 16 IP 16 IC 256 IC15 256 ICG 128 UI 16 UA 16 PP 8 VI 16 HI 128 HM 256 KI 16 KF 16"),
+        (u16, "EL 64 REP 8 LL 256 LE 128 LH 256 LP 16 LN 8 LF 8 LQ 8"),
+        (f32, "COL 32 DL 128 RB 64 CT 8 CBC 16 NMX 8 ISX 8 IX2 8 KCF 8 THK 8 KC 1024 US 384 KK 128 HC 272 KS 256 E2M 128 HIM 128 "
+              "SENT 8 KF1 8 KB 8 KRS 144 NMW 144 SLW 144 IF 128 TI 128 TPS 128 SDS 128 SDN 128 NMI 128 NM0 128 FLN 128 SL0 128 WSL 128 "
+              "MS 128 MQ 128 D0 512 DS 512 DN 512 SS 512 SN 512 PR 256 YO 128")):
     _l = _l.split()
     for _i in range(0, len(_l), 2):
         SCRATCH[_l[_i]] = ("sbuf", [128, int(_l[_i + 1])], _d)
 BANKS = ("BK0", "BK1", "PK0", "PK1", "HS", "KA", "VP0", "VP1")
 for _n in BANKS:
     SCRATCH[_n] = ("psum", [128, 512], f32)
-SEMAPHORES = ["v", "s", "t", "gp", "nm", "hn", "ft", "fs", "ls", "hz0", "hz1"] + ["d%d" % i for i in range(20)] + \
-    ["ta%d" % q for q in range(NR)] + ["tb%d" % q for q in range(NR)]
+SEMAPHORES = ["v", "s", "t", "gp", "nm", "ft", "fs", "ls", "hz0", "hz1", "hz2"] + ["d%d" % i for i in range(8)] + \
+    ["tz%d" % q for q in range(NR)]
 
 
 def mask_of(engs):
@@ -44,6 +47,46 @@ def places(T, topo):
     return chips, relay
 
 
+def order_calls(ops):
+    succ = [[] for _ in ops]
+    for i, o in enumerate(ops):
+        for j, lat in o["pre"].items():
+            succ[j].append((i, lat))
+    tail = [0.0] * len(ops)
+    for i in range(len(ops) - 1, -1, -1):
+        tail[i] = ops[i]["ns"] + max([lat + tail[j] for j, lat in succ[i]] + [0.0])
+    left = [len(o["pre"]) for o in ops]
+    ready = [0.0] * len(ops)
+    free, pool, out = {}, {}, []
+    for i, o in enumerate(ops):
+        free[o["e"]] = 0.0
+        pool.setdefault(o["e"], [])
+        if not left[i]:
+            pool[o["e"]].append(i)
+    while len(out) < len(ops):
+        e = min((x for x in pool if pool[x]), key=lambda x: max(free[x], min(ready[i] for i in pool[x])))
+        now = max(free[e], min(ready[i] for i in pool[e]))
+        rows = sorted(pool[e], key=lambda i: (-tail[i], i))
+        pick = None
+        for n, i in enumerate(rows):
+            if ready[i] <= now and all(now + ops[i]["ns"] <= ready[j] + 30 or ready[j] + ops[j]["ns"] + tail[i] > now + ops[i]["ns"] + tail[j]
+                                       for j in rows[:n]):
+                pick = i
+                break
+        if pick is None:
+            free[e] = min(ready[i] for i in pool[e] if ready[i] > now)
+            continue
+        pool[e].remove(pick)
+        out.append(pick)
+        free[e] = now + ops[pick]["ns"]
+        for j, lat in succ[pick]:
+            ready[j] = max(ready[j], free[e] + lat)
+            left[j] -= 1
+            if not left[j]:
+                pool[ops[j]["e"]].append(j)
+    return out
+
+
 def rank_program(g, core, T, topo):
     chips, relay = places(T, topo)
     ncl = len(chips)
@@ -53,106 +96,116 @@ def rank_program(g, core, T, topo):
         n = [i for i in range(ncl) if r in chips[i]][0]
         return [T.cores[chips[(n - 1 - d) % ncl][-1]] for d in range(ncl - 1)]
 
+    def did(c):
+        a = topo.addr(c)
+        return DstId(rid=a[0], pnc=a[1])
+
     def send(dst, lo, hi, sem, engs):
         rid, pid = topo.addr(dst)[:2]
         g.remote_dma(T.TZ[:, lo:hi], T.TZ[:, lo:hi], T.sem[sem], T.sem.ls, pid, rid, mask_of(engs))
         ls[0] += len(engs)
 
     rank = T.rank_of(core)
-    H2, Q4 = W // 2, W // 4
     if rank is None:
         for r in range(NR):
             if relay[r] == core:
+                mine = [c for c in chips if r in c][0]
+                if r == mine[-1]:
+                    d = targets(r)[0]
+                    g.wait_ge(T.sem.hz2, 4)
+                    send(d, mine[0] * W + Q4, mine[0] * W + H2, "tz%d" % mine[0], topo.engines(core, d)[:8])
                 for n, d in enumerate(targets(r)):
                     for i in range(2):
                         if n == 0:
-                            g.wait_ge(T.sem["hz%d" % i], 8)
+                            g.wait_ge(T.sem["hz%d" % i], 4 if i == 0 and r != mine[-1] else 8)
                         o = r * W + H2 + i * Q4
-                        send(d, o, o + Q4, "tb%d" % r, topo.engines(core, d)[:8])
+                        send(d, o, o + Q4, "tz%d" % r, topo.engines(core, d)[:8])
                 g.wait_ge(T.sem.ls, ls[0])
         return
 
-    Q = {"v": g.vector, "s": g.scalar, "t": g.tensor, "g": g, "y": g.sync}
-    SEM = {"v": "v", "s": "s", "t": "t", "g": "gp"}
-    cnt = {e: 0 for e in SEM}
-    clk = {e: {} for e in Q}
-    hist, lastw, readers, ndma = {}, {}, {}, [0]
+    ops, lastw, readers = [], {}, {}
 
-    def wait(e, need):
-        for s, n in sorted(need.items()):
-            if clk[e].get(s, 0) < n:
-                Q[e].wait_ge(T.sem[s], n)
-                for s2, n2 in hist.get((s, n), {}).items():
-                    clk[e][s2] = max(clk[e].get(s2, 0), n2)
-                clk[e][s] = max(clk[e].get(s, 0), n)
+    def op(e, fn, R, Wt, ns, kind="c"):
+        me = len(ops)
+        pre, sems, ext = {}, set(), []
 
-    def deps(e, R, Wt):
-        toks = [k for tg in R for k in lastw.get(tg, ())]
-        toks += [k for tg in R if tg in BANKS for k in readers.get(tg, {}).items() if k[0] != SEM.get(e)]
-        toks += [k for tg in Wt for k in lastw.get(tg, ()) if not (e == "t" and k[0] == "t")]
-        toks += [k for tg in Wt for k in readers.get(tg, {}).items() if k[0] != SEM.get(e)]
-        need = {}
-        for s, n in toks:
-            need[s] = max(need.get(s, 0), n)
-        return need
-
-    def done(tok, R, Wt):
+        def edge(j, signal):
+            lat = ops[j]["lat"] if signal else 0.0
+            pre[j] = max(pre.get(j, 0.0), lat)
+            if signal:
+                sems.add(j)
         for tg in R:
-            readers.setdefault(tg, {})[tok[0]] = tok[1]
+            w = lastw.get(tg)
+            if isinstance(w, tuple):
+                ext.append(w[:2])
+                pre[w[2]] = max(pre.get(w[2], 0.0), w[3])
+            elif w is not None:
+                edge(w, True)
+            if tg in BANKS:
+                for j in readers.get(tg, ()):
+                    edge(j, ops[j]["e"] != e)
         for tg in Wt:
-            lastw[tg] = [tok]
-            readers[tg] = {}
-
-    def op(e, fn, R, Wt):
-        wait(e, deps(e, R, Wt))
-        ins = fn()
-        for i in (ins if isinstance(ins, list) else [ins]):
-            i.then_inc(T.sem[SEM[e]], 1)
-            cnt[e] += 1
-            hist[(SEM[e], cnt[e])] = dict(clk[e])
-        done((SEM[e], cnt[e]), R, Wt)
-
-    def dma(e, out, in_, R, Wt):
-        wait(e, deps(e, R, Wt))
-        s = "d%d" % ndma[0]
-        ndma[0] += 1
-        Q[e].dma_start(out, in_).then_inc(T.sem[s], 16)
-        hist[(s, 16)] = dict(clk[e])
-        done((s, 16), R, Wt)
+            if tg in lastw:
+                edge(lastw[tg], not (e == ops[lastw[tg]]["e"] and e in "tg"))
+            for j in readers.get(tg, ()):
+                edge(j, True)
+        ops.append({"e": e, "fn": fn, "pre": pre, "sems": sems, "ext": ext, "ns": ns, "kind": kind,
+                    "lat": WAKE + (2200.0 if kind == "d" else 60.0 if e == "t" else 0.0)})
+        for tg in R:
+            readers.setdefault(tg, []).append(me)
+        for tg in Wt:
+            lastw[tg] = me
+            readers[tg] = []
+        return me
 
     V, S, PE = g.vector, g.scalar, g.tensor
     mm = PE.matmul
 
-    def ts(out, a, s1, o1, R, Wt, s2=None, o2=None):
+    def ns(n, k=1.0):
+        return max(53.0, 0.83 * n * k)
+
+    def gns(n):
+        return 55.0 + 1.25 * n
+
+    def dma(e, out, in_, R, Wt):
+        op(e, lambda: {"y": g.sync, "s": S}[e].dma_start(out, in_), R, Wt, 60.0, "d")
+
+    def ts(out, a, s1, o1, R, Wt, s2=None, o2=None, t=53.0):
         if o2 is None:
-            op("v", lambda: V.tensor_scalar(out, a, s1, None, o1), R, Wt)
+            op("v", lambda: V.tensor_scalar(out, a, s1, None, o1), R, Wt, t)
         else:
-            op("v", lambda: V.tensor_scalar(out, a, s1, s2, o1, o2), R, Wt)
+            op("v", lambda: V.tensor_scalar(out, a, s1, s2, o1, o2), R, Wt, t)
 
-    def tt(out, a, b, o, R, Wt):
-        op("v", lambda: V.tensor_tensor(out, a, b, o), R, Wt)
+    def tt(out, a, b, o, R, Wt, t=53.0):
+        op("v", lambda: V.tensor_tensor(out, a, b, o), R, Wt, t)
 
-    def cp(out, a, R, Wt):
-        op("v", lambda: V.tensor_copy(out, a), R, Wt)
+    def cp(out, a, R, Wt, t=53.0):
+        op("v", lambda: V.tensor_copy(out, a), R, Wt, t)
 
-    def fill(ap, x, Wt):
-        op("v", lambda: V.memset(ap, x), [], Wt)
+    def fill(ap, x, Wt, t=53.0):
+        op("v", lambda: V.memset(ap, x), [], Wt, t)
 
-    def scan(out, d0, d1, o0, o1, R, Wt):
-        op("v", lambda: V.tensor_tensor_scan(out, d0, d1, 0.0, o0, o1), R, Wt)
+    def scan(out, d0, d1, o0, o1, R, Wt, t=53.0):
+        op("v", lambda: V.tensor_tensor_scan(out, d0, d1, 0.0, o0, o1), R, Wt, t)
 
-    def act(out, a, R, Wt, func=AF.Copy, bias=0.0, scale=1.0):
-        op("s", lambda: S.activation(out, a, func, bias=bias, scale=scale), R, Wt)
+    def act(out, a, R, Wt, func=AF.Copy, bias=0.0, scale=1.0, t=53.0):
+        op("s", lambda: S.activation(out, a, func, bias=bias, scale=scale), R, Wt, t)
+
+    def pe(calls, R, bank, cols):
+        op("t", lambda: [mm(*c) for c in calls][-1 if len(calls) == 16 else 0:], R, [bank], 0.5 * cols)
+
+    def rem(fn, R):
+        return op("g", fn, R, ["g"], 700.0, "r")
 
     z0 = rank * W
     dma("y", T.TPI[:], T.tp[:], [], ["TPI"])
     dma("s", T.SDI[:], T.sd[:], [], ["SDI"])
+    dma("y", T.TZ[:, z0:z0 + H2], T.tz[:, 0:H2], [], ["TZa"])
+    dma("s", T.TZ[:, z0 + H2:z0 + W], T.tz[:, H2:W], [], ["TZb"])
     dma("y", T.HWI[:], T.hw[:], [], ["HWI"])
     dma("s", T.THI[:], T.th[:], [], ["THI"])
-    dma("y", T.TZ[:, z0:z0 + H2], T.tz[:, 0:H2], [], ["TZa%d" % rank])
-    dma("s", T.TZ[:, z0 + H2:z0 + W], T.tz[:, H2:W], [], ["TZb%d" % rank])
-    op("g", lambda: g.iota(T.IP[:, 0:1], [[0, 1]], 0, 1), [], ["IP"])
-    op("g", lambda: g.iota(T.IC[:], [[1, 256]], 0, 0), [], ["IC"])
+    op("g", lambda: g.iota(T.IP[:, 0:1], [[0, 1]], 0, 1), [], ["IP", "g"], 130.0)
+    op("g", lambda: g.iota(T.IC[:], [[1, 256]], 0, 0), [], ["IC", "g"], 560.0)
 
     C = {}
     ip = {"P": T.IP[:, 0:1]}
@@ -164,8 +217,9 @@ def rank_program(g, core, T, topo):
 
     def col(name, src, s1, o1, s2=None, o2=None, R=()):
         i = len(C)
+        a = C[src[1:]] if src[0] == "c" else ip[src]
         C[name] = T.COL[:, i:i + 1]
-        ts(C[name], src, s1, o1, ["IP"] + ["i" + x for x in ip] + list(R), ["c" + name], s2, o2)
+        ts(C[name], a, s1, o1, ["IP", src if src[0] == "c" else "i" + src] + list(R), ["c" + name], s2, o2)
 
     AND, SHR = OP.bitwise_and, OP.arith_shift_right
     icol("K", 15, AND)
@@ -176,493 +230,425 @@ def rank_program(g, core, T, topo):
     icol("B4", 4, SHR, 1, AND)
     icol("B5", 5, SHR)
     icol("L", 7, AND)
-    col("S8", ip["S"], 8.0, OP.mult)
-    col("G8", ip["G"], 1.0, OP.mult)
-    col("PM0", ip["Q"], 16.0, OP.mult, C["S8"], OP.add, ["cS8"])
-    col("PM", C["PM0"], C["G8"], OP.add, None, None, ["cPM0", "cG8"])
-    col("P", ip["P"], 1.0, OP.mult)
-    ts(T.PERM[:, 0:256], T.IC[:], C["PM"], OP.is_equal, ["IC", "cPM"], ["PERM0"])
-    ts(T.PERM[:, 256:512], T.IC[:], -16.0, OP.add, ["IC", "cPM"], ["PERM1"], C["PM"], OP.is_equal)
-    ts(T.IH[:], T.IC[:, 0:128], C["P"], OP.is_equal, ["IC", "cP"], ["IH"])
-    ts(T.TPH[:, 0:128], T.TPI[:], -2047.0, OP.add, ["TPI"], ["TPH0"])
-    ts(T.TPH[:, 128:256], T.SDI[:], -2047.0, OP.add, ["SDI"], ["TPH1"])
-
-    def turn():
-        mm(T.HS[:, 0:256], T.TPH[:, 0:128], T.PERM[:, 0:256], True, False)
-        return mm(T.HS[:, 0:256], T.TPH[:, 128:256], T.PERM[:, 256:512], False, True)
-    op("t", turn, ["TPH0", "TPH1", "PERM0", "PERM1"], ["HS"])
-    cp(T.HWO[:, 0:3], T.HWI[:], ["HWI"], ["HWO0"])
-    ts(T.HWO[:, 3:4], T.THI[:], -2048.0, OP.add, ["THI"], ["HWO1"])
-    cp(T.NMO[:], T.HS[:, 0:256], ["HS"], ["NMO"])
+    col("S8", "S", 8.0, OP.mult)
+    col("G8", "G", 1.0, OP.mult)
+    col("PM0", "Q", 16.0, OP.mult, C["S8"], OP.add, ["cS8"])
+    col("PM", "cPM0", C["G8"], OP.add, None, None, ["cG8"])
+    col("P", "P", 1.0, OP.mult)
+    ic = T.IC[:, 0:128]
+    ts(T.PERM[:, 0:256], T.IC[:], C["PM"], OP.is_equal, ["IC", "cPM"], ["PERM0"], t=212)
+    ts(T.PERM[:, 256:512], T.IC[:], -16.0, OP.add, ["IC", "cPM"], ["PERM1"], C["PM"], OP.is_equal, t=212)
+    ts(T.IH[:], ic, C["P"], OP.is_equal, ["IC", "cP"], ["IH"], t=106)
+    ts(T.TPH[:, 0:128], T.TPI[:], -2047.0, OP.add, ["TPI"], ["TPH0"], t=106)
+    ts(T.TPH[:, 128:256], T.SDI[:], -2047.0, OP.add, ["SDI"], ["TPH1"], t=106)
+    pe([(T.HS[:, 0:256], T.TPH[:, 0:128], T.PERM[:, 0:256], True, False),
+        (T.HS[:, 0:256], T.TPH[:, 128:256], T.PERM[:, 256:512], False, True)], ["TPH0", "TPH1", "PERM0", "PERM1"], "HS", 512)
+    cp(T.NMO[:], T.HS[:, 0:256], ["HS"], ["NMO"], 212)
     cp(T.NM[:, rank * 32:rank * 32 + 32], T.NMO[:, rank * 32:rank * 32 + 32], ["NMO"], ["NMo"])
-    cp(T.HWN[:, rank * 8:rank * 8 + 4], T.HWO[:], ["HWO0", "HWO1"], ["HWo"])
 
     mine = [c for c in chips if rank in c][0]
-    far = [r for r in range(NR) if r not in mine]
+    here = chips.index(mine)
+    far = [r for d in range(1, ncl) for r in chips[(here + d) % ncl]]
     near = [r for r in mine if r != rank][0]
     others = far + [near]
     last = rank == mine[-1]
     fe = topo.engines(core, T.cores[far[0]])
     ne = [e for e in topo.engines(core, T.cores[near]) if e not in fe]
-    slots = fe[:6] + [fe[6]] if last else fe[4:] + fe[4:6] + [ne[0]]
 
-    def did(r):
-        a = topo.addr(T.cores[r])
-        return DstId(rid=a[0], pnc=a[1])
+    def spread(src, dst, sem):
+        for n in range(0, len(far), 2):
+            to = [(far[n], fe[:4]), (far[n + 1], fe[4:8])] + ([(near, ne[:4])] if n == 0 else [])
+            g.remote_dma_fused([RemoteDMATransfer(dst_ids=[did(T.cores[r])], dma_engine_mask=mask_of(e), remote_sem=T.sem[sem],
+                                                  srcs=[src(r)], dsts=[dst]) for r, e in to], local_sem=T.sem.ls)
+            ls[0] += 4 * len(to)
 
-    def spread(src, dst, sem, engs):
-        todo = [(r, e) for r, e in zip(others, engs)]
-        while todo:
-            tr, seen, rest = [], [], []
-            for r, e in todo:
-                if e in seen:
-                    rest.append((r, e))
-                else:
-                    seen.append(e)
-                    tr.append(RemoteDMATransfer(dst_ids=[did(r)], dma_engine_mask=1 << e, remote_sem=T.sem[sem], srcs=[src(r)], dsts=[dst]))
-            g.remote_dma_fused(tr, local_sem=T.sem.ls)
-            ls[0] += len(tr)
-            todo = rest
+    sent = rem(lambda: spread(lambda r: T.NMO[:, r * 32:r * 32 + 32], T.NM[:, rank * 32:rank * 32 + 32], "nm"), ["NMO"])
+    lastw["NM"] = ("nm", 28, sent, 5000.0)
 
-    wait("g", deps("g", ["NMO"], []))
-    spread(lambda r: T.NMO[:, r * 32:r * 32 + 32], T.NM[:, rank * 32:rank * 32 + 32], "nm", fe)
-    wait("g", deps("g", ["HWO0", "HWO1"], []))
-    g.remote_dma_fused([RemoteDMATransfer(dst_ids=[did(r) for r in others], dma_engine_mask=1 << fe[7], remote_sem=T.sem.hn, srcs=[T.HWO[:]],
-                                          dsts=[T.HWN[:, rank * 8:rank * 8 + 4] for _ in others])], local_sem=T.sem.ls)
-    ls[0] += 1
-    lastw["NM"], lastw["HWN"] = [("nm", 7)], [("hn", 7)]
-
-    def direct(d, engs):
-        wait("g", deps("g", ["TZa%d" % rank], []))
-        for i in range(8 // len(engs)):
-            n = H2 * len(engs) // 8
-            send(d, z0 + i * n, z0 + i * n + n, "ta%d" % rank, engs)
-
-    def to_relay():
-        wait("g", deps("g", ["TZb%d" % rank], []))
-        for i in range(2):
-            send(relay[rank], z0 + H2 + i * Q4, z0 + H2 + (i + 1) * Q4, "hz%d" % i, ne[:8])
+    def first_quarters():
+        to = [(targets(rank)[0], 0, "tz%d" % rank, fe[:8]), (relay[near], 1, "hz2", ne[:4]), (relay[rank], 2, "hz0", ne[4:8])]
+        g.remote_dma_fused([RemoteDMATransfer(dst_ids=[did(d)], dma_engine_mask=mask_of(e), remote_sem=T.sem[s],
+                                              srcs=[T.TZ[:, z0 + i * Q4:z0 + (i + 1) * Q4]], dsts=[T.TZ[:, z0 + i * Q4:z0 + (i + 1) * Q4]])
+                            for d, i, s, e in to], local_sem=T.sem.ls)
+        ls[0] += 16
+        send(relay[rank], z0 + 3 * Q4, z0 + W, "hz1", ne[:8])
 
     def hand_on(q):
-        for h, x in enumerate("ab"):
-            wait("g", deps("g", ["TZ%s%d" % (x, q)], []))
-            send(T.cores[near], q * W + h * H2, q * W + (h + 1) * H2, "t%s%d" % (x, q), ne)
+        rem(lambda: send(T.cores[near], q * W, (q + 1) * W, "tz%d" % q, ne[:8]), ["TZa", "TZb"] if q == rank else ["TZ%d" % q])
 
     if last:
         hand_on(rank)
+        rem(lambda: [send(relay[rank], z0 + H2 + i * Q4, z0 + H2 + (i + 1) * Q4, "hz%d" % i, ne[:8]) for i in range(2)], ["TZb"])
     else:
-        direct(targets(rank)[0], fe[:4])
-        to_relay()
-    ntb = {q: 16 if last and q in far else 8 for q in range(NR)}
-    for q in range(NR):
-        if q != rank:
-            lastw["TZa%d" % q] = [("ta%d" % q, 8)]
-            lastw["TZb%d" % q] = [("tb%d" % q, ntb[q])]
+        rem(first_quarters, ["TZa", "TZb"])
+    ntz = {q: (32 if q == far[0] else 24) if last and q in far else 8 for q in range(NR) if q != rank}
 
-    col("K", ip["K"], 1.0, OP.mult)
-    col("PG", ip["G"], 16.0, OP.mult)
-    col("PGF", C["PG"], 15.0, OP.add, None, None, ["cPG"])
-    col("QB", ip["Q"], 512.0, OP.mult)
-    col("S128", ip["S"], 128.0, OP.mult)
-    col("E0", ip["K"], 0.0, OP.is_equal)
-    col("E1", ip["K"], 1.0, OP.is_equal, 2048.0, OP.mult)
-    col("J128", ip["K"], 128.0, OP.mult)
-    col("B3", ip["B3"], 8.0, OP.add)
-    col("R2", ip["B5"], 2.0, OP.mult, C["B3"], OP.add, ["cB3"])
-    col("SW", ip["L"], 16.0, OP.mult, C["R2"], OP.add, ["cR2"])
-    col("T1", ip["B4"], 1.0, OP.mult)
-    col("T0", ip["B4"], 0.0, OP.is_equal)
-    ic = T.IC[:, 0:128]
+    col("K", "K", 1.0, OP.mult)
+    col("B3", "B3", 8.0, OP.add)
+    col("R2", "B5", 2.0, OP.mult, C["B3"], OP.add, ["cB3"])
+    col("SW", "L", 16.0, OP.mult, C["R2"], OP.add, ["cR2"])
+    col("T1", "B4", 1.0, OP.mult)
+    col("T0", "B4", 0.0, OP.is_equal)
     for ty in range(2):
-        ts(T.SW[:, ty * 136:ty * 136 + 136], T.IC[:, 0:136], C["SW"], OP.is_equal, ["IC", "cSW", "cT%d" % ty], ["SW%d" % ty], C["T%d" % ty], OP.mult)
-    fill(T.F0[:, 2048:2064], -256.0, ["F0e"])
-    ts(T.L0T[:], ic, C["J128"], OP.add, ["IC", "cJ128"], ["L0T"])
-    pr = [T.PR[:, i * 128:i * 128 + 128] for i in range(8)]
-    ts(pr[0], T.TPI[:], 0.0, OP.is_lt, ["TPI"], ["pr0"], 2048.0, OP.mult)
-    tt(pr[1], T.L0T[:], pr[0], OP.max, ["L0T", "pr0"], ["pr1"])
-    cp(T.LE[:], pr[1], ["pr1"], ["LE"])
-    for b, (x, y) in enumerate(((0.0, 1.0), (255.0, 0.0))):
-        rm = (T.RM, T.R255)[b]
-        fill(rm[:], y, ["RM%d" % b])
-        fill(rm[:, 0::16], x, ["RM%d" % b])
-    fill(T.RU[:], 0.0, ["RU"])
-    fill(T.RU[:, 0::16], -1e9, ["RU"])
-    fill(T.RB[:], 0.0, ["RB"])
-    fill(T.RB[:, 0::16], 1e9, ["RB"])
-    op("t", lambda: [mm(T.HS[:, b * 128:b * 128 + 128], T.NM[:, b * 128:b * 128 + 128], T.IH[:], True, True) for b in range(2)],
-       ["NM", "NMo", "IH"], ["HS"])
-    cp(T.NMT[:], T.HS[:, 0:256], ["HS"], ["NMT"])
-
-    def back():
-        out = []
-        for ty in range(2):
-            o = T.KA[:, ty * 128:ty * 128 + 128]
-            mm(o, T.SW[:, ty * 136 + 8:ty * 136 + 136], T.NMT[:, 0:128], True, False)
-            out.append(mm(o, T.SW[:, ty * 136:ty * 136 + 128], T.NMT[:, 128:256], False, True))
-        return out
-    op("t", back, ["SW0", "SW1", "NMT"], ["KA"])
-    ts(T.LL[:], T.KA[:, 0:256], 2047.0, OP.add, ["KA"], ["LL"], 0.0, OP.max)
-    tzo = ["TZa%d" % rank, "TZb%d" % rank]
+        ts(T.SW[:, ty * 136:ty * 136 + 136], T.IC[:, 0:136], C["SW"], OP.is_equal, ["IC", "cSW", "cT%d" % ty], ["SW%d" % ty],
+           C["T%d" % ty], OP.mult, t=113)
+    pe([(T.HS[:, b * 128:b * 128 + 128], T.NM[:, b * 128:b * 128 + 128], T.IH[:], True, True) for b in range(2)], ["NM", "NMo", "IH"], "HS", 256)
+    cp(T.NMT[:], T.HS[:, 0:256], ["HS"], ["NMT"], 212)
+    for ty in range(2):
+        o = T.KA[:, ty * 128:ty * 128 + 128]
+        pe([(o, T.SW[:, ty * 136 + 8:ty * 136 + 136], T.NMT[:, 0:128], True, False),
+            (o, T.SW[:, ty * 136:ty * 136 + 128], T.NMT[:, 128:256], False, True)], ["SW0", "SW1", "NMT"], "KA", 256)
+    ts(T.LL[:], T.KA[:, 0:256], 2047.0, OP.add, ["KA"], ["LL"], 0.0, OP.max, t=212)
+    fill(T.HT[:, 7:16], 0, ["HT0"])
+    cp(T.HT[:, 0:2], T.HWI[:, 0:2], ["HWI"], ["HT1"])
+    ts(T.HT[:, 2:3], T.HWI[:, 2:3], 3840, AND, ["HWI"], ["HT2"])
+    ts(T.HT[:, 3:4], T.HWI[:, 2:3], 255, AND, ["HWI"], ["HT3"])
+    ts(T.HT[:, 6:7], T.THI[:], 4095.0, OP.min, ["THI"], ["HT6"])
+    ts(T.HT[:, 4:5], T.HT[:, 6:7], 3840, AND, ["HT6"], ["HT4"])
+    ts(T.HT[:, 5:6], T.HT[:, 6:7], 255, AND, ["HT6"], ["HT5"])
 
     def feats(ty):
-        y0 = ty * 2048
+        y0, wid, sb, f0 = ty * 2048, (MSG, 256)[ty], (T.SBT, T.SBS)[ty], (FT, FS)[ty]
         win = T.TZ[:, z0:z0 + W]
-        act(T.Y[:, y0:y0 + 1024], win.indirect(T.LL[:, ty * 128:ty * 128 + 64]), tzo + ["LL"], ["Ya%d" % ty])
-        cp(T.Y[:, y0 + 1024:y0 + 2048], win.indirect(T.LL[:, ty * 128 + 64:ty * 128 + 128]), tzo + ["LL"], ["Yb%d" % ty])
-        for r in others + [rank]:
+        act(T.Y[:, y0:y0 + 1024], win.indirect(T.LL[:, ty * 128:ty * 128 + 64]), ["TZa", "TZb", "LL"], ["Ya%d" % ty], t=gns(1024))
+        cp(T.Y[:, y0 + 1024:y0 + 2048], win.indirect(T.LL[:, ty * 128 + 64:ty * 128 + 128]), ["TZa", "TZb", "LL"], ["Yb%d" % ty], gns(1024))
+        tags = []
+        for n, r in enumerate(others + [rank]):
+            buf, o = (T.F, f0 + r * wid) if r == rank else (sb, r * wid)
             for s in range(2):
-                src = T.Y[:, y0 + 2 * r + s:y0 + 2048:16]
-                o = r * 512 + ty * 256 + s * 128
-                out, tag = T.SB[:, o:o + 128], "SB%d_%d_%d" % (r, ty, s)
-                if r == rank and ty == 0:
-                    out, tag = T.F0[:, rank * 256 + s * 128:rank * 256 + s * 128 + 128], "F0o%d" % s
-                elif r == rank:
-                    o = rank * 1024 + 256 + s * 128
-                    out, tag = T.F[:, o:o + 128], "Fso%d" % s
-                (cp if s == 0 else act)(out, src, ["Ya%d" % ty, "Yb%d" % ty], [tag])
-        wait("g", deps("g", ["SB%d_%d_%d" % (r, ty, s) for r in others for s in range(2)], []))
-        d = T.F0[:, rank * 256:rank * 256 + 256] if ty == 0 else T.F[:, rank * 1024 + 256:rank * 1024 + 512]
-        spread(lambda r: T.SB[:, r * 512 + ty * 256:r * 512 + ty * 256 + 256], d, "fs" if ty else "ft", slots)
-        lastw["Fsr" if ty else "F0r"] = [("fs" if ty else "ft", 7)]
+                tags.append("SB%d_%d_%d" % (r, ty, s))
+                a = (buf[:, o + s * 128:o + s * 128 + 128], T.Y[:, y0 + 2 * r + s:y0 + 2048:16], ["Ya%d" % ty, "Yb%d" % ty], [tags[-1]])
+                if (2 * n + s) % 3 == 2:
+                    act(*a, t=106)
+                else:
+                    cp(*a)
+            if ty == 0:
+                tags.append("SBh%d" % r)
+                cp(buf[:, o + 256:o + MSG], T.HT[:], ["HT%d" % i for i in range(7)], [tags[-1]])
+        own = 3 - ty
+        sem = ("ft", "fs")[ty]
+        sent = rem(lambda: spread(lambda r: sb[:, r * wid:(r + 1) * wid], T.F[:, f0 + rank * wid:f0 + (rank + 1) * wid], sem), tags[:-own])
+        lastw[sem] = (sem, 28, sent, 7000.0)
+        return sent, [sem] + tags[-own:]
 
-    feats(0)
-    feats(1)
-    f0 = ["F0r", "F0o0", "F0o1", "F0e"]
-    if last:
-        direct(targets(rank)[0], fe)
-        to_relay()
-    for d in targets(rank)[1:]:
-        direct(d, fe)
-    if not last:
-        hand_on(rank)
-    else:
-        n = [i for i in range(ncl) if rank in chips[i]][0]
-        for d in range(1, ncl):
-            for q in chips[(n + d) % ncl]:
-                hand_on(q)
+    fill(T.F[:, 0:FT], -256.0, ["Fe"])
+    ftp = feats(0)[1] + ["Fe"]
+    sent, fsd = feats(1)
+    for n in range(NR - 1):
+        lastw["TZ%d" % ((rank + 1 + n) % NR)] = ("tz%d" % ((rank + 1 + n) % NR), ntz[(rank + 1 + n) % NR], sent, 1000.0 + 12000.0 * n)
+    for d in targets(rank)[0 if last else 1:]:
+        rem(lambda d=d: send(d, z0, z0 + H2, "tz%d" % rank, fe[:8]), ["TZa"])
+    for q in (far if last else [rank]):
+        hand_on(q)
 
-    ts(T.IC15[:], T.IC[:], 15, AND, ["IC"], ["IC15"])
-    ts(T.ICG[:], ic, 112, AND, ["IC"], ["ICG"])
-    ts(T.C48[:], T.IC[:, 0:64], 48, AND, ["IC"], ["C48"])
-    ts(T.EL[:], T.C48[:], C["K"], OP.add, ["C48", "cK"], ["EL"])
-    ts(T.MK[:], T.IC15[:, 0:64], C["K"], OP.not_equal, ["IC15", "cK"], ["MK"], -4194304.0, OP.mult)
-    ts(T.IB[:], ic, C["P"], OP.is_equal, ["IC", "cP"], ["IB"])
-    ts(T.IBN[:], ic, C["P"], OP.is_equal, ["IC", "cP"], ["IBN"], -1.0, OP.mult)
-    ts(T.DL[:], T.IC15[:, 0:128], C["K"], OP.is_equal, ["IC15", "cK"], ["DL"])
-    ts(T.BOB[:], T.ICG[:], C["PG"], OP.is_equal, ["ICG", "cPG"], ["BOB"])
-    ts(T.BOH[:], T.ICG[:], C["PG"], OP.is_equal, ["ICG", "cPG"], ["BOH"])
-    ts(T.BOK[:], T.ICG[:], C["PG"], OP.is_equal, ["ICG", "cPG"], ["BOK"], 1024.0, OP.mult)
+    col("PG", "G", 16.0, OP.mult)
+    col("PGF", "cPG", 15.0, OP.add)
+    col("J128", "K", 128.0, OP.mult, float(FS), OP.add)
+    col("S128", "S", 128.0, OP.mult, float(FT), OP.add)
+    col("JT", "Q", MSG / 2.0, OP.mult, C["S128"], OP.add, ["cS128"])
+    col("NK", "K", -2.0, OP.mult, -2050.0, OP.add)
+    for b, (x, y) in enumerate(((0.0, 1.0), (255.0, 0.0))):
+        rm = (T.RM, T.R255)[b]
+        fill(rm[:], y, ["RM%d" % b], 212)
+        fill(rm[:, 0::16], x, ["RM%d" % b])
+    fill(T.US[:, 256:384], 0.0, ["RU"], 106)
+    fill(T.US[:, 256:384:16], -1e9, ["RU"])
+    fill(T.RB[:], 0.0, ["RB"])
+    fill(T.RB[:, 0::16], 1e9, ["RB"])
+    fill(T.NEG[:], -2048.0, ["NEG"])
+    fill(T.X[:, 4096:4224], -1024.0, ["Xe"])
+    for b, x, tag in ((T.NMW, 0.0, "NMe"), (T.SLW, 0.0, "SLe"), (T.FLW, 0.0, "FLe"), (T.KRS, -1.0, "KRe")):
+        fill(b[:, 128:144], x, [tag])
+    fill(T.D0[:, 0::4], 0.0, ["D00"], 106)
+    fill(T.DS[:, 3::4], 0.0, ["DS3"], 106)
+    fill(T.DN[:, 3::4], 0.0, ["DN3"], 106)
+    for h in range(2):
+        fill(T.E1[:, h * 64 + 48:h * 64 + 64], 0.0, ["E1z%d" % h])
+    ts(T.IC15[:], T.IC[:], 15, AND, ["IC"], ["IC15"], t=212)
+    ts(T.ICG[:], ic, 112, AND, ["IC"], ["ICG"], t=106)
+    ts(T.EL[:], T.ICG[:, 0:64], C["K"], OP.add, ["ICG", "cK"], ["EL"])
+    ts(T.MK[:], T.IC15[:, 0:128], C["K"], OP.not_equal, ["IC15", "cK"], ["MK"], -4194304.0, OP.mult, t=106)
+    ts(T.IB[:], ic, C["P"], OP.is_equal, ["IC", "cP"], ["IB"], t=106)
+    ts(T.IBN[:], ic, C["P"], OP.is_equal, ["IC", "cP"], ["IBN"], -1.0, OP.mult, t=106)
+    ts(T.IF[:], ic, C["P"], OP.is_equal, ["IC", "cP"], ["IF"], t=106)
+    ts(T.DL[:], T.IC15[:, 0:128], C["K"], OP.is_equal, ["IC15", "cK"], ["DL"], t=106)
+    ts(T.BOB[:], T.ICG[:], C["PG"], OP.is_equal, ["ICG", "cPG"], ["BOB"], t=106)
+    ts(T.BON[:], T.ICG[:], C["PG"], OP.is_equal, ["ICG", "cPG"], ["BON"], -1.0, OP.mult, t=106)
+    ts(T.BOH[:], T.ICG[:], C["PG"], OP.is_equal, ["ICG", "cPG"], ["BOH"], t=106)
     cp(T.REP[:], T.IC[:, 0:8], ["IC"], ["REP"])
-    cp(T.REP4[:], T.IC[:, 4:8], ["IC"], ["REP4"])
-    ts(T.WD[:], T.IC[:, 0:144], C["PGF"], OP.is_equal, ["IC", "cPGF"], ["WD"], 4096.0, OP.mult)
-    ts(T.WS[:], T.IC[:, 0:144], C["PGF"], OP.is_equal, ["IC", "cPGF"], ["WS"], 1024.0, OP.mult)
-    ts(T.PC1[:], T.IC15[:, 0:64], 16.0, OP.mult, ["IC15", "cK"], ["PC1"], C["K"], OP.add)
-    for i in range(4):
-        ts(T.PC2[:, i * 64:i * 64 + 64], T.C48[:], 16.0, OP.mult, ["C48"], ["PC2%d" % i], 1024.0 * i, OP.add)
-    hwn = ["HWN", "HWo"]
-    for i, x in enumerate((T.W1F, T.W2F, T.KCF)):
-        cp(x[:], T.HWN[:, i::8], hwn, ["hw%d" % i])
-    ts(T.THK[:], T.HWN[:, 3::8], 2048.0, OP.add, hwn, ["THK"], 4096.0, OP.mult)
+    ts(T.WD[:], T.IC[:, 0:144], C["PGF"], OP.is_equal, ["IC", "cPGF"], ["WD"], 512.0, OP.mult, t=120)
+    ts(T.WS[:], T.IC[:, 0:144], C["PGF"], OP.is_equal, ["IC", "cPGF"], ["WS"], t=120)
+    cp(T.PC[:], T.IC[:], ["IC"], ["PC"], 212)
+    cp(T.TI[:], ic, ["IC"], ["TI"], 106)
+    cp(T.TI2[:, 0:128], ic, ["IC"], ["TI2a"], 106)
+    ts(T.TI2[:, 128:256], ic, -1.0, OP.mult, ["IC"], ["TI2b"], t=106)
+    ts(T.CSEL[:], T.IC[:, 0:8], C["G8"], OP.is_equal, ["IC", "cG8"], ["CSEL"])
+    ts(T.CT[:], T.IC[:, 0:8], 256.0, OP.add, ["IC"], ["CT"])
+    ts(T.HC[:, 256:272], T.IC[:, 0:16], -32.0, OP.mult, ["IC", "cNK"], ["HCe"], C["NK"], OP.add)
+    ts(T.NMX[:], T.IC[:, 0:8], 2.0, OP.mult, ["IC", "cK"], ["NMX"], C["K"], OP.not_equal)
+    ts(T.ISX[:], T.IC[:, 0:8], 2.0, OP.mult, ["IC", "cK"], ["ISX"], C["K"], OP.is_equal)
+    ts(T.IX2[:], T.ISX[:], 2048.0, OP.mult, ["ISX"], ["IX2"])
+    tt(T.KCF[:], T.F[:, FT + 258:FS:MSG], T.F[:, FT + 259:FS:MSG], OP.add, ftp, ["KCF"])
+    tt(T.SENT[:], T.F[:, FT + 260:FS:MSG], T.F[:, FT + 261:FS:MSG], OP.add, ftp, ["SENT"])
+    ts(T.THK[:], T.SENT[:], -1.0, OP.add, ["SENT"], ["THK"], 512.0, OP.mult)
+    ts(T.NMI[:], T.TPI[:], 1.0, OP.add, ["TPI"], ["NMI"], t=106)
+    ts(T.SDN[:], T.SDI[:], 1.0, OP.add, ["SDI"], ["SDN"], t=106)
+    ts(T.TPS[:], ic, C["JT"], OP.add, ["IC", "cJT"], ["TPS"], t=106)
+    ts(T.PR[:, 0:128], ic, C["J128"], OP.add, ["IC", "cJ128"], ["pr0"], t=106)
+    ts(T.PR[:, 128:256], T.SDI[:], 0.0, OP.is_ge, ["SDI"], ["pr1"], t=106)
+    tt(T.SDS[:], T.PR[:, 0:128], T.PR[:, 128:256], OP.mult, ["pr0", "pr1"], ["SDS"], 212)
+    ts(T.PR[:, 128:256], T.TPI[:], 0.0, OP.is_ge, ["TPI"], ["pr1"], t=106)
+    tt(T.PR[:, 0:128], T.TPS[:], T.PR[:, 128:256], OP.mult, ["TPS", "pr1"], ["pr0"], 212)
+    cp(T.LE[:], T.PR[:, 0:128], ["pr0"], ["LE0", "LE1"], 106)
+    cp(T.A16[:], ic, ["IC"], ["A16"], 106)
+    ts(T.KX[:], T.IH[:], 128.0, OP.mult, ["IH"], ["KX"])
+    for c in range(4):
+        tt(T.RR[:, c * 128:c * 128 + 128], T.KX[:], T.A16[:], OP.max, ["KX", "A16"], ["RR%d" % c], 212)
+    for b, sg in enumerate((T.SGP, T.SGN)):
+        ts(T.CBC[:, b * 8:b * 8 + 8], T.CSEL[:], 1024.0 - 2048.0 * b, OP.mult, ["CSEL"], ["CBC%d" % b])
+        for c in range(8):
+            ts(sg[:, c * 128:c * 128 + 128], T.A16[:], 0.0, OP.mult, ["A16", "CBC%d" % b], ["SG%d_%d" % (b, c)],
+               T.CBC[:, b * 8 + c:b * 8 + c + 1], OP.add)
 
     def hash_consts(q):
         o = slice(q * 128, q * 128 + 128)
-        ts(T.W1L[:, o], T.BOB[:], T.W1F[:, q:q + 1], OP.mult, ["BOB", "hw0"], ["W1L%d" % q], 0.5, OP.mult)
-        ts(T.W2L[:, o], T.BOB[:], T.W2F[:, q:q + 1], OP.mult, ["BOB", "hw1"], ["W2L%d" % q], 0.5, OP.mult)
-        ts(T.KX[:, o], T.DL[:], T.KCF[:, q:q + 1], OP.mult, ["DL", "hw2"], ["KX%d" % q])
-        op("t", lambda: mm(T.KA[:, 256:384], T.BOH[:], T.KX[:, o], True, True), ["BOH", "KX%d" % q], ["KA"])
-        act(T.KC[:, o], T.KA[:, 256:384], ["KA"], ["KC%d" % q])
-
-    for t in range(NR):
-        hash_consts((rank + 1 + t) % NR)
-    for q in range(NR):
-        fill(T.F[:, q * 1024 + 512:(q + 1) * 1024], -256.0, ["FW%d" % q])
-    for h in range(2):
-        fill(T.E1[:, h * 64 + 48:h * 64 + 64], 0.0, ["E1z"])
-    ts(T.CWT[:], ic, 512.0, OP.add, ["IC"], ["CWT"], 1.0 / 1024, OP.mult)
-    ts(T.CW[:], T.CWT[:], C["E0"], OP.mult, ["CWT", "cE0", "cE1"], ["CW"], C["E1"], OP.add)
-    ts(T.C128[:], ic, 128.0, OP.add, ["IC"], ["C128"])
-    ts(T.CTT[:], T.IC[:, 0:8], 16.0, OP.mult, ["IC", "cK"], ["CTT"], C["K"], OP.add)
-    ts(T.CT[:], T.CTT[:], 256.0, OP.add, ["CTT"], ["CT"], 1.0 / 256, OP.mult)
-    ts(T.SG[:], ic, C["S128"], OP.add, ["IC", "cS128"], ["SG"])
-    ts(T.NMX[:], T.IC[:, 0:8], 2.0, OP.mult, ["IC", "cK"], ["NMX"], C["K"], OP.not_equal)
-    fill(T.HC[:, 256:272], -2048.0, ["HCe"])
-    for src, add, out, tag in ((T.TPI, 0.0, T.S2, "S2"), (T.SDI, 256.0, T.SDV, "SDV")):
-        ts(pr[2], src[:], 1.0, OP.add, ["TPI", "SDI"], ["pr2"], 1024.0, OP.mult)
-        tt(pr[3], pr[2], T.SG[:], OP.add, ["pr2", "SG"], ["pr3"])
-        ts(out[:], pr[3], add, OP.add, ["pr3"], [tag], 767.0, OP.max)
-    cp(T.A16[:], ic, ["IC"], ["A16"])
-    ts(T.CBC[:], T.IC[:, 0:8], C["G8"], OP.is_equal, ["IC", "cG8"], ["CBC"], -1024.0, OP.mult)
-    for c in range(8):
-        o = slice(c * 128, c * 128 + 128)
-        ts(T.RCA[:, o], ic, T.CTT[:, c:c + 1], OP.is_ge, ["IC", "CTT"], ["RCA%d" % c], 128.0, OP.mult)
-        ts(T.RCB[:, o], ic, T.CTT[:, c:c + 1], OP.is_equal, ["IC", "CTT"], ["RCB%d" % c], 128.0, OP.mult)
-        ts(T.CB[:, o], T.A16[:], 0.0, OP.mult, ["A16", "CBC"], ["CB%d_%d" % (c // 4, c % 4)], T.CBC[:, c:c + 1], OP.add)
-    for q in range(NR):
-        dma("y", T.F[:, q * 1024:q * 1024 + 256], T.F0[:, q * 256:q * 256 + 256], f0, ["Ft%d" % q])
-    fall = ["Ft%d" % q for q in range(NR)] + ["FW%d" % q for q in range(NR)] + ["Fsr", "Fso0", "Fso1"]
-
-    def run(*gens):
-        now, ready, rk = 0, [0] * len(gens), [0] * len(gens)
-        live = list(range(len(gens)))
-        while live:
-            i = min(live, key=lambda j: (max(ready[j], now), rk[j], j))
-            try:
-                cost, lat, rk[i] = next(gens[i])
-            except StopIteration:
-                live.remove(i)
-                continue
-            now = max(now, ready[i]) + cost
-            ready[i] = now + lat
+        f = FT + q * MSG + 256
+        ts(T.W1L[:, o], T.BOH[:], T.F[:, f:f + 1], OP.mult, ["BOH"] + ftp, ["W1L%d" % q], 0.5, OP.mult)
+        ts(T.W2L[:, o], T.BOH[:], T.F[:, f + 1:f + 2], OP.mult, ["BOH"] + ftp, ["W2L%d" % q], 0.5, OP.mult)
+        ts(T.KX[:], T.DL[:], T.KCF[:, q:q + 1], OP.mult, ["DL", "KCF"], ["KX"], t=106)
+        pe([(T.KA[:, 256:384], T.BOH[:], T.KX[:], True, True)], ["BOH", "KX"], "KA", 128)
+        act(T.KC[:, o], T.KA[:, 256:384], ["KA"], ["KC%d" % q], t=106)
 
     bk = [T.BK0, T.BK1]
+    CH = ((0, 384), (384, 768))
 
     def u_mm(q, h, src, tag):
         o = slice(q * 128, q * 128 + 128)
+        w = ["W1L%d" % q, "W2L%d" % q]
+        pe([(bk[h][:, 0:128], T.IB[:], T.MK[:], True, False)] +
+           [(bk[h][:, u * 64:u * 64 + 64], wl[:, o], T.NEG[:], False, False) for u, wl in enumerate((T.W1L, T.W2L))],
+           ["IB", "MK", "NEG"] + w, "BK%d" % h, 256)
+        pe([(bk[h][:, u * 64:u * 64 + 64], wl[:, o], src, False, u == 1) for u, wl in enumerate((T.W1L, T.W2L))], w + [tag], "BK%d" % h, 128)
 
-        def f():
-            out = []
-            for u, wl in enumerate((T.W1L, T.W2L)):
-                mm(bk[h][:, u * 64:u * 64 + 64], T.IB[:], T.MK[:], True, False)
-                out.append(mm(bk[h][:, u * 64:u * 64 + 64], wl[:, o], src, False, True))
-            return out
-        op("t", f, ["IB", "MK", "W1L%d" % q, "W2L%d" % q, tag], ["BK%d" % h])
-
-    def e_load(win, R):
-        for h in range(2):
-            o, l = h * 1024, h * 64
-            act(T.VF[:, o:o + 512], win.indirect(T.LE[:, l:l + 32]), R + ["LE"], ["VFa%d" % h])
-            cp(T.VF[:, o + 512:o + 1024], win.indirect(T.LE[:, l + 32:l + 64]), R + ["LE"], ["VFb%d" % h])
-            act(T.VA[:, o:o + 1024], T.VF[:, o:o + 1024], ["VFa%d" % h, "VFb%d" % h], ["VA%d" % h], AF.Abs)
-
-    def e_gen(h, q):
-        o = slice(h * 1024, h * 1024 + 1024)
+    def middle(h, q, win, R):
+        x = "%d" % h
+        for b in range(2):
+            o = slice(h * 1024 + b * 512, h * 1024 + b * 512 + 512)
+            y = x + "ab"[b]
+            src = win.indirect(T.LE[:, h * 64 + b * 32:h * 64 + b * 32 + 32])
+            if b == 0:
+                cp(T.VF[:, o], src, R + ["LE" + x], ["VF" + y], gns(512))
+            else:
+                act(T.VF[:, o], src, R + ["LE" + x], ["VF" + y], t=gns(512))
+            act(T.VA[:, o], T.VF[:, o], ["VF" + y], ["VA" + y], AF.Abs, t=425)
+            scan(T.MX[:, o], T.RM[:], T.VF[:, o], OP.mult, OP.max, ["RM0", "VF" + y], ["MX" + y], 212)
+            scan(T.MN[:, o], T.R255[:], T.VA[:, o], OP.max, OP.min, ["RM1", "VA" + y], ["MN" + y], 212)
         hh = slice(h * 64, h * 64 + 64)
         end = slice(h * 1024 + 15, h * 1024 + 1024, 16)
-        scan(T.MX[:, o], T.RM[:], T.VF[:, o], OP.mult, OP.max, ["RM0", "VFa%d" % h, "VFb%d" % h], ["MX%d" % h])
-        yield 500, 400, 0
-        ts(T.HIM[:, hh], T.MX[:, end], -0.5, OP.add, ["MX%d" % h], ["HIM%d" % h])
-        scan(T.MN[:, o], T.R255[:], T.VA[:, o], OP.max, OP.min, ["RM1", "VA%d" % h], ["MN%d" % h])
-        yield 500, 180, 0
-        tt(T.SUM[:, hh], T.HIM[:, hh], T.MN[:, end], OP.add, ["HIM%d" % h, "MN%d" % h], ["SUM%d" % h])
-        yield 120, 180, 0
-        e2 = T["E2%d" % h]
-        tg = "E2%d" % h
-        ts(e2[:], T.SUM[:, hh], MAGIC, OP.add, ["SUM%d" % h], [tg], MAGIC, OP.subtract)
-        u_mm(q, h, e2[:], tg)
-        act(T.EREP[:, o], e2[:].indirect(T.EL[:]), [tg, "EL"], ["EREP%d" % h], scale=0.5)
+        ts(T.HIM[:, hh], T.MX[:, end], 2047.5, OP.add, ["MX" + x + "a", "MX" + x + "b"], ["HIM" + x])
+        tt(T.E2H[:, hh], T.HIM[:, hh], T.MN[:, end], OP.add, ["HIM" + x, "MN" + x + "a", "MN" + x + "b"], ["E2H" + x], 106)
+        u_mm(q, h, T.E2H[:, hh], "E2H" + x)
+        e2 = T.E2[:, hh]
+        ts(e2, T.E2H[:, hh], -2048.0, OP.add, ["E2H" + x], ["E2" + x])
+        for n, (a, b) in enumerate(CH + ((768, 1024),)):
+            act(T.EREP[:, h * 1024 + a:h * 1024 + b], e2.indirect(T.EL[:, a // 16:b // 16]), ["E2" + x, "EL"], ["EREP%s_%d" % (x, n)],
+                scale=0.5, t=gns(b - a))
         b = h * 64
-        act(T.E2M[:, b:b + 48], e2[:, 0:48], [tg], ["E2Ma%d" % h], AF.Identity, bias=-0.5)
-        act(T.E2M[:, b + 48:b + 64], e2[:, 48:64], [tg], ["E2Mb%d" % h], AF.Identity, bias=-0.5, scale=0.5)
-        act(T.E1[:, b:b + 48], e2[:, 0:48], [tg, "E1z"], ["E1%d" % h], scale=0.5)
-        yield 60, 700, 0
+        act(T.E2M[:, b:b + 48], T.E2[:, b:b + 48], ["E2" + x], ["E2Ma" + x], AF.Identity, bias=2047.5)
+        act(T.E2M[:, b + 48:b + 64], T.E2[:, b + 48:b + 64], ["E2" + x], ["E2Mb" + x], AF.Identity, bias=2047.5, scale=0.5)
+        act(T.E1[:, b:b + 48], T.E2[:, b:b + 48], ["E2" + x], ["E1" + x], scale=0.5)
 
-    def hash_gen(p, h, q):
+    def hashes(p, h, q):
         x = "%d" % h
         i = p * 2 + h
         us, kk, hi = T.US[:, h * 128:h * 128 + 128], T.KK[:, h * 64:h * 64 + 64], T.HI[:, h * 64:h * 64 + 64]
         ui, ua, pp, vi = T.UI[:, h * 8:h * 8 + 8], T.UA[:, h * 8:h * 8 + 8], T.PP[:, h * 4:h * 4 + 4], T.VI[:, h * 8:h * 8 + 4]
-        scan(us, T.RU[:], bk[h][:, 0:128], OP.add, OP.max, ["RU", "BK" + x], ["US" + x])
-        yield 120, 180, 0
+        scan(us, T.US[:, 256:384], bk[h][:, 0:128], OP.add, OP.max, ["RU", "BK" + x], ["US" + x], 106)
         cp(ui, T.US[:, h * 128 + 15:h * 128 + 128:16], ["US" + x], ["UI" + x])
-        yield 60, 180, 0
         ts(ua, ui, 4095, AND, ["UI" + x], ["UA" + x])
-        yield 60, 180, 0
         tt(pp, T.UA[:, h * 8:h * 8 + 4], T.UA[:, h * 8 + 4:h * 8 + 8], OP.mult, ["UA" + x], ["PP" + x])
-        tt(kk, ua.indirect(T.REP4[:]), T.KC[:, q * 128:q * 128 + 64], OP.mult, ["UA" + x, "REP4", "KC%d" % q], ["KK" + x])
-        yield 230, 120, 0
+        tt(kk, ua.indirect(T.REP[:, 4:8]), T.KC[:, q * 128:q * 128 + 64], OP.mult, ["UA" + x, "REP", "KC%d" % q], ["KK" + x], gns(64))
         ts(vi, pp, 5, SHR, ["PP" + x], ["VI" + x])
-        yield 60, 180, 0
-        tt(hi, vi.indirect(T.REP[:, 0:4]), kk, OP.add, ["VI" + x, "KK" + x, "REP"], ["HI" + x])
-        yield 150, 180, 0
+        tt(hi, vi.indirect(T.REP[:, 0:4]), kk, OP.add, ["VI" + x, "KK" + x, "REP"], ["HI" + x], gns(64))
         hm = T.HM[:, i * 64:i * 64 + 64]
         ts(hm, hi, 4095, AND, ["HI" + x], ["HM%d" % i])
-        yield 60, 180, 0
         cp(T.LH[:, i * 64:i * 64 + 64], hm, ["HM%d" % i], ["LH%d" % i])
-        yield 60, 180, 1
+        ts(T.HC[:, i * 64:i * 64 + 64], hm, -2047.0, OP.add, ["HM%d" % i], ["HC%d" % i])
 
-    issued = []
-
-    def cand(p, h, q):
+    def search(p, h, q):
         i = p * 2 + h
+        x = "%d" % h
         x0, l0, e0 = i * 1024, i * 64, h * 1024
         tz = T.TZ[:, q * W:q * W + W]
-        R = ["TZa%d" % q, "TZb%d" % q, "LH%d" % i]
-        zb, xp = T["Z%d" % h], T["VP%d" % h][:, 0:256]
-        act(T.X[:, x0 + 768:x0 + 1024], tz.indirect(T.LH[:, l0 + 48:l0 + 64]), R, ["X%d_r" % i])
+        R = (["TZa", "TZb"] if q == rank else ["TZ%d" % q]) + ["LH%d" % i]
+        zb, xp, key = T["Z" + x], T["VP" + x][:, 0:256], bk[h][:, 128:192]
+        pe([(key, T.IB[:], T.PC[:, l0:l0 + 64], True, False)], ["IB", "PC"], "BK" + x, 64)
+        pe([(xp, T.IBN[:], T.EREP[:, e0 + 768:e0 + 1024], True, False)], ["IBN", "EREP%s_2" % x], "VP" + x, 256)
+        act(T.X[:, x0 + 768:x0 + 1024], tz.indirect(T.LH[:, l0 + 48:l0 + 64]), R, ["X%d_2" % i], t=gns(256))
+        pe([(xp, T.IB[:], T.X[:, x0 + 768:x0 + 1024], False, True)], ["IB", "X%d_2" % i], "VP" + x, 256)
+        act(zb[:, 768:1024], xp, ["VP" + x], ["Z%s_2" % x], AF.Abs, t=212)
+        for n, (a, b) in enumerate(CH):
+            tt(T.X[:, x0 + a:x0 + b], tz.indirect(T.LH[:, l0 + a // 16:l0 + b // 16]), T.EREP[:, e0 + a:e0 + b], OP.subtract,
+               R + ["EREP%s_%d" % (x, n)], ["X%d_%d" % (i, n)], gns(b - a))
+            act(zb[:, a:b], T.X[:, x0 + a:x0 + b], ["X%d_%d" % (i, n)], ["Z%s_%d" % (x, n)], AF.Abs, t=ns(b - a))
+        pe([(key, T.WD[:, 15 - k:143 - k], zb[:, k::16], False, k == 15) for k in range(16)],
+           ["WD"] + ["Z%s_%d" % (x, n) for n in range(3)], "BK" + x, 1024)
+        scan(T.KS[:, l0:l0 + 64], T.RB[:], key, OP.max, OP.min, ["RB", "BK" + x], ["KS%d" % i])
 
-        def f():
-            mm(xp, T.IB[:], T.X[:, x0 + 768:x0 + 1024], True, False)
-            return mm(xp, T.IBN[:], T.EREP[:, e0 + 768:e0 + 1024], False, True)
-        op("t", f, ["IB", "IBN", "X%d_r" % i, "EREP%d" % h], ["VP%d" % h])
-        key = bk[h][:, 128:192]
-
-        def keys():
-            mm(key, T.IB[:], T.PC1[:], True, False)
-            return mm(key, T.IB[:], T.PC2[:, i * 64:i * 64 + 64], False, False)
-        op("t", keys, ["IB", "PC1", "PC2%d" % i], ["BK%d" % h])
-        if h == 1:
-            first_dist(p)
-        tt(T.X[:, x0:x0 + 768], tz.indirect(T.LH[:, l0:l0 + 48]), T.EREP[:, e0:e0 + 768], OP.subtract, R + ["EREP%d" % h], ["X%d_0" % i])
-        act(zb[:, 0:768], T.X[:, x0:x0 + 768], ["X%d_0" % i], ["Z%d_0" % h], AF.Abs)
-        act(zb[:, 768:1024], xp, ["VP%d" % h], ["Z%d_r" % h], AF.Abs)
-        if h == 1:
-            dist(p, 1)
-        yield 400, 2300, 0
-
-    def first_dist(p):
-        if p not in issued:
-            issued.append(p)
-            dist(p, 0)
-
-    def dist(p, h):
-        zb = T["Z%d" % h]
-
-        def f():
-            for k in range(16):
-                r_ = mm(bk[h][:, 128:192], T.WD[:, 15 - k:143 - k], zb[:, k::16], False, k == 15)
-            return r_
-        op("t", f, ["WD", "Z%d_0" % h, "Z%d_r" % h], ["BK%d" % h])
-
-    def names(p, h):
-        i = p * 2 + h
-        ts(T.HC[:, i * 64:i * 64 + 64], T.HM[:, i * 64:i * 64 + 64], -2047.0, OP.add, ["HM%d" % i], ["HC%d" % i])
-
-    def best(p, h):
-        i = p * 2 + h
-        first_dist(p)
-        scan(T.KS[:, i * 64:i * 64 + 64], T.RB[:], bk[h][:, 128:192], OP.max, OP.min, ["RB", "BK%d" % h], ["KS%d" % i])
-
-    def arg_gen(h, q):
+    def restart(h, q):
         x = "%d" % h
         hh = slice(h * 64, h * 64 + 64)
-        best(0, h)
-        yield 60, 180, 0
-        ki = T.KI[:, h * 8:h * 8 + 4]
-        ka = T.KI[:, h * 8 + 4:h * 8 + 8]
-        cp(ki, T.KS[:, h * 64 + 15:h * 64 + 64:16], ["KS" + x], ["KI" + x])
-        yield 60, 180, 0
-        ts(ka, ki, 1023, AND, ["KI" + x], ["KA_" + x])
-        yield 60, 180, 0
-        lp = T.LP[:, h * 8:h * 8 + 4]
-        cp(lp, ka, ["KA_" + x], ["LP" + x])
-        yield 60, 180, 0
-        tt(T.CS[:, hh], T.X[:, h * 1024:h * 1024 + 1024].indirect(lp), T.E2M[:, hh], OP.add,
-           ["X%s_0" % x, "X%s_r" % x, "LP" + x, "E2Ma" + x, "E2Mb" + x], ["CS" + x])
-        yield 160, 180, 0
-        ts(T.C2[:, hh], T.CS[:, hh], MAGIC, OP.add, ["CS" + x], ["C2" + x], MAGIC, OP.subtract)
+        ki, ka, lp = T.KI[:, h * 8:h * 8 + 4], T.KI[:, h * 8 + 4:h * 8 + 8], T.LP[:, h * 8:h * 8 + 4]
+        ends = T.KS[:, h * 64 + 15:h * 64 + 64:16]
+        cp(ki, ends, ["KS" + x], ["KI" + x])
+        ts(ka, ki, 63, AND, ["KI" + x], ["KA_" + x])
+        ts(lp, ka, 16.0, OP.mult, ["KA_" + x, "cK"], ["LP" + x], C["K"], OP.add)
+        tt(T.C2[:, hh], T.X[:, h * 1024:h * 1024 + 1024].indirect(lp), T.E2M[:, hh], OP.add,
+           ["X%s_%d" % (x, n) for n in range(3)] + ["LP" + x, "E2Ma" + x, "E2Mb" + x], ["C2" + x], gns(64))
         u_mm(q, h, T.C2[:, hh], "C2" + x)
-        yield 60, 700, 0
+        tt(T.KF1[:, h * 4:h * 4 + 4], ends, T.SENT[:, h * 4:h * 4 + 4], OP.min, ["KS" + x, "SENT"], ["KF1" + x])
 
-    def chain(h, q):
-        yield 0, 1100 * h, 0
-        for x in (e_gen(h, q), hash_gen(0, h, q), cand(0, h, q), arg_gen(h, q), hash_gen(1, h, q), cand(1, h, q)):
-            for y in x:
-                yield y
-        names(0, h)
-        yield 60, 0, 0
-        names(1, h)
-        yield 60, 2100, 0
-        best(1, h)
-        yield 60, 0, 0
+    def winner(h, q):
+        x = "%d" % h
+        c = slice(h * 4, h * 4 + 4)
+        hh = slice(h * 64, h * 64 + 64)
+        pl = T.KF[:, 8 + h * 4:12 + h * 4]
+        tt(T.KF[:, c], T.KS[:, 128 + h * 64 + 15:192 + h * 64:16], T.KF1[:, c], OP.min, ["KS%d" % (2 + h), "KF1" + x], ["KF" + x])
+        ts(pl, T.KF[:, c], 511, AND, ["KF" + x], ["PL" + x])
+        cp(T.LN[:, c], pl, ["PL" + x], ["LN" + x])
+        tt(T.HGD[:, hh], T.HC[:].indirect(T.LN[:, c]), T.DL[:, 0:64], OP.mult, ["HC0", "HC1", "HC2", "HC3", "HCe", "LN" + x, "DL"],
+           ["HGD" + x], gns(64))
+        ts(T.LF[:, c], pl, 16.0, OP.mult, ["PL" + x, "cK"], ["LF" + x], C["K"], OP.add)
 
-    def r_mm(b):
-        pk = T["PK%d" % b]
-        mm(pk[:], T.IH[:], T.RCA[:, b * 512:b * 512 + 512], True, False)
-        for c in range(4):
-            mm(pk[:, c * 128:c * 128 + 128], T.IH[:], T.A16[:], False, False)
-        return mm(pk[:], T.IH[:], T.RCB[:, b * 512:b * 512 + 512], False, False)
-
-    def ahead(q):
-        for b in range(2):
-            op("t", lambda: r_mm(b), ["IH", "A16"] + ["RC%s%d" % (x, c) for x in "AB" for c in range(8)], ["PK%d" % b])
-        ts(T.S0M[:], T.S2[:], T.NMX[:, q:q + 1], OP.mult, ["S2", "NMX"], ["S0M"], 767.0, OP.max)
-        yield 150, 0, 0
-
+    hash_consts((rank + 1) % NR)
+    SNT = ["SN%d" % i for i in range(4)]
     for t in range(NR):
         q = (rank + 1 + t) % NR
-        if t == 0:
-            e_load(T.F0[:, 0:2064], f0)
-        else:
-            e_load(T.F[:], fall)
-        issued.clear()
-        run(chain(0, q), chain(1, q), ahead(q))
-        kf, nf, ps, pm, kl, pia = (T.KFI[:, i * 8:i * 8 + 8] for i in range(6))
-        tt(kf, T.KS[:, 15:128:16], T.KS[:, 143:256:16], OP.min, ["KS0", "KS1", "KS2", "KS3"], ["kf"])
-        ts(nf, kf, T.THK[:, q:q + 1], OP.is_ge, ["kf", "THK"], ["nf"], 256.0, OP.mult)
-        ts(ps, kf, 4095, AND, ["kf"], ["ps"], 4, SHR)
-        tt(pm, nf, ps, OP.max, ["nf", "ps"], ["pm"])
-        cp(T.LN[:], pm, ["pm"], ["LN"])
-        tt(T.HGD[:], T.HC[:].indirect(T.LN[:]), T.DL[:], OP.mult, ["HC0", "HC1", "HC2", "HC3", "HCe", "LN", "DL"], ["HGD"])
-        op("t", lambda: mm(T.HS[:, 0:128], T.HGD[:], T.IH[:], True, True), ["HGD", "IH"], ["HS"])
-
-        def sv():
-            wl = T.WS[:, 15 - 2 * q:143 - 2 * q]
-            mm(T.HS[:, 128:256], wl, T.CW[:], True, False)
-            return mm(T.HS[:, 128:256], wl, T.HGD[:], False, True)
-        op("t", sv, ["WS", "CW", "HGD"], ["HS"])
+        more = t < NR - 1
+        qc = slice(q, q + 1)
+        if more:
+            hash_consts((q + 1) % NR)
+        nmn = T.NMI[:] if t == 0 else T.SN[:, 3::4]
+        win, R = (T.F[:, 0:FS], ftp) if t == 0 else (T.F[:, 0:FW + t * 128], ftp + fsd + ["FW"])
+        for h in range(2):
+            middle(h, q, win, R)
+        ts(T.SENT[:], T.CT[:], T.THK[:, qc], OP.add, ["CT", "THK"], ["SENT"])
+        ts(T.NM0[:], nmn, T.NMX[:, qc], OP.mult, ["NMI", "NMX", "IX2"] + SNT, ["NM0"], T.IX2[:, qc], OP.add, t=106)
+        pe([(T.HS[:, 0:128], T.IF[:], T.NM0[:], True, False)], ["IF", "NM0"], "HS", 512)
         for b in range(2):
-            pk = T["PK%d" % b]
-            op("t", lambda: [mm(pk[:, c * 128:c * 128 + 128], T.BOK[:], T.HGD[:], False, False) for c in range(4)][-1],
-               ["BOK", "HGD"], ["PK%d" % b])
-            if b == 0:
-                cp(T.HTS[:], T.HS[:, 0:128], ["HS"], ["HTS"])
-            op("t", lambda: mm(pk[:], T.HTS[:], T.CB[:, b * 512:b * 512 + 512], False, True),
-               ["HTS"] + ["CB%d_%d" % (b, c) for c in range(4)], ["PK%d" % b])
-        tt(T.S1[:], T.HS[:, 128:256], T.S0M[:], OP.max, ["HS", "S0M"], ["S1"])
-        tt(T.NFT[:], nf, T.CT[:], OP.mult, ["nf", "CT"], ["NFT"])
-        ts(kl, kf, 4095, AND, ["kf"], ["kl"])
-        ts(T.NP1[:], T.S1[:], 10, SHR, ["S1"], ["NP1"])
-        cp(T.LF[:], kl, ["kl"], ["LF"])
-        ts(T.NP2[:], T.S1[:], 10, SHR, ["S1"], ["NP2"])
+            pe([(T["PK%d" % b][:], T.IH[:], T.RR[:], True, False)], ["IH"] + ["RR%d" % c for c in range(4)], "PK%d" % b, 512)
+        if more:
+            ts(T.FLN[:], nmn, 0.5, OP.is_ge, ["NMI", "NMX"] + SNT, ["FLN"], T.NMX[:, qc], OP.mult, t=106)
+            ts(T.WSL[:], ic, float(FW + t * 128), OP.add, ["IC", "ISX"], ["WSL"], T.ISX[:, qc], OP.mult, t=106)
+            for h in range(2):
+                hh, x = slice(h * 64, h * 64 + 64), "%d" % h
+                sl = T.TPS[:, hh] if t == 0 else T.SS[:, h * 256 + 3:h * 256 + 256:4]
+                tt(T.SL0[:, hh], sl, T.FLN[:, hh], OP.mult, ["TPS", "SS%d" % (2 * h), "SS%d" % (2 * h + 1), "FLN"], ["SL0" + x], 106)
+                tt(T.SLW[:, hh], T.SL0[:, hh], T.WSL[:, hh], OP.add, ["SL0" + x, "WSL"], ["SLW" + x], 106)
+                tt(T.DS[:, h * 256 + 1:h * 256 + 256:4], T.SDS[:, hh], T.SLW[:, hh], OP.subtract, ["SDS", "SLW" + x], ["DS1" + x], 106)
+            act(T.DS[:, 2::4], T.SLW[:, 0:128], ["SLW0", "SLW1"], ["DS2"], t=106)
+        for h in range(2):
+            hashes(0, h, q)
+            search(0, h, q)
+            restart(h, q)
+        for h in range(2):
+            hashes(1, h, q)
+            search(1, h, q)
+        wl = T.WS[:, 15 - 2 * q:143 - 2 * q]
+        for h in range(2):
+            winner(h, q)
+            hh = slice(h * 64, h * 64 + 64)
+            for b in range(2):
+                pk = T["PK%d" % b]
+                calls = [(pk[:, c * 128 + h * 64:c * 128 + h * 64 + 64], T.SGP[:, (b * 4 + c) * 128:(b * 4 + c + 1) * 128], T.HGD[:, hh], False, False)
+                         for c in range(4)]
+                if h == 1:
+                    calls.append((pk[:], T.HGD[:], T.SGN[:, b * 512:b * 512 + 512], False, True))
+                pe(calls, ["HGD%d" % i for i in range(h + 1)] + ["SG%d_%d" % (i, b * 4 + c) for i in range(2) for c in range(4)], "PK%d" % b, 256 + 512 * h)
+            pe([(T.HS[:, hh], wl, T.HGD[:, hh], False, h == 1)], ["WS", "HGD%d" % h], "HS", 64)
+        pe([(T.VP1[:, 0:256], T.IB[:], T.TI2[:], True, False)], ["IB", "TI2a", "TI2b"], "VP1", 256)
+        act(T.NMW[:, 0:128], T.HS[:, 0:128], ["HS"], ["NMW"], AF.Relu, t=106)
+        act(T.FLW[:, 0:128], T.NMW[:, 0:128], ["NMW"], ["FLW"], AF.Sign, t=106)
+        act(T.FLW[:, 144:272], T.NMW[:, 0:128], ["NMW"], ["FL2"], AF.Sign, t=106)
+        act(T.DN[:, 2::4], T.NMW[:, 0:128], ["NMW"], ["DN2"], t=106)
+        for h in range(2):
+            tt(T.DN[:, h * 256 + 1:h * 256 + 256:4], T.SDN[:, h * 64:h * 64 + 64], T.NMW[:, h * 64:h * 64 + 64], OP.subtract,
+               ["SDN", "NMW"], ["DN1%d" % h], 106)
+        if more:
+            tt(T.F[:, FW + t * 128:FW + t * 128 + 128], T.X[:].indirect(T.LF[:]), T.E1[:], OP.add,
+               ["X%d_%d" % (i, n) for i in range(4) for n in range(3)] + ["Xe", "LF0", "LF1", "E10", "E11", "E1z0", "E1z1"], ["FW"], gns(128))
         for c in range(8):
             pk = T["PK%d" % (c // 4)]
-            op("v", lambda: V.tensor_reduce(T.KB[:, c:c + 1], pk[:, (c % 4) * 128:(c % 4) * 128 + 128], AxisListType.X, OP.min,
-                                            apply_absolute_value=True), ["PK%d" % (c // 4)], ["KB%d" % c])
-            if c == 3 and t < NR - 1:
-                tt(T.F[:, q * 1024 + 512:q * 1024 + 640], T.X[:].indirect(T.LF[:]), T.E1[:], OP.add,
-                   ["X%d_%s" % (i, j) for i in range(4) for j in "0r"] + ["LF", "E10", "E11", "E1z"], ["FW%d" % q])
-        tt(T.KBI[:], T.KB[:], T.NFT[:], OP.max, ["KB%d" % c for c in range(8)] + ["NFT"], ["KBI"])
-        tt(T.KBX[:], T.KBI[:].indirect(T.REP[:]), T.DL[:], OP.mult, ["KBI", "REP", "DL"], ["KBX"])
-        ts(pia, T.KBI[:], 127, AND, ["KBI"], ["pia"])
-        op("t", lambda: mm(T.KA[:, 0:128], T.BOH[:], T.KBX[:], True, True), ["BOH", "KBX"], ["KA"])
-        act(T.KRS[:], T.KA[:, 0:128], ["KA"], ["KRS"])
-        cp(T.LPI[:], pia, ["pia"], ["LPI"])
-        act(T.KRP[:], T.KRS[:].indirect(T.LPI[:]), ["KRS", "LPI"], ["KRP"])
-        sp, nq, mnn, cl, bm, dsb, alt, dd = pr
-        am, ef, sa, m_, ds, kep, k0, nan = (T["VP%d" % (i // 4)][:, (i % 4) * 128:(i % 4) * 128 + 128] for i in range(8))
-        tt(nq, T.NP1[:].indirect(T.LPI[:]), T.NP2[:], OP.not_equal, ["NP1", "NP2", "LPI"], ["nq"])
-        tt(mnn, T.NP1[:].indirect(T.LPI[:]), T.NP2[:], OP.min, ["NP1", "NP2", "LPI"], ["mnn"])
-        cp(sp, T.S1[:].indirect(T.LPI[:]), ["S1", "LPI"], ["sp"])
-        ts(am, T.KRS[:], 128.0, OP.is_ge, ["KRS", "VP0", "VP1"], ["am"])
-        tt(cl, nq, mnn, OP.mult, ["nq", "mnn"], ["cl"])
-        tt(sa, sp, am, OP.mult, ["sp", "am"], ["sa"])
-        tt(bm, T.KRP[:], T.C128[:], OP.is_equal, ["KRP", "C128"], ["bm"])
-        tt(m_, T.S1[:], sa, OP.max, ["S1", "sa"], ["m"])
-        tt(ef, am, bm, OP.max, ["am", "bm"], ["ef"])
-        tt(ds, T.SDV[:], m_, OP.subtract, ["SDV", "m"], ["ds"])
-        tt(T.CLE[:], cl, ef, OP.mult, ["cl", "ef"], ["CLE"])
-        op("t", lambda: mm(T.KA[:, 128:256], T.BOB[:], T.CLE[:], True, True), ["BOB", "CLE"], ["KA"])
-        tt(dsb, ds, bm, OP.mult, ["ds", "bm"], ["dsb"])
-        ts(kep, T.CLE[:], 0.0, OP.is_equal, ["CLE"], ["kep"])
-        tt(alt, m_, dsb, OP.add, ["m", "dsb"], ["alt"])
-        tt(k0, T.S1[:], kep, OP.mult, ["S1", "kep"], ["k0"])
-        ts(k0, k0, 767.0, OP.max, ["k0"], ["k0"])
-        ts(nan, T.KA[:, 128:256], 0.0, OP.is_equal, ["KA"], ["nan"])
-        tt(dd, alt, k0, OP.subtract, ["alt", "k0"], ["dd"])
-        tt(dsb, dd, nan, OP.mult, ["dd", "nan"], ["dsb"])
-        tt(T.S2[:], k0, dsb, OP.add, ["k0", "dsb", "VP0", "VP1"], ["S2"])
-        if t < NR - 1:
-            ts(T.L0T[:], T.S2[:], 1023, AND, ["S2"], ["L0T"])
-            ts(T.LE[:], T.L0T[:], C["QB"], OP.add, ["L0T", "cQB"], ["LE"])
-    ts(T.L0T[:], T.S2[:], 10, SHR, ["S2"], ["L0T"])
-    ts(T.YO[:], T.L0T[:], -1.0, OP.add, ["L0T"], ["YO"])
+            op("v", lambda c=c, pk=pk: V.tensor_reduce(T.KB[:, c:c + 1], pk[:, (c % 4) * 128:(c % 4) * 128 + 128], AxisListType.X, OP.min,
+                                                       apply_absolute_value=True), ["PK%d" % (c // 4)], ["KB%d" % c], 106.0)
+        kb = ["KB%d" % c for c in range(8)] + ["REP"]
+        tt(T.M1[:], T.KB[:].indirect(T.REP[:]), T.DL[:], OP.mult, kb + ["DL"], ["M1"], gns(128))
+        act(T.MU[:], T.KB[:].indirect(T.REP[:]), kb, ["MU"], t=gns(128))
+        pe([(T.KA[:, 0:8], T.M1[:], T.CSEL[:], True, True)], ["M1", "CSEL"], "KA", 64)
+        pe([(T.VP0[:, 0:128], T.MU[:], T.IB[:], True, True)], ["MU", "IB"], "VP0", 128)
+        cp(T.LQ[:], T.KA[:, 0:8], ["KA"], ["LQ"])
+        act(T.KRS[:, 0:128], T.VP0[:, 0:128], ["VP0"], ["KRS"], t=106)
+        act(T.KRP[:], T.KRS[:].indirect(T.LQ[:]), ["KRS", "KRe", "LQ"], ["KRP"], t=gns(128))
+        tt(T.NE1[:], T.NMW[:].indirect(T.LQ[:]), T.DN[:, 2::4], OP.not_equal, ["NMW", "NMe", "DN2", "LQ"], ["NE1"], gns(128))
+        tt(T.NE2[:], T.FLW[:, 0:144].indirect(T.LQ[:]), T.FLW[:, 144:272], OP.not_equal, ["FLW", "FLe", "FL2", "LQ"], ["NE2"], gns(128))
+        pq = (T.VP1[:, 0:128], T.VP1[:, 128:256])
+        for tag, a, b, stop in (("NE1", T.BOB, T.IB, False), ("KRP", T.IBN, T.IB, False), ("NE2", T.BON, T.IBN, True)):
+            pe([(pq[0], a[:], T[tag][:], False, False), (pq[1], b[:], T[tag][:], False, stop)], ["BOB", "BON", "IB", "IBN", tag], "VP1", 256)
+        tt(T.D0[:, 1::4], T.KRS[:, 0:128], T.TI[:], OP.is_ge, ["KRS", "TI"], ["D01"], 212)
+        ts(T.D0[:, 2::4], pq[0], 0.5, OP.is_lt, ["VP1"], ["D02"], t=106)
+        ts(T.D0[:, 3::4], pq[1], 0.5, OP.is_lt, ["VP1"], ["D03"], t=106)
+        for on, wn, wt, m, sd, out, x in ((more, "SLW", ["SLW0", "SLW1", "SLe"], "MS", "SDS", "SS", "DS"),
+                                          (True, "NMW", ["NMW", "NMe"], "MQ", "SDN", "SN", "DN")):
+            for h in range(2 if on else 0):
+                hh, y = slice(h * 64, h * 64 + 64), "%d" % h
+                tt(T[m][:, hh], T[wn][:].indirect(T.LQ[:, h * 4:h * 4 + 4]), T[x][:, h * 256 + 2:h * 256 + 256:4], OP.max,
+                   wt + [x + "2", "LQ"], [m + y], gns(64))
+                tt(T[x][:, h * 256:h * 256 + 256:4], T[m][:, hh], T[sd][:, hh], OP.subtract, [m + y, sd], [x + "0" + y], 106)
+                for o in range(h * 256, h * 256 + 256, 128):
+                    scan(T[out][:, o:o + 128], T.D0[:, o:o + 128], T[x][:, o:o + 128], OP.mult, OP.add,
+                         ["D0%d" % i for i in range(4)] + [x + "0" + y, x + "1" + y, x + "2", x + "3"], [out + "%d" % (o // 128)], 106)
+                if x == "DS":
+                    cp(T.LE[:, hh], T.SS[:, h * 256 + 3:h * 256 + 256:4], ["SS%d" % (2 * h), "SS%d" % (2 * h + 1)], ["LE" + y])
+    ts(T.YO[:], T.SN[:, 3::4], -1.0, OP.add, SNT, ["YO"], t=106)
     dma("y", T.yp[:], T.YO[:], ["YO"], ["yp"])
 
-    need = {"v": cnt["v"], "s": cnt["s"], "t": cnt["t"], "gp": cnt["g"], "ls": ls[0], "nm": 7, "hn": 7, "ft": 7, "fs": 7}
+    Q = {"v": V, "s": S, "t": PE, "g": g, "y": g.sync}
+    SEM = {"v": "v", "s": "s", "t": "t", "g": "gp"}
+    cnt = {e: 0 for e in SEM}
+    clk = {e: {} for e in Q}
+    hist, tok, ndma = {}, {}, [0]
+
+    def wait(e, need):
+        for s, n in sorted(need.items()):
+            if clk[e].get(s, 0) < n:
+                Q[e].wait_ge(T.sem[s], n)
+                for s2, n2 in hist.get((s, n), {}).items():
+                    clk[e][s2] = max(clk[e].get(s2, 0), n2)
+                clk[e][s] = max(clk[e].get(s, 0), n)
+
+    for i in order_calls(ops):
+        o = ops[i]
+        e = o["e"]
+        need = {}
+        for s, n in [tok[j] for j in o["sems"]] + o["ext"]:
+            need[s] = max(need.get(s, 0), n)
+        wait(e, need)
+        ins = o["fn"]()
+        if o["kind"] == "d":
+            tok[i] = ("d%d" % ndma[0], 16)
+            ndma[0] += 1
+            ins.then_inc(T.sem[tok[i][0]], 16)
+        elif o["kind"] == "c":
+            for x in (ins if isinstance(ins, list) else [ins]):
+                x.then_inc(T.sem[SEM[e]], 1)
+                cnt[e] += 1
+            tok[i] = (SEM[e], cnt[e])
+        if i in tok:
+            hist[tok[i]] = dict(clk[e])
+
+    need = {"v": cnt["v"], "s": cnt["s"], "t": cnt["t"], "gp": cnt["g"], "ls": ls[0], "nm": 28, "ft": 28, "fs": 28}
     for i in range(ndma[0]):
         need["d%d" % i] = 16
-    for q in range(NR):
-        if q != rank:
-            need["ta%d" % q] = 8
-            need["tb%d" % q] = ntb[q]
+    for q in ntz:
+        need["tz%d" % q] = ntz[q]
     wait("y", need)

@@ -6,25 +6,27 @@ AF = ActivationFunctionType
 NR, W = 8, 4096
 H2, Q4 = W // 2, W // 4
 MSG = 272
-FT, FS, FW = 16, 16 + NR * MSG, 16 + NR * MSG + 2048
+FT = 16 + (NR - 1) * 128
+FS = FT + NR * MSG
+BIG = 4194304.0
 WAKE = 160
 
 f32, b16, h16, i32, u16 = "float32", "bfloat16", "float16", "int32", "uint16"
 SCRATCH = {}
 for _d, _l in (
-        (b16, "TZ 32768 F 5136 X 4224 Z0 1024 Z1 1024 VF 2048 VA 2048 MX 2048 MN 2048 EREP 2048 SBT 2176 SBS 2048 Y 4096 RM 512 R255 512 "
-              "BOB 128 BON 128 IB 128 IBN 128 WD 144 MK 128 PC 256 E2 128 E1 128 FLW 272 NE1 128 NE2 128 KRP 128 M1 128 MU 128 CSEL 8 TI2 256"),
-        (h16, "TPH 256 PERM 512 NMO 256 NM 256 NMT 256 SW 272 BOH 128 IH 128 WS 144 RR 512 SGP 1024 SGN 1024 "
+        (b16, "TZ 32768 F 5136 X 4224 Z0 1024 Z1 1024 VF 2048 LT 128 FLB 128 MX 2048 MN 2048 SBT 2176 SBS 2048 Y 4096 RM 512 R255 512 SEL 1024 EREP 2048 E1 128 "
+              "BOB 128 BON 128 IB 128 IBN 128 WD 144 MK 128 PC 128 ET 256 FLW 272 NE1 128 NE2 128 KRP 128 MM 256 MSK 32 CSEL 8"),
+        (h16, "TPH 256 PERM 512 NMO 256 NM 256 NMT 256 SW 272 BOH 128 IH 128 WS 144 RR 256 SGP 1024 SGN 1024 "
               "A16 128 KX 128 HGD 128 W1L 1024 W2L 1024 NEG 64 E2H 128 C2 128"),
         (i32, "TPI 128 SDI 128 HWI 3 THI 1 HT 16 IP 16 IC 256 IC15 256 ICG 128 UI 16 UA 16 PP 8 VI 16 HI 128 HM 256 KI 16 KF 16"),
-        (u16, "EL 64 REP 8 LL 256 LE 128 LH 256 LP 16 LN 8 LF 8 LQ 8"),
-        (f32, "COL 32 DL 128 RB 64 CT 8 CBC 16 NMX 8 ISX 8 IX2 8 KCF 8 THK 8 KC 1024 US 384 KK 128 HC 272 KS 256 E2M 128 HIM 128 "
-              "SENT 8 KF1 8 KB 8 KRS 144 NMW 144 SLW 144 IF 128 TI 128 TPS 128 SDS 128 SDN 128 NMI 128 NM0 128 FLN 128 SL0 128 WSL 128 "
-              "MS 128 MQ 128 D0 512 DS 512 DN 512 SS 512 SN 512 PR 256 YO 128")):
+        (u16, "REP 8 LL 256 LE 128 LH 256 LP 16 LN 8 LF 8 LQ 8 LR 8"),
+        (f32, "COL 32 DL 128 RB 320 CT 8 CBC 16 NMX 8 ISX 8 IX2 8 WB 8 KCF 8 THK 8 KC 1024 US 384 KK 128 HC 272 KS 384 E2M 128 HIM 128 "
+              "SENT 16 KB 8 KRS 144 NMW 144 SLW 144 IF 128 TI 128 TPS 128 NMI 128 NM0 128 SL0 128 FST 128 OWN 128 BOF 128 "
+              "D0 896 DS 512 DN 512 BS 1552 BN 1552 SS 384 SN 384 PR 256 YO 128")):
     _l = _l.split()
     for _i in range(0, len(_l), 2):
         SCRATCH[_l[_i]] = ("sbuf", [128, int(_l[_i + 1])], _d)
-BANKS = ("BK0", "BK1", "PK0", "PK1", "HS", "KA", "VP0", "VP1")
+BANKS = ("BK0", "BK1", "D00", "D01", "D10", "D11", "HS", "KA")
 for _n in BANKS:
     SCRATCH[_n] = ("psum", [128, 512], f32)
 SEMAPHORES = ["v", "s", "t", "gp", "nm", "ft", "fs", "ls", "hz0", "hz1", "hz2"] + ["d%d" % i for i in range(8)] + \
@@ -107,20 +109,17 @@ def rank_program(g, core, T, topo):
 
     rank = T.rank_of(core)
     if rank is None:
-        for r in range(NR):
-            if relay[r] == core:
-                mine = [c for c in chips if r in c][0]
-                if r == mine[-1]:
-                    d = targets(r)[0]
-                    g.wait_ge(T.sem.hz2, 4)
-                    send(d, mine[0] * W + Q4, mine[0] * W + H2, "tz%d" % mine[0], topo.engines(core, d)[:8])
-                for n, d in enumerate(targets(r)):
-                    for i in range(2):
-                        if n == 0:
-                            g.wait_ge(T.sem["hz%d" % i], 4 if i == 0 and r != mine[-1] else 8)
-                        o = r * W + H2 + i * Q4
-                        send(d, o, o + Q4, "tz%d" % r, topo.engines(core, d)[:8])
-                g.wait_ge(T.sem.ls, ls[0])
+        for a, b in chips:
+            to = targets(a)
+            jobs = {relay[b]: [("hz2", to[0], a, Q4, H2)],
+                    relay[a]: [("hz0", to[0], a, H2, H2 + Q4), ("hz1", to[0], a, H2 + Q4, W), ("hz2", to[0], b, H2, W)] +
+                              [(None, d, r, H2, W) for d in to[1:] for r in (a, b)]}
+            for sem, d, r, lo, hi in jobs.get(core, ()):
+                if sem:
+                    g.wait_ge(T.sem[sem], 8)
+                send(d, r * W + lo, r * W + hi, "tz%d" % r, topo.engines(core, d)[:8])
+        if ls[0]:
+            g.wait_ge(T.sem.ls, ls[0])
         return
 
     ops, lastw, readers = [], {}, {}
@@ -191,8 +190,8 @@ def rank_program(g, core, T, topo):
     def act(out, a, R, Wt, func=AF.Copy, bias=0.0, scale=1.0, t=53.0):
         op("s", lambda: S.activation(out, a, func, bias=bias, scale=scale), R, Wt, t)
 
-    def pe(calls, R, bank, cols):
-        op("t", lambda: [mm(*c) for c in calls][-1 if len(calls) == 16 else 0:], R, [bank], 0.5 * cols)
+    def pe(calls, R, bank, cols, line=()):
+        op("t", lambda: [mm(*c) for c in calls][-1 if len(calls) == 16 else 0:], R, [bank] + list(line), 0.5 * cols)
 
     def rem(fn, R):
         return op("g", fn, R, ["g"], 700.0, "r")
@@ -255,33 +254,35 @@ def rank_program(g, core, T, topo):
     fe = topo.engines(core, T.cores[far[0]])
     ne = [e for e in topo.engines(core, T.cores[near]) if e not in fe]
 
-    def spread(src, dst, sem):
-        for n in range(0, len(far), 2):
-            to = [(far[n], fe[:4]), (far[n + 1], fe[4:8])] + ([(near, ne[:4])] if n == 0 else [])
+    short = ([(far[n], fe[2 * n:2 * n + 2]) for n in range(4)], [(far[4], fe[0:2]), (far[5], fe[2:4]), (near, fe[4:8])])
+    long = [[(far[n], fe[:4]), (far[n + 1], fe[4:8])] + [(near, ne[:8])][:n // 4] for n in range(0, 6, 2)]
+
+    def spread(src, dst, sem, calls):
+        for to in calls:
             g.remote_dma_fused([RemoteDMATransfer(dst_ids=[did(T.cores[r])], dma_engine_mask=mask_of(e), remote_sem=T.sem[sem],
                                                   srcs=[src(r)], dsts=[dst]) for r, e in to], local_sem=T.sem.ls)
-            ls[0] += 4 * len(to)
+            ls[0] += sum(len(e) for r, e in to)
 
-    sent = rem(lambda: spread(lambda r: T.NMO[:, r * 32:r * 32 + 32], T.NM[:, rank * 32:rank * 32 + 32], "nm"), ["NMO"])
-    lastw["NM"] = ("nm", 28, sent, 5000.0)
+    sent = rem(lambda: spread(lambda r: T.NMO[:, r * 32:r * 32 + 32], T.NM[:, rank * 32:rank * 32 + 32], "nm", short), ["NMO"])
+    lastw["NM"] = ("nm", 16, sent, 5000.0)
 
     def first_quarters():
-        to = [(targets(rank)[0], 0, "tz%d" % rank, fe[:8]), (relay[near], 1, "hz2", ne[:4]), (relay[rank], 2, "hz0", ne[4:8])]
+        to = [(targets(rank)[0], 0, "tz%d" % rank, fe[:8]), (relay[rank], 2, "hz0", ne[:8])]
         g.remote_dma_fused([RemoteDMATransfer(dst_ids=[did(d)], dma_engine_mask=mask_of(e), remote_sem=T.sem[s],
                                               srcs=[T.TZ[:, z0 + i * Q4:z0 + (i + 1) * Q4]], dsts=[T.TZ[:, z0 + i * Q4:z0 + (i + 1) * Q4]])
                             for d, i, s, e in to], local_sem=T.sem.ls)
         ls[0] += 16
+        send(relay[near], z0 + Q4, z0 + H2, "hz2", ne[:8])
         send(relay[rank], z0 + 3 * Q4, z0 + W, "hz1", ne[:8])
 
     def hand_on(q):
-        rem(lambda: send(T.cores[near], q * W, (q + 1) * W, "tz%d" % q, ne[:8]), ["TZa", "TZb"] if q == rank else ["TZ%d" % q])
+        rem(lambda: send(T.cores[near], q * W, (q + 1) * W, "tz%d" % q, fe + ne if last else ne), ["TZa", "TZb"] if q == rank else ["TZ%d" % q])
 
     if last:
-        hand_on(rank)
-        rem(lambda: [send(relay[rank], z0 + H2 + i * Q4, z0 + H2 + (i + 1) * Q4, "hz%d" % i, ne[:8]) for i in range(2)], ["TZb"])
+        rem(lambda: send(T.cores[near], z0, z0 + H2, "tz%d" % rank, ne[:8]), ["TZa"])
     else:
         rem(first_quarters, ["TZa", "TZb"])
-    ntz = {q: (32 if q == far[0] else 24) if last and q in far else 8 for q in range(NR) if q != rank}
+    ntz = {q: 32 if last and q == far[0] else 8 if last and q == near else 16 for q in range(NR) if q != rank}
 
     col("K", "K", 1.0, OP.mult)
     col("B3", "B3", 8.0, OP.add)
@@ -327,19 +328,23 @@ def rank_program(g, core, T, topo):
                 cp(buf[:, o + 256:o + MSG], T.HT[:], ["HT%d" % i for i in range(7)], [tags[-1]])
         own = 3 - ty
         sem = ("ft", "fs")[ty]
-        sent = rem(lambda: spread(lambda r: sb[:, r * wid:(r + 1) * wid], T.F[:, f0 + rank * wid:f0 + (rank + 1) * wid], sem), tags[:-own])
-        lastw[sem] = (sem, 28, sent, 7000.0)
+        sent = rem(lambda: spread(lambda r: sb[:, r * wid:(r + 1) * wid], T.F[:, f0 + rank * wid:f0 + (rank + 1) * wid], sem, long), tags[:-own])
+        lastw[sem] = (sem, 32, sent, 7000.0)
+        if last and ty == 0:
+            rem(lambda: send(T.cores[near], z0 + H2, z0 + W, "tz%d" % rank, ne[:8]), ["TZb"])
+            rem(lambda: send(relay[near], z0 + H2, z0 + W, "hz2", ne[:8]), ["TZb"])
         return sent, [sem] + tags[-own:]
 
-    fill(T.F[:, 0:FT], -256.0, ["Fe"])
+    fill(T.F[:, 0:FT], 127.0, ["Fe", "FW"], 380)
     ftp = feats(0)[1] + ["Fe"]
     sent, fsd = feats(1)
     for n in range(NR - 1):
         lastw["TZ%d" % ((rank + 1 + n) % NR)] = ("tz%d" % ((rank + 1 + n) % NR), ntz[(rank + 1 + n) % NR], sent, 1000.0 + 12000.0 * n)
-    for d in targets(rank)[0 if last else 1:]:
-        rem(lambda d=d: send(d, z0, z0 + H2, "tz%d" % rank, fe[:8]), ["TZa"])
     for q in (far if last else [rank]):
         hand_on(q)
+    if not last:
+        for d, r in [(d, r) for d in targets(rank) for r in mine][1:]:
+            rem(lambda d=d, r=r: send(d, r * W, r * W + H2, "tz%d" % r, fe[:8]), ["TZa", "TZ%d" % near])
 
     col("PG", "G", 16.0, OP.mult)
     col("PGF", "cPG", 15.0, OP.add)
@@ -353,20 +358,24 @@ def rank_program(g, core, T, topo):
         fill(rm[:, 0::16], x, ["RM%d" % b])
     fill(T.US[:, 256:384], 0.0, ["RU"], 106)
     fill(T.US[:, 256:384:16], -1e9, ["RU"])
-    fill(T.RB[:], 0.0, ["RB"])
-    fill(T.RB[:, 0::16], 1e9, ["RB"])
+    col("KH", "K", -1024.0, OP.add)
+    fill(T.RB[:, 0:256], -1.0, ["RB"], 212)
+    ts(T.RB[:, 15:256:16], T.IC[:, 15:256:16], BIG, OP.add, ["IC"], ["RB"])
+    fill(T.RB[:, 256:320], 0.0, ["RB"])
+    fill(T.RB[:, 271:320:16], BIG, ["RB"])
     fill(T.NEG[:], -2048.0, ["NEG"])
-    fill(T.X[:, 4096:4224], -1024.0, ["Xe"])
     for b, x, tag in ((T.NMW, 0.0, "NMe"), (T.SLW, 0.0, "SLe"), (T.FLW, 0.0, "FLe"), (T.KRS, -1.0, "KRe")):
         fill(b[:, 128:144], x, [tag])
-    fill(T.D0[:, 0::4], 0.0, ["D00"], 106)
-    fill(T.DS[:, 3::4], 0.0, ["DS3"], 106)
-    fill(T.DN[:, 3::4], 0.0, ["DN3"], 106)
-    for h in range(2):
-        fill(T.E1[:, h * 64 + 48:h * 64 + 64], 0.0, ["E1z%d" % h])
+    for a, x in ((T.D0[:, 1:512:2], 1.0), (T.D0[:, 0:512:4], 0.0), (T.D0[:, 512::3], 0.0)):
+        fill(a, x, ["F0"], 106)
+    fill(T.E1[:], 0.0, ["E1z", "E10", "E11"])
+    fill(T.BN[:, 17::12], 0.0, ["DN5"], 106)
     ts(T.IC15[:], T.IC[:], 15, AND, ["IC"], ["IC15"], t=212)
     ts(T.ICG[:], ic, 112, AND, ["IC"], ["ICG"], t=106)
-    ts(T.EL[:], T.ICG[:, 0:64], C["K"], OP.add, ["ICG", "cK"], ["EL"])
+    for c in range(4):
+        ts(T.SEL[:, c * 256:c * 256 + 256], T.IC15[:], 16.0 * c, OP.add, ["IC15", "cP"], ["SEL%d" % c], C["P"], OP.is_equal, t=212)
+    ts(T.MSK[:, 0::2], T.IC[:, 0:16], C["K"], OP.is_equal, ["IC", "cK"], ["MSK0"])
+    fill(T.MSK[:, 1::2], 1.0, ["MSK1"])
     ts(T.MK[:], T.IC15[:, 0:128], C["K"], OP.not_equal, ["IC15", "cK"], ["MK"], -4194304.0, OP.mult, t=106)
     ts(T.IB[:], ic, C["P"], OP.is_equal, ["IC", "cP"], ["IB"], t=106)
     ts(T.IBN[:], ic, C["P"], OP.is_equal, ["IC", "cP"], ["IBN"], -1.0, OP.mult, t=106)
@@ -378,31 +387,49 @@ def rank_program(g, core, T, topo):
     cp(T.REP[:], T.IC[:, 0:8], ["IC"], ["REP"])
     ts(T.WD[:], T.IC[:, 0:144], C["PGF"], OP.is_equal, ["IC", "cPGF"], ["WD"], 512.0, OP.mult, t=120)
     ts(T.WS[:], T.IC[:, 0:144], C["PGF"], OP.is_equal, ["IC", "cPGF"], ["WS"], t=120)
-    cp(T.PC[:], T.IC[:], ["IC"], ["PC"], 212)
+    cp(T.PC[:], ic, ["IC"], ["PC"], 106)
     cp(T.TI[:], ic, ["IC"], ["TI"], 106)
-    cp(T.TI2[:, 0:128], ic, ["IC"], ["TI2a"], 106)
-    ts(T.TI2[:, 128:256], ic, -1.0, OP.mult, ["IC"], ["TI2b"], t=106)
     ts(T.CSEL[:], T.IC[:, 0:8], C["G8"], OP.is_equal, ["IC", "cG8"], ["CSEL"])
-    ts(T.CT[:], T.IC[:, 0:8], 256.0, OP.add, ["IC"], ["CT"])
+    ts(T.CT[:], T.IC[:, 0:8], BIG + 256.0, OP.add, ["IC"], ["CT"])
     ts(T.HC[:, 256:272], T.IC[:, 0:16], -32.0, OP.mult, ["IC", "cNK"], ["HCe"], C["NK"], OP.add)
     ts(T.NMX[:], T.IC[:, 0:8], 2.0, OP.mult, ["IC", "cK"], ["NMX"], C["K"], OP.not_equal)
     ts(T.ISX[:], T.IC[:, 0:8], 2.0, OP.mult, ["IC", "cK"], ["ISX"], C["K"], OP.is_equal)
     ts(T.IX2[:], T.ISX[:], 2048.0, OP.mult, ["ISX"], ["IX2"])
     tt(T.KCF[:], T.F[:, FT + 258:FS:MSG], T.F[:, FT + 259:FS:MSG], OP.add, ftp, ["KCF"])
-    tt(T.SENT[:], T.F[:, FT + 260:FS:MSG], T.F[:, FT + 261:FS:MSG], OP.add, ftp, ["SENT"])
-    ts(T.THK[:], T.SENT[:], -1.0, OP.add, ["SENT"], ["THK"], 512.0, OP.mult)
+    tt(T.SENT[:, 0:8], T.F[:, FT + 260:FS:MSG], T.F[:, FT + 261:FS:MSG], OP.add, ftp, ["SENT"])
+    ts(T.THK[:], T.SENT[:, 0:8], -1.0, OP.add, ["SENT"], ["THK"], 512.0, OP.mult)
     ts(T.NMI[:], T.TPI[:], 1.0, OP.add, ["TPI"], ["NMI"], t=106)
-    ts(T.SDN[:], T.SDI[:], 1.0, OP.add, ["SDI"], ["SDN"], t=106)
+    ts(T.DN[:, 2::4], T.SDI[:], 1.0, OP.add, ["SDI"], ["DN2"], t=106)
+    ts(T.DN[:, 1::4], T.SDI[:], 1.0, OP.add, ["SDI"], ["DN1"], -1.0, OP.mult, t=106)
     ts(T.TPS[:], ic, C["JT"], OP.add, ["IC", "cJT"], ["TPS"], t=106)
     ts(T.PR[:, 0:128], ic, C["J128"], OP.add, ["IC", "cJ128"], ["pr0"], t=106)
-    ts(T.PR[:, 128:256], T.SDI[:], 0.0, OP.is_ge, ["SDI"], ["pr1"], t=106)
-    tt(T.SDS[:], T.PR[:, 0:128], T.PR[:, 128:256], OP.mult, ["pr0", "pr1"], ["SDS"], 212)
-    ts(T.PR[:, 128:256], T.TPI[:], 0.0, OP.is_ge, ["TPI"], ["pr1"], t=106)
-    tt(T.PR[:, 0:128], T.TPS[:], T.PR[:, 128:256], OP.mult, ["TPS", "pr1"], ["pr0"], 212)
-    cp(T.LE[:], T.PR[:, 0:128], ["pr0"], ["LE0", "LE1"], 106)
+    ts(T.BOF[:], T.ICG[:], C["PG"], OP.is_equal, ["ICG", "cPG"], ["BOF"], t=106)
+    ts(T.LT[:], ic, C["P"], OP.is_gt, ["IC", "cP", "cPGF"], ["LT"], t=106)
+    tt(T.LT[:], T.LT[:], T.BOB[:], OP.mult, ["LT", "BOB"], ["LT"], 212)
+
+    def first_row(masked):
+        pe([(T.KA[:, 256:384], T.LT[:], T.FLB[:], True, True)], ["LT", "FLB"], "KA", 128)
+        act(T.KA[:, 384:512], T.KA[:, 256:384], ["KA"], ["KA"], AF.Relu, bias=1.0, scale=-1.0, t=106)
+        tt(T.FST[:], T.SL0[:], T.KA[:, 384:512], OP.mult, ["SL0", "KA"], ["FST"], 106)
+        pe([(T.KA[:, 256:384], T.IB[:], T.MK[:], True, False)][:masked] + [(T.KA[:, 256:384], T.BOF[:], T.FST[:], not masked, True)],
+           ["IB", "MK", "BOF", "FST"], "KA", 640)
+
+    for src, sl, tag in ((T.TPI, T.TPS[:], "TPS"), (T.SDI, T.PR[:, 0:128], "pr0")):
+        ts(T.FLB[:], src[:], 0.0, OP.is_ge, ["TPI", "SDI"], ["FLB"], t=106)
+        tt(T.SL0[:], sl, T.FLB[:], OP.mult, [tag, "FLB"], ["SL0"], 212)
+        first_row(False)
+        ts(T.PR[:, 128:256], src[:], 0.0, OP.is_lt, ["TPI", "SDI"], ["pr1"], t=106)
+        tt(T.OWN[:], T.PR[:, 128:256], T.KA[:, 256:384], OP.mult, ["pr1", "KA"], ["OWN"], 106)
+        tt(T.DS[:, 2::4], T.OWN[:], T.SL0[:], OP.add, ["OWN", "SL0"], ["DS2"], 212)
+        if tag == "TPS":
+            cp(T.LE[:], T.DS[:, 2::4], ["DS2"], ["LE0", "LE1"], 106)
+    ts(T.DS[:, 1::4], T.DS[:, 2::4], -1.0, OP.mult, ["DS2"], ["DS1"], t=106)
+    for t in range(NR - 1):
+        q = (rank + 1 + t) % NR
+        ts(T.WB[:, t:t + 1], T.ISX[:, q:q + 1], float(FT - 128 - t * 128), OP.mult, ["ISX"], ["WB%d" % t])
     cp(T.A16[:], ic, ["IC"], ["A16"], 106)
     ts(T.KX[:], T.IH[:], 128.0, OP.mult, ["IH"], ["KX"])
-    for c in range(4):
+    for c in range(2):
         tt(T.RR[:, c * 128:c * 128 + 128], T.KX[:], T.A16[:], OP.max, ["KX", "A16"], ["RR%d" % c], 212)
     for b, sg in enumerate((T.SGP, T.SGN)):
         ts(T.CBC[:, b * 8:b * 8 + 8], T.CSEL[:], 1024.0 - 2048.0 * b, OP.mult, ["CSEL"], ["CBC%d" % b])
@@ -420,7 +447,14 @@ def rank_program(g, core, T, topo):
         act(T.KC[:, o], T.KA[:, 256:384], ["KA"], ["KC%d" % q], t=106)
 
     bk = [T.BK0, T.BK1]
-    CH = ((0, 384), (384, 768))
+    VN = 768
+    CH = [((0, 384), (384, 768)), ((0, 384), (384, 640), (640, 768))]
+    AB = CH
+    EC = [(("v", 0, 384), ("s", 384, 704), ("s", 704, 1024)), (("s", 0, 384), ("s", 384, 704), ("s", 704, 1024))]
+    SELT = ["SEL%d" % c for c in range(4)]
+
+    def xtags(i):
+        return ["X%d_s" % i] + ["X%d_%d" % (i, a) for a, b in CH[i % 2]]
 
     def u_mm(q, h, src, tag):
         o = slice(q * 128, q * 128 + 128)
@@ -432,31 +466,29 @@ def rank_program(g, core, T, topo):
 
     def middle(h, q, win, R):
         x = "%d" % h
-        for b in range(2):
-            o = slice(h * 1024 + b * 512, h * 1024 + b * 512 + 512)
-            y = x + "ab"[b]
-            src = win.indirect(T.LE[:, h * 64 + b * 32:h * 64 + b * 32 + 32])
-            if b == 0:
-                cp(T.VF[:, o], src, R + ["LE" + x], ["VF" + y], gns(512))
-            else:
-                act(T.VF[:, o], src, R + ["LE" + x], ["VF" + y], t=gns(512))
-            act(T.VA[:, o], T.VF[:, o], ["VF" + y], ["VA" + y], AF.Abs, t=425)
-            scan(T.MX[:, o], T.RM[:], T.VF[:, o], OP.mult, OP.max, ["RM0", "VF" + y], ["MX" + y], 212)
-            scan(T.MN[:, o], T.R255[:], T.VA[:, o], OP.max, OP.min, ["RM1", "VA" + y], ["MN" + y], 212)
+        for e, a, b in EC[h]:
+            o = slice(h * 1024 + a, h * 1024 + b)
+            y = x + "_%d" % a
+            src = win.indirect(T.LE[:, h * 64 + a // 16:h * 64 + b // 16])
+            (cp if e == "v" else act)(T.VF[:, o], src, R + ["LE" + x], ["VF" + y], t=gns(b - a))
+            scan(T.MX[:, o], T.RM[:, 0:b - a], T.VF[:, o], OP.mult, OP.max, ["RM0", "VF" + y], ["MX" + y], ns(b - a, 0.5))
+            scan(T.MN[:, o], T.R255[:, 0:b - a], T.VF[:, o], OP.max, OP.min, ["RM1", "VF" + y], ["MN" + y], ns(b - a, 0.5))
         hh = slice(h * 64, h * 64 + 64)
         end = slice(h * 1024 + 15, h * 1024 + 1024, 16)
-        ts(T.HIM[:, hh], T.MX[:, end], 2047.5, OP.add, ["MX" + x + "a", "MX" + x + "b"], ["HIM" + x])
-        tt(T.E2H[:, hh], T.HIM[:, hh], T.MN[:, end], OP.add, ["HIM" + x, "MN" + x + "a", "MN" + x + "b"], ["E2H" + x], 106)
+        ts(T.HIM[:, hh], T.MX[:, end], 2047.5, OP.add, ["MX%d_%d" % (h, c[1]) for c in EC[h]], ["HIM" + x])
+        tt(T.E2H[:, hh], T.HIM[:, hh], T.MN[:, end], OP.add, ["HIM" + x] + ["MN%d_%d" % (h, c[1]) for c in EC[h]], ["E2H" + x], 106)
         u_mm(q, h, T.E2H[:, hh], "E2H" + x)
-        e2 = T.E2[:, hh]
-        ts(e2, T.E2H[:, hh], -2048.0, OP.add, ["E2H" + x], ["E2" + x])
-        for n, (a, b) in enumerate(CH + ((768, 1024),)):
-            act(T.EREP[:, h * 1024 + a:h * 1024 + b], e2.indirect(T.EL[:, a // 16:b // 16]), ["E2" + x, "EL"], ["EREP%s_%d" % (x, n)],
-                scale=0.5, t=gns(b - a))
-        b = h * 64
-        act(T.E2M[:, b:b + 48], T.E2[:, b:b + 48], ["E2" + x], ["E2Ma" + x], AF.Identity, bias=2047.5)
-        act(T.E2M[:, b + 48:b + 64], T.E2[:, b + 48:b + 64], ["E2" + x], ["E2Mb" + x], AF.Identity, bias=2047.5, scale=0.5)
-        act(T.E1[:, b:b + 48], T.E2[:, b:b + 48], ["E2" + x], ["E1" + x], scale=0.5)
+        o = slice(h * 128, h * 128 + 128)
+        pe([(T.KA[0:64, o], T.E2H[:, hh], T.IH[:], True, True)], ["E2H" + x, "IH"], "KA", 128)
+        act(T.ET[0:64, o], T.KA[0:64, o], ["KA"], ["ET" + x], AF.Identity, bias=1024.0, scale=-0.5, t=106)
+        for b in range(2 if VN > 512 else 1):
+            n, bank = min(512, VN - 512 * b), "D%d%d" % (h, b)
+            pe([(T[bank][:, 0:n], T.ET[0:64, o], T.SEL[0:64, b * 512:b * 512 + n], True, True)], ["ET" + x] + SELT, bank, n)
+            act(T.EREP[:, h * 1024 + b * 512:h * 1024 + b * 512 + n], T[bank][:, 0:n], [bank], ["EREP%d%d" % (h, b)], scale=-1.0, t=ns(n))
+        a, b = slice(h * 64, h * 64 + VN // 16), slice(h * 64 + VN // 16, h * 64 + 64)
+        ts(T.E2M[:, a], T.E2H[:, a], -0.5, OP.add, ["E2H" + x], ["E2Ma" + x])
+        ts(T.E2M[:, b], T.E2H[:, b], 0.5, OP.mult, ["E2H" + x], ["E2Mb" + x], 1023.5, OP.add)
+        ts(T.E1[:, a], T.E2H[:, a], 0.5, OP.mult, ["E2H" + x], ["E1" + x], -1024.0, OP.add)
 
     def hashes(p, h, q):
         x = "%d" % h
@@ -478,42 +510,44 @@ def rank_program(g, core, T, topo):
     def search(p, h, q):
         i = p * 2 + h
         x = "%d" % h
-        x0, l0, e0 = i * 1024, i * 64, h * 1024
+        x0, l0 = i * 1024, i * 64
         tz = T.TZ[:, q * W:q * W + W]
         R = (["TZa", "TZb"] if q == rank else ["TZ%d" % q]) + ["LH%d" % i]
-        zb, xp, key = T["Z" + x], T["VP" + x][:, 0:256], bk[h][:, 128:192]
-        pe([(key, T.IB[:], T.PC[:, l0:l0 + 64], True, False)], ["IB", "PC"], "BK" + x, 64)
-        pe([(xp, T.IBN[:], T.EREP[:, e0 + 768:e0 + 1024], True, False)], ["IBN", "EREP%s_2" % x], "VP" + x, 256)
-        act(T.X[:, x0 + 768:x0 + 1024], tz.indirect(T.LH[:, l0 + 48:l0 + 64]), R, ["X%d_2" % i], t=gns(256))
-        pe([(xp, T.IB[:], T.X[:, x0 + 768:x0 + 1024], False, True)], ["IB", "X%d_2" % i], "VP" + x, 256)
-        act(zb[:, 768:1024], xp, ["VP" + x], ["Z%s_2" % x], AF.Abs, t=212)
-        for n, (a, b) in enumerate(CH):
-            tt(T.X[:, x0 + a:x0 + b], tz.indirect(T.LH[:, l0 + a // 16:l0 + b // 16]), T.EREP[:, e0 + a:e0 + b], OP.subtract,
-               R + ["EREP%s_%d" % (x, n)], ["X%d_%d" % (i, n)], gns(b - a))
-            act(zb[:, a:b], T.X[:, x0 + a:x0 + b], ["X%d_%d" % (i, n)], ["Z%s_%d" % (x, n)], AF.Abs, t=ns(b - a))
-        pe([(key, T.WD[:, 15 - k:143 - k], zb[:, k::16], False, k == 15) for k in range(16)],
-           ["WD"] + ["Z%s_%d" % (x, n) for n in range(3)], "BK" + x, 1024)
-        scan(T.KS[:, l0:l0 + 64], T.RB[:], key, OP.max, OP.min, ["RB", "BK" + x], ["KS%d" % i])
+        zb, key = T["Z" + x], bk[h][:, 128:192]
+        bank, xp = "D%d1" % h, T["D%d1" % h][:, VN - 512:512]
+        pe([(xp, T.ET[0:64, h * 128:h * 128 + 128], T.SEL[0:64, VN:1024], True, False)], ["ET" + x] + SELT, bank, 1024 - VN)
+        act(T.X[:, x0 + VN:x0 + 1024], tz.indirect(T.LH[:, l0 + VN // 16:l0 + 64]), R, ["X%d_s" % i], t=gns(1024 - VN))
+        pe([(xp, T.IB[:], T.X[:, x0 + VN:x0 + 1024], False, True)], ["IB", "X%d_s" % i], bank, 1024 - VN)
+        act(zb[:, VN:1024], xp, [bank], ["Z%s_s" % x], AF.Abs, t=ns(1024 - VN))
+        for a, b in CH[h]:
+            tt(T.X[:, x0 + a:x0 + b], tz.indirect(T.LH[:, l0 + a // 16:l0 + b // 16]), T.EREP[:, h * 1024 + a:h * 1024 + b], OP.subtract,
+               R + ["EREP%d%d" % (h, c) for c in range(a // 512, (b - 1) // 512 + 1)], ["X%d_%d" % (i, a)], gns(b - a))
+        for a, b in AB[h]:
+            act(zb[:, a:b], T.X[:, x0 + a:x0 + b], ["X%d_%d" % (i, c) for c, d in CH[h] if c < b and d > a], ["Z%s_%d" % (x, a)], AF.Abs, t=ns(b - a))
+        pe([(key, T.WD[:, 15 - k:143 - k], zb[:, k::16], k == 0, k == 15) for k in range(16)],
+           ["WD", "Z%s_s" % x] + ["Z%s_%d" % (x, a) for a, b in AB[h]], "BK" + x, 1024)
+        op("v", lambda: V.tensor_tensor_scan(T.KS[:, l0:l0 + 64], key, T.RB[:, l0:l0 + 64], BIG, OP.min, OP.add), ["RB", "BK" + x], ["KS%d" % i], 53.0)
+        if p == 0:
+            op("v", lambda: V.tensor_tensor_scan(T.KS[:, 256 + l0:320 + l0], key, T.RB[:, 256:320], BIG, OP.min, OP.add), ["RB", "BK" + x], ["KD%d" % i], 53.0)
 
     def restart(h, q):
         x = "%d" % h
         hh = slice(h * 64, h * 64 + 64)
-        ki, ka, lp = T.KI[:, h * 8:h * 8 + 4], T.KI[:, h * 8 + 4:h * 8 + 8], T.LP[:, h * 8:h * 8 + 4]
+        ka, lp = T.KI[:, h * 4:h * 4 + 4], T.LP[:, h * 8:h * 8 + 4]
         ends = T.KS[:, h * 64 + 15:h * 64 + 64:16]
-        cp(ki, ends, ["KS" + x], ["KI" + x])
-        ts(ka, ki, 63, AND, ["KI" + x], ["KA_" + x])
-        ts(lp, ka, 16.0, OP.mult, ["KA_" + x, "cK"], ["LP" + x], C["K"], OP.add)
+        tt(ka, ends, T.KS[:, 256 + h * 64 + 15:256 + h * 64 + 64:16], OP.subtract, ["KS" + x, "KD" + x], ["KI" + x])
+        ts(lp, ka, 16.0, OP.mult, ["KI" + x, "cK", "cKH"], ["LP" + x], C["K" if h == 0 else "KH"], OP.add)
         tt(T.C2[:, hh], T.X[:, h * 1024:h * 1024 + 1024].indirect(lp), T.E2M[:, hh], OP.add,
-           ["X%s_%d" % (x, n) for n in range(3)] + ["LP" + x, "E2Ma" + x, "E2Mb" + x], ["C2" + x], gns(64))
+           xtags(h) + ["LP" + x, "E2Ma" + x, "E2Mb" + x], ["C2" + x], gns(64))
         u_mm(q, h, T.C2[:, hh], "C2" + x)
-        tt(T.KF1[:, h * 4:h * 4 + 4], ends, T.SENT[:, h * 4:h * 4 + 4], OP.min, ["KS" + x, "SENT"], ["KF1" + x])
+        tt(T.SENT[:, 8 + h * 4:12 + h * 4], ends, T.SENT[:, h * 4:h * 4 + 4], OP.min, ["KS" + x, "SENT"], ["KF1" + x])
 
     def winner(h, q):
         x = "%d" % h
         c = slice(h * 4, h * 4 + 4)
         hh = slice(h * 64, h * 64 + 64)
         pl = T.KF[:, 8 + h * 4:12 + h * 4]
-        tt(T.KF[:, c], T.KS[:, 128 + h * 64 + 15:192 + h * 64:16], T.KF1[:, c], OP.min, ["KS%d" % (2 + h), "KF1" + x], ["KF" + x])
+        tt(T.KF[:, c], T.KS[:, 128 + h * 64 + 15:192 + h * 64:16], T.SENT[:, 8 + h * 4:12 + h * 4], OP.min, ["KS%d" % (2 + h), "KF1" + x], ["KF" + x])
         ts(pl, T.KF[:, c], 511, AND, ["KF" + x], ["PL" + x])
         cp(T.LN[:, c], pl, ["PL" + x], ["LN" + x])
         tt(T.HGD[:, hh], T.HC[:].indirect(T.LN[:, c]), T.DL[:, 0:64], OP.mult, ["HC0", "HC1", "HC2", "HC3", "HCe", "LN" + x, "DL"],
@@ -521,32 +555,37 @@ def rank_program(g, core, T, topo):
         ts(T.LF[:, c], pl, 16.0, OP.mult, ["PL" + x, "cK"], ["LF" + x], C["K"], OP.add)
 
     hash_consts((rank + 1) % NR)
-    SNT = ["SN%d" % i for i in range(4)]
+    SNT, SST = ["SN%d" % i for i in range(4)], ["SS%d" % i for i in range(4)]
+    PK = ("D00", "D01", "D10", "D11")
     for t in range(NR):
         q = (rank + 1 + t) % NR
         more = t < NR - 1
         qc = slice(q, q + 1)
         if more:
             hash_consts((q + 1) % NR)
-        nmn = T.NMI[:] if t == 0 else T.SN[:, 3::4]
-        win, R = (T.F[:, 0:FS], ftp) if t == 0 else (T.F[:, 0:FW + t * 128], ftp + fsd + ["FW"])
+        nmn = T.NMI[:] if t == 0 else T.SN[:, 2::3]
+        win, R = (T.F[:, 0:FS], ftp) if t == 0 else (T.F[:], ftp + fsd + ["FW"])
+        fw = FT - 128 - t * 128
         for h in range(2):
             middle(h, q, win, R)
-        ts(T.SENT[:], T.CT[:], T.THK[:, qc], OP.add, ["CT", "THK"], ["SENT"])
-        ts(T.NM0[:], nmn, T.NMX[:, qc], OP.mult, ["NMI", "NMX", "IX2"] + SNT, ["NM0"], T.IX2[:, qc], OP.add, t=106)
+        ts(T.SENT[:, 0:8], T.CT[:], T.THK[:, qc], OP.add, ["CT", "THK"], ["SENT"])
+        act(T.NM0[:], nmn, ["NMI", "NMX", "IX2"] + SNT, ["NM0"], AF.Identity, bias=T.IX2[:, qc], scale=T.NMX[:, qc], t=106)
         pe([(T.HS[:, 0:128], T.IF[:], T.NM0[:], True, False)], ["IF", "NM0"], "HS", 512)
-        for b in range(2):
-            pe([(T["PK%d" % b][:], T.IH[:], T.RR[:], True, False)], ["IH"] + ["RR%d" % c for c in range(4)], "PK%d" % b, 512)
         if more:
-            ts(T.FLN[:], nmn, 0.5, OP.is_ge, ["NMI", "NMX"] + SNT, ["FLN"], T.NMX[:, qc], OP.mult, t=106)
-            ts(T.WSL[:], ic, float(FW + t * 128), OP.add, ["IC", "ISX"], ["WSL"], T.ISX[:, qc], OP.mult, t=106)
-            for h in range(2):
-                hh, x = slice(h * 64, h * 64 + 64), "%d" % h
-                sl = T.TPS[:, hh] if t == 0 else T.SS[:, h * 256 + 3:h * 256 + 256:4]
-                tt(T.SL0[:, hh], sl, T.FLN[:, hh], OP.mult, ["TPS", "SS%d" % (2 * h), "SS%d" % (2 * h + 1), "FLN"], ["SL0" + x], 106)
-                tt(T.SLW[:, hh], T.SL0[:, hh], T.WSL[:, hh], OP.add, ["SL0" + x, "WSL"], ["SLW" + x], 106)
-                tt(T.DS[:, h * 256 + 1:h * 256 + 256:4], T.SDS[:, hh], T.SLW[:, hh], OP.subtract, ["SDS", "SLW" + x], ["DS1" + x], 106)
-            act(T.DS[:, 2::4], T.SLW[:, 0:128], ["SLW0", "SLW1"], ["DS2"], t=106)
+            act(T.KA[:, 0:128], nmn, ["NMI", "NMX"] + SNT, ["KA"], AF.Sign, scale=T.NMX[:, qc], t=106)
+            act(T.KA[:, 128:256], T.TI[:], ["TI", "ISX", "WB%d" % t], ["KA"], AF.Identity, bias=T.WB[:, t:t + 1], scale=T.ISX[:, qc], t=106)
+            tt(T.SL0[:], T.TPS[:] if t == 0 else T.SS[:, 2::3], T.KA[:, 0:128], OP.mult, ["TPS", "KA"] + SST, ["SL0"], 106)
+            tt(T.SLW[:, 0:128], T.SL0[:], T.KA[:, 128:256], OP.add, ["SL0", "KA"], ["SLW"], 106)
+            act(T.KA[:, 0:128], T.TI[:], ["TI"], ["KA"], AF.Identity, bias=float(fw), t=106)
+            act(T.BS[:, 17::12], T.TI[:], ["TI"], ["DS5"], AF.Identity, bias=float(fw), t=106)
+            tt(T.OWN[:], T.SL0[:], T.KA[:, 0:128], OP.max, ["SL0", "KA"], ["OWN"], 106)
+            tt(T.BS[:, 13:1549:12], T.OWN[:], T.KA[:, 0:128], OP.subtract, ["OWN", "KA"], ["DS4"], 106)
+            act(T.DS[:, 3::4], T.OWN[:], ["OWN"], ["DS3"], scale=-1.0, t=106)
+            act(T.FLB[:], nmn, ["NMI", "NMX"] + SNT, ["FLB"], AF.Sign, scale=T.NMX[:, qc], t=106)
+            first_row(True)
+            scan(T.PR[:, 0:128], T.US[:, 256:384], T.KA[:, 256:384], OP.add, OP.max, ["RU", "KA"], ["pr0"], 106)
+            cp(T.LR[:], T.PR[:, 15:128:16], ["pr0"], ["LR"])
+            tt(T.X[:, 4096:4224], win.indirect(T.LR[:]), T.E1[:], OP.subtract, R + ["LR", "E10", "E11", "E1z"], ["Xe"], gns(128))
         for h in range(2):
             hashes(0, h, q)
             search(0, h, q)
@@ -555,61 +594,68 @@ def rank_program(g, core, T, topo):
             hashes(1, h, q)
             search(1, h, q)
         wl = T.WS[:, 15 - 2 * q:143 - 2 * q]
+        for b in range(4):
+            pe([(T[PK[b]][:, 0:256], T.IH[:], T.RR[:], True, False)], ["IH", "RR0", "RR1"], PK[b], 256)
+        for b in range(2):
+            pe([(bk[b][:, 256:384], (T.IB, T.IBN)[b][:], T.PC[:, 0:128], True, False)], ["IB", "IBN", "PC"], "BK%d" % b, 128)
         for h in range(2):
             winner(h, q)
             hh = slice(h * 64, h * 64 + 64)
-            for b in range(2):
-                pk = T["PK%d" % b]
-                calls = [(pk[:, c * 128 + h * 64:c * 128 + h * 64 + 64], T.SGP[:, (b * 4 + c) * 128:(b * 4 + c + 1) * 128], T.HGD[:, hh], False, False)
-                         for c in range(4)]
+            for b in range(4):
+                pk = T[PK[b]]
+                calls = [(pk[:, c * 128 + h * 64:c * 128 + h * 64 + 64], T.SGP[:, (b * 2 + c) * 128:(b * 2 + c + 1) * 128], T.HGD[:, hh], False, False)
+                         for c in range(2)]
                 if h == 1:
-                    calls.append((pk[:], T.HGD[:], T.SGN[:, b * 512:b * 512 + 512], False, True))
-                pe(calls, ["HGD%d" % i for i in range(h + 1)] + ["SG%d_%d" % (i, b * 4 + c) for i in range(2) for c in range(4)], "PK%d" % b, 256 + 512 * h)
+                    calls.append((pk[:, 0:256], T.HGD[:], T.SGN[:, b * 256:b * 256 + 256], False, True))
+                pe(calls, ["HGD%d" % i for i in range(h + 1)] + ["SG%d_%d" % (i, b * 2 + c) for i in range(2) for c in range(2)], PK[b], 128 + 256 * h)
             pe([(T.HS[:, hh], wl, T.HGD[:, hh], False, h == 1)], ["WS", "HGD%d" % h], "HS", 64)
-        pe([(T.VP1[:, 0:256], T.IB[:], T.TI2[:], True, False)], ["IB", "TI2a", "TI2b"], "VP1", 256)
         act(T.NMW[:, 0:128], T.HS[:, 0:128], ["HS"], ["NMW"], AF.Relu, t=106)
+        act(T.BN[:, 13:1549:12], T.HS[:, 0:128], ["HS"], ["DN4"], AF.Relu, t=106)
         act(T.FLW[:, 0:128], T.NMW[:, 0:128], ["NMW"], ["FLW"], AF.Sign, t=106)
         act(T.FLW[:, 144:272], T.NMW[:, 0:128], ["NMW"], ["FL2"], AF.Sign, t=106)
-        act(T.DN[:, 2::4], T.NMW[:, 0:128], ["NMW"], ["DN2"], t=106)
-        for h in range(2):
-            tt(T.DN[:, h * 256 + 1:h * 256 + 256:4], T.SDN[:, h * 64:h * 64 + 64], T.NMW[:, h * 64:h * 64 + 64], OP.subtract,
-               ["SDN", "NMW"], ["DN1%d" % h], 106)
+        act(T.DN[:, 3::4], T.NMW[:, 0:128], ["NMW"], ["DN3"], scale=-1.0, t=106)
         if more:
-            tt(T.F[:, FW + t * 128:FW + t * 128 + 128], T.X[:].indirect(T.LF[:]), T.E1[:], OP.add,
-               ["X%d_%d" % (i, n) for i in range(4) for n in range(3)] + ["Xe", "LF0", "LF1", "E10", "E11", "E1z0", "E1z1"], ["FW"], gns(128))
+            tt(T.F[:, fw:fw + 128], T.X[:].indirect(T.LF[:]), T.E1[:], OP.add,
+               [a for i in range(4) for a in xtags(i)] + ["Xe", "LF0", "LF1", "E10", "E11", "E1z"], ["FW"], gns(128))
         for c in range(8):
-            pk = T["PK%d" % (c // 4)]
-            op("v", lambda c=c, pk=pk: V.tensor_reduce(T.KB[:, c:c + 1], pk[:, (c % 4) * 128:(c % 4) * 128 + 128], AxisListType.X, OP.min,
-                                                       apply_absolute_value=True), ["PK%d" % (c // 4)], ["KB%d" % c], 106.0)
-        kb = ["KB%d" % c for c in range(8)] + ["REP"]
-        tt(T.M1[:], T.KB[:].indirect(T.REP[:]), T.DL[:], OP.mult, kb + ["DL"], ["M1"], gns(128))
-        act(T.MU[:], T.KB[:].indirect(T.REP[:]), kb, ["MU"], t=gns(128))
-        pe([(T.KA[:, 0:8], T.M1[:], T.CSEL[:], True, True)], ["M1", "CSEL"], "KA", 64)
-        pe([(T.VP0[:, 0:128], T.MU[:], T.IB[:], True, True)], ["MU", "IB"], "VP0", 128)
+            pk = T[PK[c // 2]]
+            op("v", lambda c=c, pk=pk: V.tensor_reduce(T.KB[:, c:c + 1], pk[:, (c % 2) * 128:(c % 2) * 128 + 128], AxisListType.X, OP.min,
+                                                       apply_absolute_value=True), [PK[c // 2]], ["KB%d" % c], 106.0)
+            act(T.MM[:, c * 32:c * 32 + 32], T.MSK[:], ["KB%d" % c, "MSK0", "MSK1"], ["MM%d" % c], scale=T.KB[:, c:c + 1])
+        mmt = ["MM%d" % c for c in range(8)]
+        pe([(T.KA[:, 0:8], T.MM[:, 0::2], T.CSEL[:], True, True)], mmt + ["CSEL"], "KA", 64, ["first"])
+        pe([(T.HS[:, 128:256], T.MM[:, 1::2], T.IB[:], True, True)], mmt + ["IB"], "HS", 128, ["first"])
+        pe([(T.D00[:, 0:128], T.MM[:, 1::2], T.IB[:], True, False),
+            (T.D00[:, 0:128], T.IBN[:], T.PC[:, 0:128], False, True)], mmt + ["IB", "IBN", "PC"], "D00", 256, ["first"])
         cp(T.LQ[:], T.KA[:, 0:8], ["KA"], ["LQ"])
-        act(T.KRS[:, 0:128], T.VP0[:, 0:128], ["VP0"], ["KRS"], t=106)
+        act(T.KRS[:, 0:128], T.HS[:, 128:256], ["HS"], ["KRS"], t=106)
+        act(T.FST[:], T.D00[:, 0:128], ["D00"], ["FST"], AF.Relu, t=106)
         act(T.KRP[:], T.KRS[:].indirect(T.LQ[:]), ["KRS", "KRe", "LQ"], ["KRP"], t=gns(128))
-        tt(T.NE1[:], T.NMW[:].indirect(T.LQ[:]), T.DN[:, 2::4], OP.not_equal, ["NMW", "NMe", "DN2", "LQ"], ["NE1"], gns(128))
+        act(T.D0[:, 2:512:4], T.FST[:], ["FST"], ["F2"], AF.Sign, t=106)
+        tt(T.NE1[:], T.NMW[:].indirect(T.LQ[:]), T.BN[:, 13:1549:12], OP.not_equal, ["NMW", "NMe", "DN4", "LQ"], ["NE1"], gns(128))
         tt(T.NE2[:], T.FLW[:, 0:144].indirect(T.LQ[:]), T.FLW[:, 144:272], OP.not_equal, ["FLW", "FLe", "FL2", "LQ"], ["NE2"], gns(128))
-        pq = (T.VP1[:, 0:128], T.VP1[:, 128:256])
         for tag, a, b, stop in (("NE1", T.BOB, T.IB, False), ("KRP", T.IBN, T.IB, False), ("NE2", T.BON, T.IBN, True)):
-            pe([(pq[0], a[:], T[tag][:], False, False), (pq[1], b[:], T[tag][:], False, stop)], ["BOB", "BON", "IB", "IBN", tag], "VP1", 256)
-        tt(T.D0[:, 1::4], T.KRS[:, 0:128], T.TI[:], OP.is_ge, ["KRS", "TI"], ["D01"], 212)
-        ts(T.D0[:, 2::4], pq[0], 0.5, OP.is_lt, ["VP1"], ["D02"], t=106)
-        ts(T.D0[:, 3::4], pq[1], 0.5, OP.is_lt, ["VP1"], ["D03"], t=106)
-        for on, wn, wt, m, sd, out, x in ((more, "SLW", ["SLW0", "SLW1", "SLe"], "MS", "SDS", "SS", "DS"),
-                                          (True, "NMW", ["NMW", "NMe"], "MQ", "SDN", "SN", "DN")):
+            pe([(T.BK0[:, 256:384], a[:], T[tag][:], False, stop)], ["BOB", "BON", "IBN", tag], "BK0", 128)
+            pe([(T.BK1[:, 256:384], b[:], T[tag][:], False, stop)], ["IB", "IBN", tag], "BK1", 128)
+        act(T.D0[:, 513::3], T.BK0[:, 256:384], ["BK0"], ["F4"], AF.Relu, bias=1.0, scale=-1.0, t=106)
+        ts(T.D0[:, 514::3], T.BK1[:, 256:384], 0.5, OP.is_lt, ["BK1"], ["F5"], t=106)
+        for on, wn, out, x, b in ((more, "SLW", "SS", "DS", "BS"), (True, "NMW", "SN", "DN", "BN")):
             for h in range(2 if on else 0):
-                hh, y = slice(h * 64, h * 64 + 64), "%d" % h
-                tt(T[m][:, hh], T[wn][:].indirect(T.LQ[:, h * 4:h * 4 + 4]), T[x][:, h * 256 + 2:h * 256 + 256:4], OP.max,
-                   wt + [x + "2", "LQ"], [m + y], gns(64))
-                tt(T[x][:, h * 256:h * 256 + 256:4], T[m][:, hh], T[sd][:, hh], OP.subtract, [m + y, sd], [x + "0" + y], 106)
-                for o in range(h * 256, h * 256 + 256, 128):
-                    scan(T[out][:, o:o + 128], T.D0[:, o:o + 128], T[x][:, o:o + 128], OP.mult, OP.add,
-                         ["D0%d" % i for i in range(4)] + [x + "0" + y, x + "1" + y, x + "2", x + "3"], [out + "%d" % (o // 128)], 106)
+                y = "%d" % h
+                own = T.OWN[:, h * 64:h * 64 + 64] if x == "DS" else T.BN[:, h * 768 + 13:h * 768 + 781:12]
+                tt(T[x][:, h * 256:h * 256 + 256:4], T[wn][:].indirect(T.LQ[:, h * 4:h * 4 + 4]), own, OP.max,
+                   [wn, wn[:2] + "e", "OWN" if x == "DS" else "DN4", "LQ"], [x + "0" + y], gns(64))
+                for i in range(2 * h, 2 * h + 2):
+                    scan(T[b][:, i * 384:i * 384 + 384:3], T.D0[:, i * 128:i * 128 + 128], T[x][:, i * 128:i * 128 + 128], OP.mult, OP.add,
+                         ["F0", "F2", x + "0" + y] + [x + "%d" % j for j in range(1, 4)], [b + "%d" % i], 106)
+                for i in ([(2 * h, 2)] if x == "DS" or not more else [(2 * h, 1), (2 * h + 1, 1)]):
+                    tags = ["%d" % j for j in range(i[0], i[0] + i[1])]
+                    o, n = i[0] * 96, i[1] * 96
+                    scan(T[out][:, o:o + n], T.D0[:, 512 + o:512 + o + n], T[b][:, 4 * o + 9:4 * (o + n) + 9:4], OP.mult, OP.add,
+                         ["F0", "F4", "F5", x + "4", x + "5"] + [b + j for j in tags], [out + j for j in tags], ns(n))
                 if x == "DS":
-                    cp(T.LE[:, hh], T.SS[:, h * 256 + 3:h * 256 + 256:4], ["SS%d" % (2 * h), "SS%d" % (2 * h + 1)], ["LE" + y])
-    ts(T.YO[:], T.SN[:, 3::4], -1.0, OP.add, SNT, ["YO"], t=106)
+                    cp(T.LE[:, h * 64:h * 64 + 64], T.SS[:, h * 192 + 2:h * 192 + 192:3], SST[2 * h:2 * h + 2], ["LE" + y])
+    ts(T.YO[:], T.SN[:, 2::3], -1.0, OP.add, SNT, ["YO"], t=106)
     dma("y", T.yp[:], T.YO[:], ["YO"], ["yp"])
 
     Q = {"v": V, "s": S, "t": PE, "g": g, "y": g.sync}
@@ -646,7 +692,7 @@ def rank_program(g, core, T, topo):
         if i in tok:
             hist[tok[i]] = dict(clk[e])
 
-    need = {"v": cnt["v"], "s": cnt["s"], "t": cnt["t"], "gp": cnt["g"], "ls": ls[0], "nm": 28, "ft": 28, "fs": 28}
+    need = {"v": cnt["v"], "s": cnt["s"], "t": cnt["t"], "gp": cnt["g"], "ls": ls[0], "nm": 16, "ft": 32, "fs": 32}
     for i in range(ndma[0]):
         need["d%d" % i] = 16
     for q in ntz:

from concourse.bass import DstId, RemoteDMATransfer
from concourse.mybir import AluOpType, AxisListType, ActivationFunctionType

OP = AluOpType
AF = ActivationFunctionType
NR, W = 8, 4096
H2, Q4 = W // 2, W // 4
MSG = 272
FT = 16 + (NR - 1) * 128
FS = FT + NR * MSG
BIG = 4194304.0
WAKE = 160

f32, b16, h16, i32, u16 = "float32", "bfloat16", "float16", "int32", "uint16"
SCRATCH = {}
for _d, _l in (
        (b16, "TZ 32768 F 5136 X 4224 Z0 1024 Z1 1024 VF 2048 LT 128 FLB 128 MX 2048 MN 2048 SBT 2176 SBS 2048 Y 4096 RM 512 R255 512 SEL 1024 EREP 2048 E1 128 "
              "BOB 128 BON 128 IB 128 IBN 128 WD 144 MK 128 PC 128 ET 256 FLW 272 NE1 128 NE2 128 KRP 128 MM 256 MSK 32 CSEL 8"),
        (h16, "TPH 256 PERM 512 NMO 256 NM 256 NMT 256 SW 272 BOH 128 IH 128 WS 144 RR 256 SGP 1024 SGN 1024 "
              "A16 128 KX 128 HGD 128 W1L 1024 W2L 1024 NEG 64 E2H 128 C2 128"),
        (i32, "TPI 128 SDI 128 HWI 3 THI 1 HT 16 IP 16 IC 256 IC15 256 ICG 128 UI 16 UA 16 PP 8 VI 16 HI 128 HM 256 KI 16 KF 16"),
        (u16, "REP 8 LL 256 LE 128 LH 256 LP 16 LN 8 LF 8 LQ 8 LR 8"),
        (f32, "COL 32 DL 128 RB 320 CT 8 CBC 16 NMX 8 ISX 8 IX2 8 WB 8 KCF 8 THK 8 KC 1024 US 384 KK 128 HC 272 KS 384 E2M 128 HIM 128 "
              "SENT 16 KB 8 KRS 144 NMW 144 SLW 144 IF 128 TI 128 TPS 128 NMI 128 NM0 128 SL0 128 FST 128 OWN 128 BOF 128 "
              "D0 896 DS 512 DN 512 BS 1552 BN 1552 SS 384 SN 384 PR 256 YO 128")):
    _l = _l.split()
    for _i in range(0, len(_l), 2):
        SCRATCH[_l[_i]] = ("sbuf", [128, int(_l[_i + 1])], _d)
BANKS = ("BK0", "BK1", "D00", "D01", "D10", "D11", "HS", "KA")
for _n in BANKS:
    SCRATCH[_n] = ("psum", [128, 512], f32)
SEMAPHORES = ["v", "s", "t", "gp", "nm", "ft", "fs", "ls", "hz0", "hz1", "hz2"] + ["d%d" % i for i in range(8)] + \
    ["tz%d" % q for q in range(NR)]


def mask_of(engs):
    return sum(1 << e for e in engs)


def places(T, topo):
    chips, relay, used = [], {}, []
    for r, c in enumerate(T.cores):
        if not chips or topo.chip(T.cores[chips[-1][0]]) != topo.chip(c):
            chips.append([])
        chips[-1].append(r)
        relay[r] = [x for x in topo.cores_of(c) if x not in T.cores and x not in used and topo.die(x) != topo.die(c)
                    and all(topo.may_write(x, d) for d in T.cores)][0]
        used.append(relay[r])
    return chips, relay


def order_calls(ops):
    succ = [[] for _ in ops]
    for i, o in enumerate(ops):
        for j, lat in o["pre"].items():
            succ[j].append((i, lat))
    tail = [0.0] * len(ops)
    for i in range(len(ops) - 1, -1, -1):
        tail[i] = ops[i]["ns"] + max([lat + tail[j] for j, lat in succ[i]] + [0.0])
    left = [len(o["pre"]) for o in ops]
    ready = [0.0] * len(ops)
    free, pool, out = {}, {}, []
    for i, o in enumerate(ops):
        free[o["e"]] = 0.0
        pool.setdefault(o["e"], [])
        if not left[i]:
            pool[o["e"]].append(i)
    while len(out) < len(ops):
        e = min((x for x in pool if pool[x]), key=lambda x: max(free[x], min(ready[i] for i in pool[x])))
        now = max(free[e], min(ready[i] for i in pool[e]))
        rows = sorted(pool[e], key=lambda i: (-tail[i], i))
        pick = None
        for n, i in enumerate(rows):
            if ready[i] <= now and all(now + ops[i]["ns"] <= ready[j] + 30 or ready[j] + ops[j]["ns"] + tail[i] > now + ops[i]["ns"] + tail[j]
                                       for j in rows[:n]):
                pick = i
                break
        if pick is None:
            free[e] = min(ready[i] for i in pool[e] if ready[i] > now)
            continue
        pool[e].remove(pick)
        out.append(pick)
        free[e] = now + ops[pick]["ns"]
        for j, lat in succ[pick]:
            ready[j] = max(ready[j], free[e] + lat)
            left[j] -= 1
            if not left[j]:
                pool[ops[j]["e"]].append(j)
    return out


def rank_program(g, core, T, topo):
    chips, relay = places(T, topo)
    ncl = len(chips)
    ls = [0]

    def targets(r):
        n = [i for i in range(ncl) if r in chips[i]][0]
        return [T.cores[chips[(n - 1 - d) % ncl][-1]] for d in range(ncl - 1)]

    def did(c):
        a = topo.addr(c)
        return DstId(rid=a[0], pnc=a[1])

    def send(dst, lo, hi, sem, engs):
        rid, pid = topo.addr(dst)[:2]
        g.remote_dma(T.TZ[:, lo:hi], T.TZ[:, lo:hi], T.sem[sem], T.sem.ls, pid, rid, mask_of(engs))
        ls[0] += len(engs)

    rank = T.rank_of(core)
    if rank is None:
        for a, b in chips:
            to = targets(a)
            jobs = {relay[b]: [("hz2", to[0], a, Q4, H2)],
                    relay[a]: [("hz0", to[0], a, H2, H2 + Q4), ("hz1", to[0], a, H2 + Q4, W), ("hz2", to[0], b, H2, W)] +
                              [(None, d, r, H2, W) for d in to[1:] for r in (a, b)]}
            for sem, d, r, lo, hi in jobs.get(core, ()):
                if sem:
                    g.wait_ge(T.sem[sem], 8)
                send(d, r * W + lo, r * W + hi, "tz%d" % r, topo.engines(core, d)[:8])
        if ls[0]:
            g.wait_ge(T.sem.ls, ls[0])
        return

    ops, lastw, readers = [], {}, {}

    def op(e, fn, R, Wt, ns, kind="c"):
        me = len(ops)
        pre, sems, ext = {}, set(), []

        def edge(j, signal):
            lat = ops[j]["lat"] if signal else 0.0
            pre[j] = max(pre.get(j, 0.0), lat)
            if signal:
                sems.add(j)
        for tg in R:
            w = lastw.get(tg)
            if isinstance(w, tuple):
                ext.append(w[:2])
                pre[w[2]] = max(pre.get(w[2], 0.0), w[3])
            elif w is not None:
                edge(w, True)
            if tg in BANKS:
                for j in readers.get(tg, ()):
                    edge(j, ops[j]["e"] != e)
        for tg in Wt:
            if tg in lastw:
                edge(lastw[tg], not (e == ops[lastw[tg]]["e"] and e in "tg"))
            for j in readers.get(tg, ()):
                edge(j, True)
        ops.append({"e": e, "fn": fn, "pre": pre, "sems": sems, "ext": ext, "ns": ns, "kind": kind,
                    "lat": WAKE + (2200.0 if kind == "d" else 60.0 if e == "t" else 0.0)})
        for tg in R:
            readers.setdefault(tg, []).append(me)
        for tg in Wt:
            lastw[tg] = me
            readers[tg] = []
        return me

    V, S, PE = g.vector, g.scalar, g.tensor
    mm = PE.matmul

    def ns(n, k=1.0):
        return max(53.0, 0.83 * n * k)

    def gns(n):
        return 55.0 + 1.25 * n

    def dma(e, out, in_, R, Wt):
        op(e, lambda: {"y": g.sync, "s": S}[e].dma_start(out, in_), R, Wt, 60.0, "d")

    def ts(out, a, s1, o1, R, Wt, s2=None, o2=None, t=53.0):
        if o2 is None:
            op("v", lambda: V.tensor_scalar(out, a, s1, None, o1), R, Wt, t)
        else:
            op("v", lambda: V.tensor_scalar(out, a, s1, s2, o1, o2), R, Wt, t)

    def tt(out, a, b, o, R, Wt, t=53.0):
        op("v", lambda: V.tensor_tensor(out, a, b, o), R, Wt, t)

    def cp(out, a, R, Wt, t=53.0):
        op("v", lambda: V.tensor_copy(out, a), R, Wt, t)

    def fill(ap, x, Wt, t=53.0):
        op("v", lambda: V.memset(ap, x), [], Wt, t)

    def scan(out, d0, d1, o0, o1, R, Wt, t=53.0):
        op("v", lambda: V.tensor_tensor_scan(out, d0, d1, 0.0, o0, o1), R, Wt, t)

    def act(out, a, R, Wt, func=AF.Copy, bias=0.0, scale=1.0, t=53.0):
        op("s", lambda: S.activation(out, a, func, bias=bias, scale=scale), R, Wt, t)

    def pe(calls, R, bank, cols, line=()):
        op("t", lambda: [mm(*c) for c in calls][-1 if len(calls) == 16 else 0:], R, [bank] + list(line), 0.5 * cols)

    def rem(fn, R):
        return op("g", fn, R, ["g"], 700.0, "r")

    z0 = rank * W
    dma("y", T.TPI[:], T.tp[:], [], ["TPI"])
    dma("s", T.SDI[:], T.sd[:], [], ["SDI"])
    dma("y", T.TZ[:, z0:z0 + H2], T.tz[:, 0:H2], [], ["TZa"])
    dma("s", T.TZ[:, z0 + H2:z0 + W], T.tz[:, H2:W], [], ["TZb"])
    dma("y", T.HWI[:], T.hw[:], [], ["HWI"])
    dma("s", T.THI[:], T.th[:], [], ["THI"])
    op("g", lambda: g.iota(T.IP[:, 0:1], [[0, 1]], 0, 1), [], ["IP", "g"], 130.0)
    op("g", lambda: g.iota(T.IC[:], [[1, 256]], 0, 0), [], ["IC", "g"], 560.0)

    C = {}
    ip = {"P": T.IP[:, 0:1]}

    def icol(name, *a):
        n = len(ip)
        ip[name] = T.IP[:, n:n + 1]
        ts(ip[name], ip["P"], a[0], a[1], ["IP"], ["i" + name], *a[2:])

    def col(name, src, s1, o1, s2=None, o2=None, R=()):
        i = len(C)
        a = C[src[1:]] if src[0] == "c" else ip[src]
        C[name] = T.COL[:, i:i + 1]
        ts(C[name], a, s1, o1, ["IP", src if src[0] == "c" else "i" + src] + list(R), ["c" + name], s2, o2)

    AND, SHR = OP.bitwise_and, OP.arith_shift_right
    icol("K", 15, AND)
    icol("Q", 14, AND)
    icol("S", 1, AND)
    icol("G", 4, SHR)
    icol("B3", 3, SHR, 1, AND)
    icol("B4", 4, SHR, 1, AND)
    icol("B5", 5, SHR)
    icol("L", 7, AND)
    col("S8", "S", 8.0, OP.mult)
    col("G8", "G", 1.0, OP.mult)
    col("PM0", "Q", 16.0, OP.mult, C["S8"], OP.add, ["cS8"])
    col("PM", "cPM0", C["G8"], OP.add, None, None, ["cG8"])
    col("P", "P", 1.0, OP.mult)
    ic = T.IC[:, 0:128]
    ts(T.PERM[:, 0:256], T.IC[:], C["PM"], OP.is_equal, ["IC", "cPM"], ["PERM0"], t=212)
    ts(T.PERM[:, 256:512], T.IC[:], -16.0, OP.add, ["IC", "cPM"], ["PERM1"], C["PM"], OP.is_equal, t=212)
    ts(T.IH[:], ic, C["P"], OP.is_equal, ["IC", "cP"], ["IH"], t=106)
    ts(T.TPH[:, 0:128], T.TPI[:], -2047.0, OP.add, ["TPI"], ["TPH0"], t=106)
    ts(T.TPH[:, 128:256], T.SDI[:], -2047.0, OP.add, ["SDI"], ["TPH1"], t=106)
    pe([(T.HS[:, 0:256], T.TPH[:, 0:128], T.PERM[:, 0:256], True, False),
        (T.HS[:, 0:256], T.TPH[:, 128:256], T.PERM[:, 256:512], False, True)], ["TPH0", "TPH1", "PERM0", "PERM1"], "HS", 512)
    cp(T.NMO[:], T.HS[:, 0:256], ["HS"], ["NMO"], 212)
    cp(T.NM[:, rank * 32:rank * 32 + 32], T.NMO[:, rank * 32:rank * 32 + 32], ["NMO"], ["NMo"])

    mine = [c for c in chips if rank in c][0]
    here = chips.index(mine)
    far = [r for d in range(1, ncl) for r in chips[(here + d) % ncl]]
    near = [r for r in mine if r != rank][0]
    others = far + [near]
    last = rank == mine[-1]
    fe = topo.engines(core, T.cores[far[0]])
    ne = [e for e in topo.engines(core, T.cores[near]) if e not in fe]

    short = ([(far[n], fe[2 * n:2 * n + 2]) for n in range(4)], [(far[4], fe[0:2]), (far[5], fe[2:4]), (near, fe[4:8])])
    long = [[(far[n], fe[:4]), (far[n + 1], fe[4:8])] + [(near, ne[:8])][:n // 4] for n in range(0, 6, 2)]

    def spread(src, dst, sem, calls):
        for to in calls:
            g.remote_dma_fused([RemoteDMATransfer(dst_ids=[did(T.cores[r])], dma_engine_mask=mask_of(e), remote_sem=T.sem[sem],
                                                  srcs=[src(r)], dsts=[dst]) for r, e in to], local_sem=T.sem.ls)
            ls[0] += sum(len(e) for r, e in to)

    sent = rem(lambda: spread(lambda r: T.NMO[:, r * 32:r * 32 + 32], T.NM[:, rank * 32:rank * 32 + 32], "nm", short), ["NMO"])
    lastw["NM"] = ("nm", 16, sent, 5000.0)

    def first_quarters():
        to = [(targets(rank)[0], 0, "tz%d" % rank, fe[:8]), (relay[rank], 2, "hz0", ne[:8])]
        g.remote_dma_fused([RemoteDMATransfer(dst_ids=[did(d)], dma_engine_mask=mask_of(e), remote_sem=T.sem[s],
                                              srcs=[T.TZ[:, z0 + i * Q4:z0 + (i + 1) * Q4]], dsts=[T.TZ[:, z0 + i * Q4:z0 + (i + 1) * Q4]])
                            for d, i, s, e in to], local_sem=T.sem.ls)
        ls[0] += 16
        send(relay[near], z0 + Q4, z0 + H2, "hz2", ne[:8])
        send(relay[rank], z0 + 3 * Q4, z0 + W, "hz1", ne[:8])

    def hand_on(q):
        rem(lambda: send(T.cores[near], q * W, (q + 1) * W, "tz%d" % q, fe + ne if last else ne), ["TZa", "TZb"] if q == rank else ["TZ%d" % q])

    if last:
        rem(lambda: send(T.cores[near], z0, z0 + H2, "tz%d" % rank, ne[:8]), ["TZa"])
    else:
        rem(first_quarters, ["TZa", "TZb"])
    ntz = {q: 32 if last and q == far[0] else 8 if last and q == near else 16 for q in range(NR) if q != rank}

    col("K", "K", 1.0, OP.mult)
    col("B3", "B3", 8.0, OP.add)
    col("R2", "B5", 2.0, OP.mult, C["B3"], OP.add, ["cB3"])
    col("SW", "L", 16.0, OP.mult, C["R2"], OP.add, ["cR2"])
    col("T1", "B4", 1.0, OP.mult)
    col("T0", "B4", 0.0, OP.is_equal)
    for ty in range(2):
        ts(T.SW[:, ty * 136:ty * 136 + 136], T.IC[:, 0:136], C["SW"], OP.is_equal, ["IC", "cSW", "cT%d" % ty], ["SW%d" % ty],
           C["T%d" % ty], OP.mult, t=113)
    pe([(T.HS[:, b * 128:b * 128 + 128], T.NM[:, b * 128:b * 128 + 128], T.IH[:], True, True) for b in range(2)], ["NM", "NMo", "IH"], "HS", 256)
    cp(T.NMT[:], T.HS[:, 0:256], ["HS"], ["NMT"], 212)
    for ty in range(2):
        o = T.KA[:, ty * 128:ty * 128 + 128]
        pe([(o, T.SW[:, ty * 136 + 8:ty * 136 + 136], T.NMT[:, 0:128], True, False),
            (o, T.SW[:, ty * 136:ty * 136 + 128], T.NMT[:, 128:256], False, True)], ["SW0", "SW1", "NMT"], "KA", 256)
    ts(T.LL[:], T.KA[:, 0:256], 2047.0, OP.add, ["KA"], ["LL"], 0.0, OP.max, t=212)
    fill(T.HT[:, 7:16], 0, ["HT0"])
    cp(T.HT[:, 0:2], T.HWI[:, 0:2], ["HWI"], ["HT1"])
    ts(T.HT[:, 2:3], T.HWI[:, 2:3], 3840, AND, ["HWI"], ["HT2"])
    ts(T.HT[:, 3:4], T.HWI[:, 2:3], 255, AND, ["HWI"], ["HT3"])
    ts(T.HT[:, 6:7], T.THI[:], 4095.0, OP.min, ["THI"], ["HT6"])
    ts(T.HT[:, 4:5], T.HT[:, 6:7], 3840, AND, ["HT6"], ["HT4"])
    ts(T.HT[:, 5:6], T.HT[:, 6:7], 255, AND, ["HT6"], ["HT5"])

    def feats(ty):
        y0, wid, sb, f0 = ty * 2048, (MSG, 256)[ty], (T.SBT, T.SBS)[ty], (FT, FS)[ty]
        win = T.TZ[:, z0:z0 + W]
        act(T.Y[:, y0:y0 + 1024], win.indirect(T.LL[:, ty * 128:ty * 128 + 64]), ["TZa", "TZb", "LL"], ["Ya%d" % ty], t=gns(1024))
        cp(T.Y[:, y0 + 1024:y0 + 2048], win.indirect(T.LL[:, ty * 128 + 64:ty * 128 + 128]), ["TZa", "TZb", "LL"], ["Yb%d" % ty], gns(1024))
        tags = []
        for n, r in enumerate(others + [rank]):
            buf, o = (T.F, f0 + r * wid) if r == rank else (sb, r * wid)
            for s in range(2):
                tags.append("SB%d_%d_%d" % (r, ty, s))
                a = (buf[:, o + s * 128:o + s * 128 + 128], T.Y[:, y0 + 2 * r + s:y0 + 2048:16], ["Ya%d" % ty, "Yb%d" % ty], [tags[-1]])
                if (2 * n + s) % 3 == 2:
                    act(*a, t=106)
                else:
                    cp(*a)
            if ty == 0:
                tags.append("SBh%d" % r)
                cp(buf[:, o + 256:o + MSG], T.HT[:], ["HT%d" % i for i in range(7)], [tags[-1]])
        own = 3 - ty
        sem = ("ft", "fs")[ty]
        sent = rem(lambda: spread(lambda r: sb[:, r * wid:(r + 1) * wid], T.F[:, f0 + rank * wid:f0 + (rank + 1) * wid], sem, long), tags[:-own])
        lastw[sem] = (sem, 32, sent, 7000.0)
        if last and ty == 0:
            rem(lambda: send(T.cores[near], z0 + H2, z0 + W, "tz%d" % rank, ne[:8]), ["TZb"])
            rem(lambda: send(relay[near], z0 + H2, z0 + W, "hz2", ne[:8]), ["TZb"])
        return sent, [sem] + tags[-own:]

    fill(T.F[:, 0:FT], 127.0, ["Fe", "FW"], 380)
    ftp = feats(0)[1] + ["Fe"]
    sent, fsd = feats(1)
    for n in range(NR - 1):
        lastw["TZ%d" % ((rank + 1 + n) % NR)] = ("tz%d" % ((rank + 1 + n) % NR), ntz[(rank + 1 + n) % NR], sent, 1000.0 + 12000.0 * n)
    for q in (far if last else [rank]):
        hand_on(q)
    if not last:
        for d, r in [(d, r) for d in targets(rank) for r in mine][1:]:
            rem(lambda d=d, r=r: send(d, r * W, r * W + H2, "tz%d" % r, fe[:8]), ["TZa", "TZ%d" % near])

    col("PG", "G", 16.0, OP.mult)
    col("PGF", "cPG", 15.0, OP.add)
    col("J128", "K", 128.0, OP.mult, float(FS), OP.add)
    col("S128", "S", 128.0, OP.mult, float(FT), OP.add)
    col("JT", "Q", MSG / 2.0, OP.mult, C["S128"], OP.add, ["cS128"])
    col("NK", "K", -2.0, OP.mult, -2050.0, OP.add)
    for b, (x, y) in enumerate(((0.0, 1.0), (255.0, 0.0))):
        rm = (T.RM, T.R255)[b]
        fill(rm[:], y, ["RM%d" % b], 212)
        fill(rm[:, 0::16], x, ["RM%d" % b])
    fill(T.US[:, 256:384], 0.0, ["RU"], 106)
    fill(T.US[:, 256:384:16], -1e9, ["RU"])
    col("KH", "K", -1024.0, OP.add)
    fill(T.RB[:, 0:256], -1.0, ["RB"], 212)
    ts(T.RB[:, 15:256:16], T.IC[:, 15:256:16], BIG, OP.add, ["IC"], ["RB"])
    fill(T.RB[:, 256:320], 0.0, ["RB"])
    fill(T.RB[:, 271:320:16], BIG, ["RB"])
    fill(T.NEG[:], -2048.0, ["NEG"])
    for b, x, tag in ((T.NMW, 0.0, "NMe"), (T.SLW, 0.0, "SLe"), (T.FLW, 0.0, "FLe"), (T.KRS, -1.0, "KRe")):
        fill(b[:, 128:144], x, [tag])
    for a, x in ((T.D0[:, 1:512:2], 1.0), (T.D0[:, 0:512:4], 0.0), (T.D0[:, 512::3], 0.0)):
        fill(a, x, ["F0"], 106)
    fill(T.E1[:], 0.0, ["E1z", "E10", "E11"])
    fill(T.BN[:, 17::12], 0.0, ["DN5"], 106)
    ts(T.IC15[:], T.IC[:], 15, AND, ["IC"], ["IC15"], t=212)
    ts(T.ICG[:], ic, 112, AND, ["IC"], ["ICG"], t=106)
    for c in range(4):
        ts(T.SEL[:, c * 256:c * 256 + 256], T.IC15[:], 16.0 * c, OP.add, ["IC15", "cP"], ["SEL%d" % c], C["P"], OP.is_equal, t=212)
    ts(T.MSK[:, 0::2], T.IC[:, 0:16], C["K"], OP.is_equal, ["IC", "cK"], ["MSK0"])
    fill(T.MSK[:, 1::2], 1.0, ["MSK1"])
    ts(T.MK[:], T.IC15[:, 0:128], C["K"], OP.not_equal, ["IC15", "cK"], ["MK"], -4194304.0, OP.mult, t=106)
    ts(T.IB[:], ic, C["P"], OP.is_equal, ["IC", "cP"], ["IB"], t=106)
    ts(T.IBN[:], ic, C["P"], OP.is_equal, ["IC", "cP"], ["IBN"], -1.0, OP.mult, t=106)
    ts(T.IF[:], ic, C["P"], OP.is_equal, ["IC", "cP"], ["IF"], t=106)
    ts(T.DL[:], T.IC15[:, 0:128], C["K"], OP.is_equal, ["IC15", "cK"], ["DL"], t=106)
    ts(T.BOB[:], T.ICG[:], C["PG"], OP.is_equal, ["ICG", "cPG"], ["BOB"], t=106)
    ts(T.BON[:], T.ICG[:], C["PG"], OP.is_equal, ["ICG", "cPG"], ["BON"], -1.0, OP.mult, t=106)
    ts(T.BOH[:], T.ICG[:], C["PG"], OP.is_equal, ["ICG", "cPG"], ["BOH"], t=106)
    cp(T.REP[:], T.IC[:, 0:8], ["IC"], ["REP"])
    ts(T.WD[:], T.IC[:, 0:144], C["PGF"], OP.is_equal, ["IC", "cPGF"], ["WD"], 512.0, OP.mult, t=120)
    ts(T.WS[:], T.IC[:, 0:144], C["PGF"], OP.is_equal, ["IC", "cPGF"], ["WS"], t=120)
    cp(T.PC[:], ic, ["IC"], ["PC"], 106)
    cp(T.TI[:], ic, ["IC"], ["TI"], 106)
    ts(T.CSEL[:], T.IC[:, 0:8], C["G8"], OP.is_equal, ["IC", "cG8"], ["CSEL"])
    ts(T.CT[:], T.IC[:, 0:8], BIG + 256.0, OP.add, ["IC"], ["CT"])
    ts(T.HC[:, 256:272], T.IC[:, 0:16], -32.0, OP.mult, ["IC", "cNK"], ["HCe"], C["NK"], OP.add)
    ts(T.NMX[:], T.IC[:, 0:8], 2.0, OP.mult, ["IC", "cK"], ["NMX"], C["K"], OP.not_equal)
    ts(T.ISX[:], T.IC[:, 0:8], 2.0, OP.mult, ["IC", "cK"], ["ISX"], C["K"], OP.is_equal)
    ts(T.IX2[:], T.ISX[:], 2048.0, OP.mult, ["ISX"], ["IX2"])
    tt(T.KCF[:], T.F[:, FT + 258:FS:MSG], T.F[:, FT + 259:FS:MSG], OP.add, ftp, ["KCF"])
    tt(T.SENT[:, 0:8], T.F[:, FT + 260:FS:MSG], T.F[:, FT + 261:FS:MSG], OP.add, ftp, ["SENT"])
    ts(T.THK[:], T.SENT[:, 0:8], -1.0, OP.add, ["SENT"], ["THK"], 512.0, OP.mult)
    ts(T.NMI[:], T.TPI[:], 1.0, OP.add, ["TPI"], ["NMI"], t=106)
    ts(T.DN[:, 2::4], T.SDI[:], 1.0, OP.add, ["SDI"], ["DN2"], t=106)
    ts(T.DN[:, 1::4], T.SDI[:], 1.0, OP.add, ["SDI"], ["DN1"], -1.0, OP.mult, t=106)
    ts(T.TPS[:], ic, C["JT"], OP.add, ["IC", "cJT"], ["TPS"], t=106)
    ts(T.PR[:, 0:128], ic, C["J128"], OP.add, ["IC", "cJ128"], ["pr0"], t=106)
    ts(T.BOF[:], T.ICG[:], C["PG"], OP.is_equal, ["ICG", "cPG"], ["BOF"], t=106)
    ts(T.LT[:], ic, C["P"], OP.is_gt, ["IC", "cP", "cPGF"], ["LT"], t=106)
    tt(T.LT[:], T.LT[:], T.BOB[:], OP.mult, ["LT", "BOB"], ["LT"], 212)

    def first_row(masked):
        pe([(T.KA[:, 256:384], T.LT[:], T.FLB[:], True, True)], ["LT", "FLB"], "KA", 128)
        act(T.KA[:, 384:512], T.KA[:, 256:384], ["KA"], ["KA"], AF.Relu, bias=1.0, scale=-1.0, t=106)
        tt(T.FST[:], T.SL0[:], T.KA[:, 384:512], OP.mult, ["SL0", "KA"], ["FST"], 106)
        pe([(T.KA[:, 256:384], T.IB[:], T.MK[:], True, False)][:masked] + [(T.KA[:, 256:384], T.BOF[:], T.FST[:], not masked, True)],
           ["IB", "MK", "BOF", "FST"], "KA", 640)

    for src, sl, tag in ((T.TPI, T.TPS[:], "TPS"), (T.SDI, T.PR[:, 0:128], "pr0")):
        ts(T.FLB[:], src[:], 0.0, OP.is_ge, ["TPI", "SDI"], ["FLB"], t=106)
        tt(T.SL0[:], sl, T.FLB[:], OP.mult, [tag, "FLB"], ["SL0"], 212)
        first_row(False)
        ts(T.PR[:, 128:256], src[:], 0.0, OP.is_lt, ["TPI", "SDI"], ["pr1"], t=106)
        tt(T.OWN[:], T.PR[:, 128:256], T.KA[:, 256:384], OP.mult, ["pr1", "KA"], ["OWN"], 106)
        tt(T.DS[:, 2::4], T.OWN[:], T.SL0[:], OP.add, ["OWN", "SL0"], ["DS2"], 212)
        if tag == "TPS":
            cp(T.LE[:], T.DS[:, 2::4], ["DS2"], ["LE0", "LE1"], 106)
    ts(T.DS[:, 1::4], T.DS[:, 2::4], -1.0, OP.mult, ["DS2"], ["DS1"], t=106)
    for t in range(NR - 1):
        q = (rank + 1 + t) % NR
        ts(T.WB[:, t:t + 1], T.ISX[:, q:q + 1], float(FT - 128 - t * 128), OP.mult, ["ISX"], ["WB%d" % t])
    cp(T.A16[:], ic, ["IC"], ["A16"], 106)
    ts(T.KX[:], T.IH[:], 128.0, OP.mult, ["IH"], ["KX"])
    for c in range(2):
        tt(T.RR[:, c * 128:c * 128 + 128], T.KX[:], T.A16[:], OP.max, ["KX", "A16"], ["RR%d" % c], 212)
    for b, sg in enumerate((T.SGP, T.SGN)):
        ts(T.CBC[:, b * 8:b * 8 + 8], T.CSEL[:], 1024.0 - 2048.0 * b, OP.mult, ["CSEL"], ["CBC%d" % b])
        for c in range(8):
            ts(sg[:, c * 128:c * 128 + 128], T.A16[:], 0.0, OP.mult, ["A16", "CBC%d" % b], ["SG%d_%d" % (b, c)],
               T.CBC[:, b * 8 + c:b * 8 + c + 1], OP.add)

    def hash_consts(q):
        o = slice(q * 128, q * 128 + 128)
        f = FT + q * MSG + 256
        ts(T.W1L[:, o], T.BOH[:], T.F[:, f:f + 1], OP.mult, ["BOH"] + ftp, ["W1L%d" % q], 0.5, OP.mult)
        ts(T.W2L[:, o], T.BOH[:], T.F[:, f + 1:f + 2], OP.mult, ["BOH"] + ftp, ["W2L%d" % q], 0.5, OP.mult)
        ts(T.KX[:], T.DL[:], T.KCF[:, q:q + 1], OP.mult, ["DL", "KCF"], ["KX"], t=106)
        pe([(T.KA[:, 256:384], T.BOH[:], T.KX[:], True, True)], ["BOH", "KX"], "KA", 128)
        act(T.KC[:, o], T.KA[:, 256:384], ["KA"], ["KC%d" % q], t=106)

    bk = [T.BK0, T.BK1]
    VN = 768
    CH = [((0, 384), (384, 768)), ((0, 384), (384, 640), (640, 768))]
    AB = CH
    EC = [(("v", 0, 384), ("s", 384, 704), ("s", 704, 1024)), (("s", 0, 384), ("s", 384, 704), ("s", 704, 1024))]
    SELT = ["SEL%d" % c for c in range(4)]

    def xtags(i):
        return ["X%d_s" % i] + ["X%d_%d" % (i, a) for a, b in CH[i % 2]]

    def u_mm(q, h, src, tag):
        o = slice(q * 128, q * 128 + 128)
        w = ["W1L%d" % q, "W2L%d" % q]
        pe([(bk[h][:, 0:128], T.IB[:], T.MK[:], True, False)] +
           [(bk[h][:, u * 64:u * 64 + 64], wl[:, o], T.NEG[:], False, False) for u, wl in enumerate((T.W1L, T.W2L))],
           ["IB", "MK", "NEG"] + w, "BK%d" % h, 256)
        pe([(bk[h][:, u * 64:u * 64 + 64], wl[:, o], src, False, u == 1) for u, wl in enumerate((T.W1L, T.W2L))], w + [tag], "BK%d" % h, 128)

    def middle(h, q, win, R):
        x = "%d" % h
        for e, a, b in EC[h]:
            o = slice(h * 1024 + a, h * 1024 + b)
            y = x + "_%d" % a
            src = win.indirect(T.LE[:, h * 64 + a // 16:h * 64 + b // 16])
            (cp if e == "v" else act)(T.VF[:, o], src, R + ["LE" + x], ["VF" + y], t=gns(b - a))
            scan(T.MX[:, o], T.RM[:, 0:b - a], T.VF[:, o], OP.mult, OP.max, ["RM0", "VF" + y], ["MX" + y], ns(b - a, 0.5))
            scan(T.MN[:, o], T.R255[:, 0:b - a], T.VF[:, o], OP.max, OP.min, ["RM1", "VF" + y], ["MN" + y], ns(b - a, 0.5))
        hh = slice(h * 64, h * 64 + 64)
        end = slice(h * 1024 + 15, h * 1024 + 1024, 16)
        ts(T.HIM[:, hh], T.MX[:, end], 2047.5, OP.add, ["MX%d_%d" % (h, c[1]) for c in EC[h]], ["HIM" + x])
        tt(T.E2H[:, hh], T.HIM[:, hh], T.MN[:, end], OP.add, ["HIM" + x] + ["MN%d_%d" % (h, c[1]) for c in EC[h]], ["E2H" + x], 106)
        u_mm(q, h, T.E2H[:, hh], "E2H" + x)
        o = slice(h * 128, h * 128 + 128)
        pe([(T.KA[0:64, o], T.E2H[:, hh], T.IH[:], True, True)], ["E2H" + x, "IH"], "KA", 128)
        act(T.ET[0:64, o], T.KA[0:64, o], ["KA"], ["ET" + x], AF.Identity, bias=1024.0, scale=-0.5, t=106)
        for b in range(2 if VN > 512 else 1):
            n, bank = min(512, VN - 512 * b), "D%d%d" % (h, b)
            pe([(T[bank][:, 0:n], T.ET[0:64, o], T.SEL[0:64, b * 512:b * 512 + n], True, True)], ["ET" + x] + SELT, bank, n)
            act(T.EREP[:, h * 1024 + b * 512:h * 1024 + b * 512 + n], T[bank][:, 0:n], [bank], ["EREP%d%d" % (h, b)], scale=-1.0, t=ns(n))
        a, b = slice(h * 64, h * 64 + VN // 16), slice(h * 64 + VN // 16, h * 64 + 64)
        ts(T.E2M[:, a], T.E2H[:, a], -0.5, OP.add, ["E2H" + x], ["E2Ma" + x])
        ts(T.E2M[:, b], T.E2H[:, b], 0.5, OP.mult, ["E2H" + x], ["E2Mb" + x], 1023.5, OP.add)
        ts(T.E1[:, a], T.E2H[:, a], 0.5, OP.mult, ["E2H" + x], ["E1" + x], -1024.0, OP.add)

    def hashes(p, h, q):
        x = "%d" % h
        i = p * 2 + h
        us, kk, hi = T.US[:, h * 128:h * 128 + 128], T.KK[:, h * 64:h * 64 + 64], T.HI[:, h * 64:h * 64 + 64]
        ui, ua, pp, vi = T.UI[:, h * 8:h * 8 + 8], T.UA[:, h * 8:h * 8 + 8], T.PP[:, h * 4:h * 4 + 4], T.VI[:, h * 8:h * 8 + 4]
        scan(us, T.US[:, 256:384], bk[h][:, 0:128], OP.add, OP.max, ["RU", "BK" + x], ["US" + x], 106)
        cp(ui, T.US[:, h * 128 + 15:h * 128 + 128:16], ["US" + x], ["UI" + x])
        ts(ua, ui, 4095, AND, ["UI" + x], ["UA" + x])
        tt(pp, T.UA[:, h * 8:h * 8 + 4], T.UA[:, h * 8 + 4:h * 8 + 8], OP.mult, ["UA" + x], ["PP" + x])
        tt(kk, ua.indirect(T.REP[:, 4:8]), T.KC[:, q * 128:q * 128 + 64], OP.mult, ["UA" + x, "REP", "KC%d" % q], ["KK" + x], gns(64))
        ts(vi, pp, 5, SHR, ["PP" + x], ["VI" + x])
        tt(hi, vi.indirect(T.REP[:, 0:4]), kk, OP.add, ["VI" + x, "KK" + x, "REP"], ["HI" + x], gns(64))
        hm = T.HM[:, i * 64:i * 64 + 64]
        ts(hm, hi, 4095, AND, ["HI" + x], ["HM%d" % i])
        cp(T.LH[:, i * 64:i * 64 + 64], hm, ["HM%d" % i], ["LH%d" % i])
        ts(T.HC[:, i * 64:i * 64 + 64], hm, -2047.0, OP.add, ["HM%d" % i], ["HC%d" % i])

    def search(p, h, q):
        i = p * 2 + h
        x = "%d" % h
        x0, l0 = i * 1024, i * 64
        tz = T.TZ[:, q * W:q * W + W]
        R = (["TZa", "TZb"] if q == rank else ["TZ%d" % q]) + ["LH%d" % i]
        zb, key = T["Z" + x], bk[h][:, 128:192]
        bank, xp = "D%d1" % h, T["D%d1" % h][:, VN - 512:512]
        pe([(xp, T.ET[0:64, h * 128:h * 128 + 128], T.SEL[0:64, VN:1024], True, False)], ["ET" + x] + SELT, bank, 1024 - VN)
        act(T.X[:, x0 + VN:x0 + 1024], tz.indirect(T.LH[:, l0 + VN // 16:l0 + 64]), R, ["X%d_s" % i], t=gns(1024 - VN))
        pe([(xp, T.IB[:], T.X[:, x0 + VN:x0 + 1024], False, True)], ["IB", "X%d_s" % i], bank, 1024 - VN)
        act(zb[:, VN:1024], xp, [bank], ["Z%s_s" % x], AF.Abs, t=ns(1024 - VN))
        for a, b in CH[h]:
            tt(T.X[:, x0 + a:x0 + b], tz.indirect(T.LH[:, l0 + a // 16:l0 + b // 16]), T.EREP[:, h * 1024 + a:h * 1024 + b], OP.subtract,
               R + ["EREP%d%d" % (h, c) for c in range(a // 512, (b - 1) // 512 + 1)], ["X%d_%d" % (i, a)], gns(b - a))
        for a, b in AB[h]:
            act(zb[:, a:b], T.X[:, x0 + a:x0 + b], ["X%d_%d" % (i, c) for c, d in CH[h] if c < b and d > a], ["Z%s_%d" % (x, a)], AF.Abs, t=ns(b - a))
        pe([(key, T.WD[:, 15 - k:143 - k], zb[:, k::16], k == 0, k == 15) for k in range(16)],
           ["WD", "Z%s_s" % x] + ["Z%s_%d" % (x, a) for a, b in AB[h]], "BK" + x, 1024)
        op("v", lambda: V.tensor_tensor_scan(T.KS[:, l0:l0 + 64], key, T.RB[:, l0:l0 + 64], BIG, OP.min, OP.add), ["RB", "BK" + x], ["KS%d" % i], 53.0)
        if p == 0:
            op("v", lambda: V.tensor_tensor_scan(T.KS[:, 256 + l0:320 + l0], key, T.RB[:, 256:320], BIG, OP.min, OP.add), ["RB", "BK" + x], ["KD%d" % i], 53.0)

    def restart(h, q):
        x = "%d" % h
        hh = slice(h * 64, h * 64 + 64)
        ka, lp = T.KI[:, h * 4:h * 4 + 4], T.LP[:, h * 8:h * 8 + 4]
        ends = T.KS[:, h * 64 + 15:h * 64 + 64:16]
        tt(ka, ends, T.KS[:, 256 + h * 64 + 15:256 + h * 64 + 64:16], OP.subtract, ["KS" + x, "KD" + x], ["KI" + x])
        ts(lp, ka, 16.0, OP.mult, ["KI" + x, "cK", "cKH"], ["LP" + x], C["K" if h == 0 else "KH"], OP.add)
        tt(T.C2[:, hh], T.X[:, h * 1024:h * 1024 + 1024].indirect(lp), T.E2M[:, hh], OP.add,
           xtags(h) + ["LP" + x, "E2Ma" + x, "E2Mb" + x], ["C2" + x], gns(64))
        u_mm(q, h, T.C2[:, hh], "C2" + x)
        tt(T.SENT[:, 8 + h * 4:12 + h * 4], ends, T.SENT[:, h * 4:h * 4 + 4], OP.min, ["KS" + x, "SENT"], ["KF1" + x])

    def winner(h, q):
        x = "%d" % h
        c = slice(h * 4, h * 4 + 4)
        hh = slice(h * 64, h * 64 + 64)
        pl = T.KF[:, 8 + h * 4:12 + h * 4]
        tt(T.KF[:, c], T.KS[:, 128 + h * 64 + 15:192 + h * 64:16], T.SENT[:, 8 + h * 4:12 + h * 4], OP.min, ["KS%d" % (2 + h), "KF1" + x], ["KF" + x])
        ts(pl, T.KF[:, c], 511, AND, ["KF" + x], ["PL" + x])
        cp(T.LN[:, c], pl, ["PL" + x], ["LN" + x])
        tt(T.HGD[:, hh], T.HC[:].indirect(T.LN[:, c]), T.DL[:, 0:64], OP.mult, ["HC0", "HC1", "HC2", "HC3", "HCe", "LN" + x, "DL"],
           ["HGD" + x], gns(64))
        ts(T.LF[:, c], pl, 16.0, OP.mult, ["PL" + x, "cK"], ["LF" + x], C["K"], OP.add)

    hash_consts((rank + 1) % NR)
    SNT, SST = ["SN%d" % i for i in range(4)], ["SS%d" % i for i in range(4)]
    PK = ("D00", "D01", "D10", "D11")
    for t in range(NR):
        q = (rank + 1 + t) % NR
        more = t < NR - 1
        qc = slice(q, q + 1)
        if more:
            hash_consts((q + 1) % NR)
        nmn = T.NMI[:] if t == 0 else T.SN[:, 2::3]
        win, R = (T.F[:, 0:FS], ftp) if t == 0 else (T.F[:], ftp + fsd + ["FW"])
        fw = FT - 128 - t * 128
        for h in range(2):
            middle(h, q, win, R)
        ts(T.SENT[:, 0:8], T.CT[:], T.THK[:, qc], OP.add, ["CT", "THK"], ["SENT"])
        act(T.NM0[:], nmn, ["NMI", "NMX", "IX2"] + SNT, ["NM0"], AF.Identity, bias=T.IX2[:, qc], scale=T.NMX[:, qc], t=106)
        pe([(T.HS[:, 0:128], T.IF[:], T.NM0[:], True, False)], ["IF", "NM0"], "HS", 512)
        if more:
            act(T.KA[:, 0:128], nmn, ["NMI", "NMX"] + SNT, ["KA"], AF.Sign, scale=T.NMX[:, qc], t=106)
            act(T.KA[:, 128:256], T.TI[:], ["TI", "ISX", "WB%d" % t], ["KA"], AF.Identity, bias=T.WB[:, t:t + 1], scale=T.ISX[:, qc], t=106)
            tt(T.SL0[:], T.TPS[:] if t == 0 else T.SS[:, 2::3], T.KA[:, 0:128], OP.mult, ["TPS", "KA"] + SST, ["SL0"], 106)
            tt(T.SLW[:, 0:128], T.SL0[:], T.KA[:, 128:256], OP.add, ["SL0", "KA"], ["SLW"], 106)
            act(T.KA[:, 0:128], T.TI[:], ["TI"], ["KA"], AF.Identity, bias=float(fw), t=106)
            act(T.BS[:, 17::12], T.TI[:], ["TI"], ["DS5"], AF.Identity, bias=float(fw), t=106)
            tt(T.OWN[:], T.SL0[:], T.KA[:, 0:128], OP.max, ["SL0", "KA"], ["OWN"], 106)
            tt(T.BS[:, 13:1549:12], T.OWN[:], T.KA[:, 0:128], OP.subtract, ["OWN", "KA"], ["DS4"], 106)
            act(T.DS[:, 3::4], T.OWN[:], ["OWN"], ["DS3"], scale=-1.0, t=106)
            act(T.FLB[:], nmn, ["NMI", "NMX"] + SNT, ["FLB"], AF.Sign, scale=T.NMX[:, qc], t=106)
            first_row(True)
            scan(T.PR[:, 0:128], T.US[:, 256:384], T.KA[:, 256:384], OP.add, OP.max, ["RU", "KA"], ["pr0"], 106)
            cp(T.LR[:], T.PR[:, 15:128:16], ["pr0"], ["LR"])
            tt(T.X[:, 4096:4224], win.indirect(T.LR[:]), T.E1[:], OP.subtract, R + ["LR", "E10", "E11", "E1z"], ["Xe"], gns(128))
        for h in range(2):
            hashes(0, h, q)
            search(0, h, q)
            restart(h, q)
        for h in range(2):
            hashes(1, h, q)
            search(1, h, q)
        wl = T.WS[:, 15 - 2 * q:143 - 2 * q]
        for b in range(4):
            pe([(T[PK[b]][:, 0:256], T.IH[:], T.RR[:], True, False)], ["IH", "RR0", "RR1"], PK[b], 256)
        for b in range(2):
            pe([(bk[b][:, 256:384], (T.IB, T.IBN)[b][:], T.PC[:, 0:128], True, False)], ["IB", "IBN", "PC"], "BK%d" % b, 128)
        for h in range(2):
            winner(h, q)
            hh = slice(h * 64, h * 64 + 64)
            for b in range(4):
                pk = T[PK[b]]
                calls = [(pk[:, c * 128 + h * 64:c * 128 + h * 64 + 64], T.SGP[:, (b * 2 + c) * 128:(b * 2 + c + 1) * 128], T.HGD[:, hh], False, False)
                         for c in range(2)]
                if h == 1:
                    calls.append((pk[:, 0:256], T.HGD[:], T.SGN[:, b * 256:b * 256 + 256], False, True))
                pe(calls, ["HGD%d" % i for i in range(h + 1)] + ["SG%d_%d" % (i, b * 2 + c) for i in range(2) for c in range(2)], PK[b], 128 + 256 * h)
            pe([(T.HS[:, hh], wl, T.HGD[:, hh], False, h == 1)], ["WS", "HGD%d" % h], "HS", 64)
        act(T.NMW[:, 0:128], T.HS[:, 0:128], ["HS"], ["NMW"], AF.Relu, t=106)
        act(T.BN[:, 13:1549:12], T.HS[:, 0:128], ["HS"], ["DN4"], AF.Relu, t=106)
        act(T.FLW[:, 0:128], T.NMW[:, 0:128], ["NMW"], ["FLW"], AF.Sign, t=106)
        act(T.FLW[:, 144:272], T.NMW[:, 0:128], ["NMW"], ["FL2"], AF.Sign, t=106)
        act(T.DN[:, 3::4], T.NMW[:, 0:128], ["NMW"], ["DN3"], scale=-1.0, t=106)
        if more:
            tt(T.F[:, fw:fw + 128], T.X[:].indirect(T.LF[:]), T.E1[:], OP.add,
               [a for i in range(4) for a in xtags(i)] + ["Xe", "LF0", "LF1", "E10", "E11", "E1z"], ["FW"], gns(128))
        for c in range(8):
            pk = T[PK[c // 2]]
            op("v", lambda c=c, pk=pk: V.tensor_reduce(T.KB[:, c:c + 1], pk[:, (c % 2) * 128:(c % 2) * 128 + 128], AxisListType.X, OP.min,
                                                       apply_absolute_value=True), [PK[c // 2]], ["KB%d" % c], 106.0)
            act(T.MM[:, c * 32:c * 32 + 32], T.MSK[:], ["KB%d" % c, "MSK0", "MSK1"], ["MM%d" % c], scale=T.KB[:, c:c + 1])
        mmt = ["MM%d" % c for c in range(8)]
        pe([(T.KA[:, 0:8], T.MM[:, 0::2], T.CSEL[:], True, True)], mmt + ["CSEL"], "KA", 64, ["first"])
        pe([(T.HS[:, 128:256], T.MM[:, 1::2], T.IB[:], True, True)], mmt + ["IB"], "HS", 128, ["first"])
        pe([(T.D00[:, 0:128], T.MM[:, 1::2], T.IB[:], True, False),
            (T.D00[:, 0:128], T.IBN[:], T.PC[:, 0:128], False, True)], mmt + ["IB", "IBN", "PC"], "D00", 256, ["first"])
        cp(T.LQ[:], T.KA[:, 0:8], ["KA"], ["LQ"])
        act(T.KRS[:, 0:128], T.HS[:, 128:256], ["HS"], ["KRS"], t=106)
        act(T.FST[:], T.D00[:, 0:128], ["D00"], ["FST"], AF.Relu, t=106)
        act(T.KRP[:], T.KRS[:].indirect(T.LQ[:]), ["KRS", "KRe", "LQ"], ["KRP"], t=gns(128))
        act(T.D0[:, 2:512:4], T.FST[:], ["FST"], ["F2"], AF.Sign, t=106)
        tt(T.NE1[:], T.NMW[:].indirect(T.LQ[:]), T.BN[:, 13:1549:12], OP.not_equal, ["NMW", "NMe", "DN4", "LQ"], ["NE1"], gns(128))
        tt(T.NE2[:], T.FLW[:, 0:144].indirect(T.LQ[:]), T.FLW[:, 144:272], OP.not_equal, ["FLW", "FLe", "FL2", "LQ"], ["NE2"], gns(128))
        for tag, a, b, stop in (("NE1", T.BOB, T.IB, False), ("KRP", T.IBN, T.IB, False), ("NE2", T.BON, T.IBN, True)):
            pe([(T.BK0[:, 256:384], a[:], T[tag][:], False, stop)], ["BOB", "BON", "IBN", tag], "BK0", 128)
            pe([(T.BK1[:, 256:384], b[:], T[tag][:], False, stop)], ["IB", "IBN", tag], "BK1", 128)
        act(T.D0[:, 513::3], T.BK0[:, 256:384], ["BK0"], ["F4"], AF.Relu, bias=1.0, scale=-1.0, t=106)
        ts(T.D0[:, 514::3], T.BK1[:, 256:384], 0.5, OP.is_lt, ["BK1"], ["F5"], t=106)
        for on, wn, out, x, b in ((more, "SLW", "SS", "DS", "BS"), (True, "NMW", "SN", "DN", "BN")):
            for h in range(2 if on else 0):
                y = "%d" % h
                own = T.OWN[:, h * 64:h * 64 + 64] if x == "DS" else T.BN[:, h * 768 + 13:h * 768 + 781:12]
                tt(T[x][:, h * 256:h * 256 + 256:4], T[wn][:].indirect(T.LQ[:, h * 4:h * 4 + 4]), own, OP.max,
                   [wn, wn[:2] + "e", "OWN" if x == "DS" else "DN4", "LQ"], [x + "0" + y], gns(64))
                for i in range(2 * h, 2 * h + 2):
                    scan(T[b][:, i * 384:i * 384 + 384:3], T.D0[:, i * 128:i * 128 + 128], T[x][:, i * 128:i * 128 + 128], OP.mult, OP.add,
                         ["F0", "F2", x + "0" + y] + [x + "%d" % j for j in range(1, 4)], [b + "%d" % i], 106)
                for i in ([(2 * h, 2)] if x == "DS" or not more else [(2 * h, 1), (2 * h + 1, 1)]):
                    tags = ["%d" % j for j in range(i[0], i[0] + i[1])]
                    o, n = i[0] * 96, i[1] * 96
                    scan(T[out][:, o:o + n], T.D0[:, 512 + o:512 + o + n], T[b][:, 4 * o + 9:4 * (o + n) + 9:4], OP.mult, OP.add,
                         ["F0", "F4", "F5", x + "4", x + "5"] + [b + j for j in tags], [out + j for j in tags], ns(n))
                if x == "DS":
                    cp(T.LE[:, h * 64:h * 64 + 64], T.SS[:, h * 192 + 2:h * 192 + 192:3], SST[2 * h:2 * h + 2], ["LE" + y])
    ts(T.YO[:], T.SN[:, 2::3], -1.0, OP.add, SNT, ["YO"], t=106)
    dma("y", T.yp[:], T.YO[:], ["YO"], ["yp"])

    Q = {"v": V, "s": S, "t": PE, "g": g, "y": g.sync}
    SEM = {"v": "v", "s": "s", "t": "t", "g": "gp"}
    cnt = {e: 0 for e in SEM}
    clk = {e: {} for e in Q}
    hist, tok, ndma = {}, {}, [0]

    def wait(e, need):
        for s, n in sorted(need.items()):
            if clk[e].get(s, 0) < n:
                Q[e].wait_ge(T.sem[s], n)
                for s2, n2 in hist.get((s, n), {}).items():
                    clk[e][s2] = max(clk[e].get(s2, 0), n2)
                clk[e][s] = max(clk[e].get(s, 0), n)

    for i in order_calls(ops):
        o = ops[i]
        e = o["e"]
        need = {}
        for s, n in [tok[j] for j in o["sems"]] + o["ext"]:
            need[s] = max(need.get(s, 0), n)
        wait(e, need)
        ins = o["fn"]()
        if o["kind"] == "d":
            tok[i] = ("d%d" % ndma[0], 16)
            ndma[0] += 1
            ins.then_inc(T.sem[tok[i][0]], 16)
        elif o["kind"] == "c":
            for x in (ins if isinstance(ins, list) else [ins]):
                x.then_inc(T.sem[SEM[e]], 1)
                cnt[e] += 1
            tok[i] = (SEM[e], cnt[e])
        if i in tok:
            hist[tok[i]] = dict(clk[e])

    need = {"v": cnt["v"], "s": cnt["s"], "t": cnt["t"], "gp": cnt["g"], "ls": ls[0], "nm": 16, "ft": 32, "fs": 32}
    for i in range(ndma[0]):
        need["d%d" % i] = 16
    for q in ntz:
        need["tz%d" % q] = ntz[q]
    wait("y", need)
